import numpy as np, ml_dtypes
CORES = [40,41,42,43,44,45,46,47]
N = 8
BF = ml_dtypes.bfloat16
def gentries(a):
    return np.ascontiguousarray(a.reshape(8, 16, -1).transpose(0, 2, 1)).reshape(8, -1)
def gtable(e):
    e = np.asarray(e); return np.ascontiguousarray(e.reshape(8, -1, 16).transpose(0, 2, 1)).reshape(128, -1).astype(np.int32)
S, M, CAP, RO = 1024, 768, 16, 2
W = N * S
def look(x, k, p, wt):
    n, m = p.shape[0], p.shape[3]; gi = np.arange(8)[None, :, None]
    q = np.stack([k[gi, 3 - t, p[:, :, t]] for t in range(4)], axis=2)
    xt = np.ascontiguousarray(x.transpose(0, 2, 1))
    c = [xt[gi, q[:, :, t]].reshape(n, 8, m, 4, 4) for t in range(4)]
    board = np.concatenate([np.concatenate([c[0], c[1]], axis=4), np.concatenate([c[2], c[3]], axis=4)], axis=3)
    hot = (board == 15).astype(np.int64); near = np.zeros((n, 8, m, 4, 4), np.int64)
    for i in range(3):
        for j in range(3):
            if (i, j) != (1, 1): near = near + hot[..., 1 + i:5 + i, 1 + j:5 + j]
    mid = board[..., 2:6, 2:6]
    y = np.where(mid == 0, np.where(near == 2, 15, 0), np.maximum(mid - 1, 0)).reshape(n, 8, m, 16)
    h = np.add.reduce(y * wt[None, :, None, :], axis=3) & (W - 1)
    r0 = xt[gi, h]; r1 = xt[gi, h ^ 1]
    return q, y, h, np.all(r0 == y, axis=3), np.all(r1 == y, axis=3), r0[..., 0] < 0, r1[..., 0] < 0
def content(rng, n):
    u = rng.random((n, 16)); lo = 0.6 * rng.random((n, 1)); hi = 1 - 0.4 * rng.random((n, 1))
    return np.where(u < lo, 0, np.where(u > hi, 15, rng.integers(0, 16, (n, 16))))
def world(rng, share, few, ends=0):
    x = np.full((8, 16, W), -1, np.int64); k = np.zeros((8, 4, W), np.int64); pools = []
    for g in range(8):
        o = rng.permutation(W)
        if ends == 1: o = np.concatenate([np.array([0, W - 1]), o[(o > 0) & (o < W - 1)]])
        if ends == 2: o = o[(o > 1) & (o < W - 16)]
        n = min(int(W * float(share[g])), len(o)); a = n // 2
        c = content(rng, n); pal = content(rng, int(few[g])); c[:a] = pal[rng.integers(0, len(pal), a)]
        x[g][:, o[:n]] = c.T
        k[g][:, o[:a]] = rng.choice(o[:a], (4, a)); k[g][:, o[a:n]] = rng.choice(o[a:n], (4, n - a))
        pools.append((o[:a], o[a:n]))
    return x, k, pools
def start(rng, pools, share, m=M, pw=1.0):
    p = np.zeros((N, 8, 4, m), np.int64)
    for g in range(8):
        a, b = pools[g]
        pa = a[(len(a) * rng.random((N, 4, m)) ** pw).astype(np.int64)]; pb = b[(len(b) * rng.random((N, 4, m)) ** pw).astype(np.int64)]
        p[:, g] = np.where(rng.random((N, 1, m)) < share[:, g, None, None], pa, pb)
    return p
def plant(rng, x, k, p, wt, pools, share, flip=0.3, wrong=0.1, odd=False):
    q, y, h = look(x, k, p, wt)[:3]
    for g in range(8):
        yy = y[:, g].reshape(-1, 16); hh = h[:, g].reshape(-1); hh = hh ^ (rng.random(len(hh)) < flip).astype(np.int64)
        i = rng.permutation(len(hh))[:int(share * len(hh))]; i = i[x[g, 0, hh[i]] < 0]
        u, j = np.unique(hh[i], return_index=True); v = yy[i[j]].copy(); off = v.copy()
        rows = np.arange(len(u)); col = rng.integers(0, 16, len(u)); err = rng.random(len(u)) < wrong
        off[rows, col] = (v[rows, col] + 1) & 15
        if odd:
            sort = rng.integers(0, 4, len(u)); e = np.flatnonzero(sort == 1); off[e, col[e]] = (v[e, col[e]] + 8) & 15
            off[sort == 2] = 0
            a, b = v[:, :15], v[:, 1:]; up = (a == 15) & (b < 15)
            can = (up | ((a == 0) & (b > 0))) & (np.arange(15) % 4 < 3)
            c = np.argmax(can * (1 - rng.random(can.shape)), axis=1)
            e = np.flatnonzero((sort == 3) & np.any(can, axis=1)); c = c[e]
            off[e] = v[e]; off[e, c] = 15 - v[e, c]; off[e, c + 1] = v[e, c + 1] + np.where(up[e, c], 1, -1)
        v = np.where(err[:, None], off, v)
        kk = rng.choice(np.concatenate(pools[g]), (4, len(u)))
        if odd: kk[:, rng.random(len(u)) < 0.25] = 0
        x[g][:, u] = v.T; k[g][:, u] = kk
def pack(x, k, p, wt):
    return {"cells": np.ascontiguousarray(x.reshape(8, 16, N, S).transpose(2, 0, 1, 3)).reshape(N, 128, S).astype(np.float32).astype(BF),
            "kids": np.ascontiguousarray(k.reshape(8, 4, N, S).transpose(2, 0, 1, 3)).reshape(N, 32, S).astype(np.int32),
            "nodes": np.stack([gtable(a.reshape(8, 4 * M)) for a in p]),
            "wt": np.ascontiguousarray(np.tile(wt.reshape(1, 128, 1), (N, 1, 1))).astype(np.int32)}
def setup_inputs(rng):
    wt = rng.integers(0, W, (8, 16)); few = rng.permutation(np.array([2, 2, 3, 3, 4, 5, 6, 6]))
    x, k, pools = world(rng, 0.35 + 0.2 * rng.random(8), few)
    p = start(rng, pools, rng.choice(np.array([0.3, 0.6, 0.9]), (N, 8)))
    plant(rng, x, k, p, wt, pools, 0.3)
    return pack(x, k, p, wt)
def setup_inputs_room(rng):
    wt = rng.integers(0, W, (8, 16)); x, k, pools = world(rng, 0.35 + 0.15 * rng.random(8), rng.integers(3, 7, 8))
    cand = start(rng, pools, np.full((N, 8), 0.1), 2 * M)
    plant(rng, x, k, cand, wt, pools, 0.15)
    q, y, h, hit0, hit1, free0, free1 = look(x, k, cand, wt)
    own = np.where(hit0 | hit1 | ~(free0 | free1), -1, h // S); p = np.zeros((N, 8, 4, M), np.int64)
    want = np.where(free0, h, h ^ 1); taken = np.zeros(W, bool)
    for r in range(N):
        for g in range(8):
            sel = []
            for o in range(N):
                n = int(rng.choice(np.array([0, 1, CAP - 1, CAP, CAP + 1, 2 * CAP])))
                if r == 0 and o == 1: n = (CAP, CAP + 1, 2 * CAP, CAP - 1, 1, 0, CAP, CAP + 1)[g]
                f = rng.permutation(np.flatnonzero(own[r, g] == o))
                if g == 6 and o == 1:
                    n = CAP; f = f[np.unique(want[r, g, f], return_index=True)[1]]
                    f = rng.permutation(f[~taken[want[r, g, f]]]); taken[want[r, g, f[:n]]] = True
                sel.append(f[:n])
            sel = np.concatenate(sel); rest = np.flatnonzero(own[r, g] < 0)
            sel = rng.permutation(np.concatenate([sel, rng.choice(rest, M - len(sel))]))
            if r == 1 and g == 2:
                last = rng.permutation(np.flatnonzero(own[r, g] == 2))[:CAP]
                sel = np.concatenate([rng.choice(np.flatnonzero((own[r, g] >= 0) & (own[r, g] != 2)), M - len(last)), last])
            p[r, g] = cand[r, g][:, sel]
    return pack(x, k, p, wt)
def setup_inputs_clash(rng):
    wt = (2 * rng.integers(0, W // 2, (8, 1)) + 1) * rng.integers(0, 3, (8, 16)) & (W - 1)
    z = rng.permutation(8); wt[z[0]] = 0; wt[z[1]] = 0; wt[z[1], rng.integers(0, 16)] = W - 1
    x, k, pools = world(rng, 0.25 + 0.2 * rng.random(8), rng.integers(2, 9, 8), 2)
    p = start(rng, pools, rng.choice(np.array([0.2, 0.5, 0.8]), (N, 8)))
    return pack(x, k, p, wt)
def setup_inputs_near(rng):
    wt = rng.integers(0, W, (8, 16)); wt[rng.integers(0, 8)] = rng.integers(W - W // 8, W, 16)
    x, k, pools = world(rng, 0.15 + 0.2 * rng.random(8), rng.integers(2, 9, 8), 1)
    p = start(rng, pools, rng.choice(np.array([0.2, 0.5, 0.8]), (N, 8)))
    plant(rng, x, k, p, wt, pools, 0.5, 0.0, 0.5, True); plant(rng, x, k, p, wt, pools, 0.7, 1.0, 0.3, True)
    return pack(x, k, p, wt)
def setup_inputs_alike(rng):
    wt = rng.integers(0, W, (8, 16)); x, k, pools = world(rng, np.array([0.4, 0.98, 0.3, 0.05, 0.5, 0.4, 1.0, 0.6]), np.array([1, 3, 2, 2, 1, 4, 2, 12]), 1)
    a = pools[2][0]; k[2][:, a] = rng.choice(np.array([0, W - 1]), (4, len(a)))
    share = rng.random((N, 8)); share[:, [0, 2]] = 1.0
    p = start(rng, pools, share); p[:, 2] = rng.choice(np.array([0, W - 1]), (N, 4, M))
    for g in (3, 5, 7): p[:, g] = p[:, g][:, :, rng.integers(0, 8, M)]
    return pack(x, k, p, wt)
def setup_inputs_spread(rng):
    wt = np.minimum(np.exp2(rng.random((8, 16)) * np.log2(W)).astype(np.int64), W - 1) * (rng.random((8, 16)) > 0.0625)
    x, k, pools = world(rng, rng.permutation(np.linspace(0.08, 0.92, 8)), rng.integers(1, 41, 8))
    p = start(rng, pools, rng.random((N, 8)), M, 4.0)
    plant(rng, x, k, p, wt, pools, 0.2)
    return pack(x, k, p, wt)
def check_inputs(d):
    bad = []
    c = np.asarray(d["cells"]).astype(np.float32).reshape(N, 8, 16, S); e = c == -1
    if not np.all(e | ((c >= 0) & (c <= 15) & (c == np.floor(c)))): bad.append("numbers of cells")
    if np.any(np.any(e, axis=2) != np.all(e, axis=2)): bad.append("places of cells empty in part")
    ok = True
    for name in ("kids", "nodes", "wt"):
        if np.min(d[name]) < 0 or np.max(d[name]) > W - 1: bad.append("range of " + name); ok = False
    if np.any(d["wt"] != d["wt"][:1]): bad.append("wt alike on all ranks")
    full = ~np.any(e, axis=2).transpose(1, 0, 2).reshape(8, W)
    kd = np.asarray(d["kids"]).astype(np.int64).reshape(N, 8, 4, S).transpose(1, 2, 0, 3).reshape(8, 4, W)
    if np.any((kd != 0) & ~full[:, None, :]): bad.append("children of empty places")
    if ok:
        to = np.take_along_axis(full, kd.reshape(8, -1), 1).reshape(8, 4, W)
        if np.any(full[:, None, :] & ~to): bad.append("children name full places")
        if not all(np.all(np.take_along_axis(full, gentries(a).astype(np.int64), 1)) for a in d["nodes"]): bad.append("nodes name full places")
    return bad
def reference(cells, kids, nodes, wt):
    x = np.concatenate([a.astype(np.float32).astype(np.int64).reshape(8, 16, S) for a in cells], axis=2)
    k = np.concatenate([a.astype(np.int64).reshape(8, 4, S) for a in kids], axis=2)
    p = np.stack([gentries(a).astype(np.int64).reshape(8, 4, M) for a in nodes])
    w = wt[0].astype(np.int64).reshape(8, 16); gi = np.arange(8)[None, :, None]
    for rnd in range(RO):
        q, y, h, hit0, hit1, free0, free1 = look(x, k, p, w)
        at = np.where(hit0, h, np.where(hit1, h ^ 1, -1))
        got = np.stack([k[gi, t, np.maximum(at, 0)] for t in range(4)], axis=2)
        p = np.where(at[:, :, None] >= 0, got, q)
        want = np.where(at >= 0, -1, np.where(free0, h, np.where(free1, h ^ 1, -1)))
        keep = np.zeros(want.shape, bool)
        for o in range(N):
            mine = (want >= 0) & (want // S == o)
            keep = keep | (mine & (np.add.accumulate(mine.astype(np.int64), axis=2) <= CAP))
        for g in range(8):
            i = np.flatnonzero(keep[:, g].reshape(-1))
            u, first = np.unique(want[:, g].reshape(-1)[i], return_index=True); win = i[first]
            x[g][:, u] = y[:, g].reshape(-1, 16)[win].T
            k[g][:, u] = q[:, g].transpose(1, 0, 2).reshape(4, -1)[:, win]
    return {"ycells": np.stack([x[:, :, r * S:(r + 1) * S].reshape(128, S) for r in range(N)]).astype(np.float32).astype(BF),
            "ykids": np.stack([k[:, :, r * S:(r + 1) * S].reshape(32, S) for r in range(N)]).astype(np.float32),
            "ynodes": np.stack([gtable(a.reshape(8, 4 * M)) for a in p]).astype(np.float32)}

@@ -1,0 +1,501 @@
+from concourse.bass import DstId, RemoteDMATransfer
+from concourse.mybir import AluOpType as A, AxisListType, ActivationFunctionType as AF
+
+F32, B16, I32, F16, U16 = "float32", "bfloat16", "int32", "float16", "uint16"
+SB = {
+    "KI": ([256], I32), "KH": ([512], I32), "HL": ([512], B16), "CN": ([1152], B16), "YK": ([1152], F32), "PB": ([512], B16),
+    "WI": ([1], I32), "WH": ([2], I32), "WB": ([2], B16), "WC": ([2], F32),
+    "L": ([2048], B16), "LN": ([8, 24], I32), "LF": ([8, 24], F32), "UP": ([1024], B16), "R": ([8192], B16), "Q": ([9216], B16),
+    "O1a": ([192], U16), "O1b": ([192], U16), "G1a": ([3072], B16), "G1b": ([3072], B16), "O2": ([192], U16), "G2": ([3072], B16),
+    "Y0": ([6, 8, 16], B16), "YB": ([6, 8, 16], B16), "YXa": ([784], B16), "YXb": ([784], B16), "RB": ([784], B16),
+    "HI": ([5, 48], I32), "HF": ([48], F32), "O3": ([96], U16), "G3": ([1536], B16), "KN": ([4, 8, 2, 8], F32), "EQ": ([512], B16), "EA": ([512], B16),
+    "SM": ([14, 64], F32), "SI": ([5, 64], I32), "P": ([64, 4], F32), "M0": ([64, 4], F32), "MQ": ([64, 4], F32),
+    "OH": ([4, 8, 2, 8], B16), "AA": ([512], B16), "CS": ([512], B16), "OK": ([2064], F16), "OI": ([4, 8, 2, 8], F16), "OS": ([16], U16),
+    "GA": ([256], B16), "GB": ([256], B16), "FW": ([8, 8, 16], B16), "N3a": ([8, 24], F32), "N3b": ([8, 24], F32),
+    "DG": ([8, 128], F16), "AB": ([8, 128], B16), "SN": ([8, 8], F32), "DQ": ([1024], B16), "OQ": ([64], U16), "XQ": ([4, 8, 2], F32),
+    "LWa": ([8, 24], F32), "LWb": ([8, 24], F32), "LP": ([8, 24], F32), "OP": ([8, 2, 2, 2, 3], F32), "NP": ([16, 12], F32),
+    "XC": ([8, 16], B16), "XK": ([8, 16], F32), "XO": ([8, 16], F16), "DC": ([128], B16), "DK": ([128], F32), "OO": ([8], U16),
+    "PI": ([1], I32), "PJ": ([12], I32), "PF": ([64], F32), "XR": ([144], F32), "X16": ([128], F32), "VT": ([5, 16], F32), "VU": ([6, 16], F32),
+    "XT0": ([144], F32), "XT1": ([144], F32), "ID": ([8, 16], B16), "IDF": ([128], F32), "IDH": ([128], F16), "ID4": ([4, 128], B16),
+    "MT": ([128], B16), "MF": ([16], F32), "GM": ([8], F32), "GH": ([8], F16), "PM": ([130], B16),
+    "PW0": ([144], F32), "PW1": ([144], F32), "PT0": ([130], F32), "PT1": ([130], F32),
+    "KO": ([8, 16, 4], B16), "LR": ([8, 4, 16], B16), "WD": ([144], B16), "LU": ([32], B16), "RG": ([64], B16), "RK": ([8, 8], B16),
+    "RQ": ([8], B16), "LB": ([224], B16), "R8": ([8], B16), "LA0": ([128], B16), "LB0": ([128], B16), "SR": ([128], F32),
+    "SW": ([128], B16), "ML": ([2, 96], F32), "MD": ([96], F32), "TT": ([6, 96], B16), "ON": ([128], B16), "OF": ([128], F16),
+    "TB": ([128], B16), "D0": ([512], B16), "D1": ([512], B16), "IC": ([8], F32), "CG": ([2, 8], F32),
+}
+SCRATCH = {k: ("sbuf", [128] + s, d) for k, (s, d) in SB.items()}
+SCRATCH["D"] = ("dram", [8, 128, 256], B16)
+SCRATCH["DN"] = ("dram", [8, 128, 24], I32)
+for _b in range(8):
+    SCRATCH["B%d" % _b] = ("psum", [128, 4, 8, 2, 8], F32)
+SEMAPHORES = ["v", "s", "t", "p"] + ["d%d" % i for i in range(48)] + ["rl%d" % i for i in range(5)] + ["rr%d" % i for i in range(5)]
+S1 = ("svsv", "sssv")
+S2 = ("svsv", "ssss")
+S3 = ("vvvs", "vvvs")
+
+
+def rank_program(g, core, T, topo):
+    me = T.rank_of(core)
+    if me is None:
+        return
+    QU = {"v": g.vector, "s": g.scalar, "t": g.tensor, "p": g, "y": g.sync}
+    V, S, PE = g.vector, g.scalar, g.tensor
+    cnt = {"v": 0, "s": 0, "t": 0, "p": 0}
+    seen, lastw, reads, total = {}, {}, {}, {}
+    nd = [0]
+
+    def need(e, tok):
+        if seen.get((e, tok[0]), 0) < tok[1]:
+            QU[e].wait_ge(T.sem[tok[0]], tok[1]); seen[(e, tok[0])] = tok[1]
+
+    def deps(e, R, W):
+        toks = []
+        for k in R:
+            toks += [tok for tok in lastw.get(k, []) if not (e == "t" and tok[2] == "t")]
+            if k[0] == "B":
+                toks += [tok for tok in reads.get(k, {}).values() if tok[2] != e]
+        for k in W:
+            toks += [tok for tok in lastw.get(k, []) + list(reads.get(k, {}).values()) if tok[2] != e]
+        for tok in sorted(toks, reverse=True): need(e, tok)
+
+    def mark(tok, R, W):
+        for k in W:
+            lastw[k] = [tok]; reads[k] = {}
+        for k in R:
+            reads.setdefault(k, {})[tok[0]] = tok
+
+    def op(e, R, W, fn):
+        R, W = R.split(), W.split()
+        deps(e, R, W)
+        fn().then_inc(T.sem[e], 1); cnt[e] += 1; total[e] = cnt[e]
+        mark((e, cnt[e], e), R, W)
+
+    def dma(e, R, W, out, in_):
+        R, W = R.split(), W.split()
+        deps(e, R, W)
+        s = "d%d" % nd[0]; nd[0] += 1
+        QU[e].dma_start(out, in_).then_inc(T.sem[s], 16); total[s] = 16
+        mark((s, 16, "dma"), R, W)
+
+    others = [r for r in range(8) if r != me]
+    far = [r for r in others if topo.die(T.cores[r]) != topo.die(core)]
+    near = [r for r in others if r not in far]
+
+    def exchange(k, R, W, src, dst):
+        deps("p", R.split(), [])
+        tr = []
+        for r in others:
+            c = T.cores[r]; en = topo.engines(core, c); rid, pid, _ = topo.addr(c)
+            en = en[0::2][2 * far.index(r):] if r in far else en[1::2][2 * near.index(r):]
+            tr.append(RemoteDMATransfer(dst_ids=[DstId(rid=rid, pnc=pid)], dma_engine_mask=(1 << en[0]) | (1 << en[1]),
+                                        remote_sem=T.sem["rr%d" % k], src=src(r), dst=dst))
+        g.remote_dma_fused(tr, local_sem=T.sem["rl%d" % k])
+        total["rl%d" % k] = total["rr%d" % k] = 14
+        mark(("rl%d" % k, 14, "dma"), R.split(), [])
+        lastw[W] = [("rr%d" % k, 14, "dma")]
+
+    def ks(f, n): return " ".join(f % j for j in (range(n) if isinstance(n, int) else n))
+    def mm(R, W, out, l, r, st=True, sp=True): op("t", R, W, lambda: PE.matmul(out, l, r, st, sp))
+    def cp(R, W, o, i): op("v", R, W, lambda: V.tensor_copy(o, i))
+    def tt(R, W, o, a, b, f): op("v", R, W, lambda: V.tensor_tensor(o, a, b, f))
+    def ts(R, W, o, a, s1, f0, s2=None, f1=None):
+        op("v", R, W, (lambda: V.tensor_scalar(o, a, s1, None, f0)) if f1 is None else (lambda: V.tensor_scalar(o, a, s1, s2, f0, f1)))
+    def ms(W, o, c, R=""): op("v", R, W, lambda: V.memset(o, c))
+    def act(R, W, o, i, f=AF.Identity, **k): op("s", R, W, lambda: S.activation(o, i, f, **k))
+    def red(R, W, o, i, f): op("v", R, W, lambda: V.tensor_reduce(o, i, AxisListType.X, f))
+    def scan(R, W, o, a, b, f0, f1): op("v", R, W, lambda: V.tensor_tensor_scan(o, a, b, 0.0, f0, f1))
+    def iota(W, o, pat, base, cm=0): op("p", "", W, lambda: g.iota(o, pat, base, cm, allow_small_or_imprecise_dtypes=True))
+    def gather(e, R, W, o, win, off):
+        if e == "v": cp(R, W, o, win.indirect(off))
+        else: act(R, W, o, win.indirect(off))
+    B = [T["B%d" % b] for b in range(8)]
+    SHR, AND, EQ = A.arith_shift_right, A.bitwise_and, A.is_equal
+
+    dma("y", "", "KI", T.KI[:], T.kids[:])
+    dma("s", "", "CN", T.CN[:, 0:1024], T.cells[:])
+    dma("y", "", "DN", T.DN[:], T.nodes[:])
+    dma("s", "", "Dc", T.D[:, 0:64, :], T.cells[:])
+    dma("y", "", "WI", T.WI[:], T.wt[:])
+    op("p", "", "PI", lambda: g.iota(T.PI[:], [[0, 1]], 0, 1))
+    iota("XR", T.XR[:], [[1, 144]], 0)
+    iota("X16", T.X16[:], [[0, 8], [1, 16]], 0)
+    iota("VT1a", T.VT[:, 1, 0:12], [[8, 3], [1, 4]], 9)
+    iota("VT1b", T.VT[:, 1, 12:16], [[8, 2], [1, 2]], 18)
+    iota("VT2", T.VT[:, 2, :], [[8, 4], [1, 4]], 18)
+    iota("VT3a", T.VT[:, 3, 0:8], [[0, 2], [1, 4]], 4)
+    iota("VT3b", T.VT[:, 3, 8:16], [[1, 4], [0, 2]], 0)
+    iota("ML0", T.ML[:, 0, :], [[32, 6], [1, 16]], 0)
+    iota("ML1", T.ML[:, 1, :], [[16, 2], [64, 3], [1, 16]], 0)
+    exchange(0, "DN", "LN", lambda r: T.DN[r], T.LN[:, me, :])
+    dma("y", "DN", "LNo", T.LN[:, me, :], T.DN[me])
+
+    names = ["p", "b0", "pm", "pg", "hf", "t", "i4", "t2", "p8", "m1", "k11", "b3"]
+    rule = [(0, 127), (0, 1), (0, 15), (4, 7), (4, 1), (5, 3), (2, 3), (1, 3), (3, 15), (1, 7), (0, 11), (0, 3)]
+    col = {}
+    def C(n):
+        if n not in col: col[n] = len(col)
+        return T.PF[:, col[n]:col[n] + 1]
+    for j, (sh, an) in enumerate(rule):
+        ts("PI", "PJ%d" % j, T.PJ[:, j:j + 1], T.PI[:], sh, SHR, an, AND); C(names[j])
+    cp(ks("PJ%d", 12), ks("c%s", names), T.PF[:, 0:12], T.PJ[:])
+    def lin(n, a, x, y, f0=A.mult, f1=A.add):
+        ts(ks("c%s", [z for z in (a, x, y) if isinstance(z, str)]), "c" + n, C(n), C(a), C(x) if isinstance(x, str) else x, f0, C(y) if isinstance(y, str) else y, f1)
+    def pick(W, o, rk, n, c, w="one"):
+        ts("%s c%s c%s" % (rk, c, w), W, o, T[rk][:, 0:n], C(c), EQ, C(w), A.mult)
+    xt = [0]
+    def spick(W, o, rk, n, c, w="one"):
+        k = "XT%d" % xt[0]; xt[0] ^= 1
+        act(rk + " c" + c, k, T[k][:, 0:n], T[rk][:, 0:n], AF.Abs, scale=-1.0, bias=C(c))
+        act(k + " c" + w, W, o, T[k][:, 0:n], AF.Relu, scale=-65536.0, bias=C(w))
+    ms("cone", C("one"), 1.0); ms("cb1", C("b1"), -(1.0 + 2.0 ** -11))
+    lin("w16", "b0", 15.0, 1.0); lin("cpm", "p", 1.0, "b0", A.add, A.subtract)
+    pick("PM", T.PM[:], "XR", 130, "cpm", "w16")
+    pick("ID", T.ID[:], "XR", 128, "p")
+
+    ts("KI", "KHa", T.KH[:, 0:256], T.KI[:], 8160, AND)
+    ts("KI", "KHb", T.KH[:, 256:512], T.KI[:], 31, AND)
+    cp("KHa KHb", "HL", T.HL[:], T.KH[:])
+    dma("y", "HL", "Dh", T.D[:, 64:80, :], T.HL[:, 0:256])
+    dma("y", "HL", "Dl", T.D[:, 80:96, :], T.HL[:, 256:512])
+    mm("PM CN", "B0", B[0][:], T.PM[:, 1:129], T.CN[:, 0:512], True, False)
+    mm("PM CN", "B0", B[0][:], T.PM[:, 0:128], T.CN[:, 512:1024], False, True)
+    act("B0", "PB", T.PB[:], B[0][:])
+    dma("s", "PB", "Dp", T.D[:, 96:128, :], T.PB[:])
+    exchange(1, "Dc Dh Dl Dp", "L", lambda r: T.D[r], T.L[:, 256 * me:256 * me + 256])
+    dma("y", "Dc Dh Dl Dp", "Lo", T.L[:, 256 * me:256 * me + 256], T.D[me])
+    iota("FWz", T.FW[:], [[0, 1024]], 0)
+    iota("D1", T.D1[:], [[0, 128], [-1, 4]], 1)
+    iota("D0", T.D0[:], [[0, 64], [4096, 8]], 0)
+    iota("ON", T.ON[:], [[0, 128]], 1)
+    iota("IC", T.IC[:], [[96, 8]], 16, 1)
+    iota("CG0", T.CG[:, 0, :], [[-896, 8]], 8193, 1)
+    iota("CG1", T.CG[:, 1, :], [[128, 8]], 8192, 1)
+
+    ms("LR", T.LR[:], 0.0)
+    for t in range(4):
+        t1, t0 = t >> 1, t & 1
+        b = 4 * (5 - 4 * t1 - t0); vr, vc = 2 - 2 * t1, 2 - 2 * t0
+        act("ID LR", "LRa%d" % t, T.LR[:, 2 * t, 0:3, 0:12], T.ID[:, b // 16:b // 16 + 3, b % 16:b % 16 + 12])
+        act("ID LR", "LRb%d" % t, T.LR[:, 2 * t, 3, :], T.ID[:, vr:vr + 2, 4 * vc:4 * vc + 8])
+        act("ID LR", "LRc%d" % t, T.LR[:, 2 * t, 0:2, 12:16], T.ID[:, 4:6, 4 * (3 - t):4 * (3 - t) + 4])
+    act(ks("LRa%d", 4) + " " + ks("LRb%d", 4) + " " + ks("LRc%d", 4), "LRz", T.LR[:, 1::2], T.LR[:, 0::2])
+    pick("MF", T.MF[:], "X16", 16, "pm")
+    def table(n, row, R):
+        tt(R + " MF", "VU%d" % row, T.VU[:, row, :], T.VT[:, row, :], T.MF[:], A.mult)
+        red("VU%d" % row, "c" + n, C(n), T.VU[:, row, :], A.add)
+    ms("VT0", T.VT[:, 0, :], 0.0)
+    for a in range(3): ms("VT0%d" % a, T.VT[:, 0, 4 * a:4 * a + 3], 1.0, "VT0")
+    table("hm", 0, ks("VT0%d", 3))
+    lin("x1", "t2", 32.0, 16.0); lin("nb0", "b0", -1.0, 1.0); lin("bias", "hm", -14.0, 0.0); lin("cpw", "x1", 1.0, "p8")
+    spick("PW0", T.PW0[:], "XR", 144, "cpw", "nb0"); spick("PW1", T.PW1[:], "XR", 144, "cpw", "b0")
+    lin("km", "k11", 3.0, 1.0, EQ, A.mult); lin("cwd", "pg", 16.0, 15.0); lin("crq", "hf", 4.0, "t")
+    spick("WD", T.WD[:], "XR", 144, "cwd", "km")
+    pick("RQ", T.RQ[:], "XR", 8, "crq", "km")
+    table("pos0", 1, "VT1a VT1b")
+    for t in range(4): ms("tau%d" % t, T.PF[32 * t:32 * t + 32, 63:64], float(8 * (t >> 1) + (t & 1)))
+    ts("chm " + ks("tau%d", 4), "cx2", C("x2"), C("hm"), 2.0, A.add, T.PF[:, 63:64], A.mult)
+    lin("hw", "hm", 2.0 ** -14, 0.0); lin("vw", "pm", 12.0, 1.0, A.is_ge, A.mult); lin("nhf", "hf", -1.0, 1.0); lin("pos", "x2", 1.0, "pos0")
+    U = lambda i: T.VU[:, i, :]
+    ts("VT2 cpos", "VU2", U(2), T.VT[:, 2, :], C("pos"), A.subtract)
+    lin("mine", "pg", float(me), 1.0, EQ, A.mult)
+    tt("VU2", "VU2", U(2), U(2), U(2), A.mult)
+    spick("SW", T.SW[:], "X16", 128, "pm", "mine")
+    pick("GM", T.GM[:], "XR", 8, "pg")
+    ts("VU2 chw", "VU0", U(0), U(2), 1.0, EQ, C("hw"), A.mult)
+    ts("VU2", "VU1", U(1), U(2), 49.0, A.is_ge)
+    ts("VU2 chw", "VU4", U(4), U(2), 81.0, A.is_le, C("hw"), A.mult)
+    ts("VU2 cvw", "VU5", U(5), U(2), 0.0, EQ, C("vw"), A.mult)
+    ts("WI", "WHa", T.WH[:, 0:1], T.WI[:], 8160, AND); ts("WI", "WHb", T.WH[:, 1:2], T.WI[:], 31, AND)
+    tt("VU1 VU4", "VU1", U(1), U(1), U(4), A.mult)
+    tt("VU0 VU5", "VU0", U(0), U(0), U(5), A.add)
+    cp("WHa WHb", "WB", T.WB[:], T.WH[:])
+    mm("SW WB", "B0", B[0][:, 0, 0, 0, 0:2], T.SW[:], T.WB[:])
+    ms("VT4", T.VT[:, 4, :], 1.0)
+    tt("VU0 VU1", "VU0", U(0), U(0), U(1), A.add)
+    for j in range(1, 4): ms("VT4%d" % j, T.VT[:, 4, j::4], 16.0 ** j, "VT4")
+    ts("VU0 cnhf", "LUa", T.LU[:, 0:16], U(0), C("nhf"), A.mult)
+    ts("VU0 chf", "LUb", T.LU[:, 16:32], U(0), C("hf"), A.mult)
+    lin("crk", "pg", 8.0, "i4")
+    table("wk", 4, "VT41 VT42 VT43")
+    cp("B0", "WC", T.WC[:], B[0][:, 0, 0, 0, 0:2])
+    pick("RKz", T.RK[:], "XR", 64, "crk", "wk")
+    lin("ge8", "pm", 8.0, 1.0, A.is_ge, A.mult); lin("x4", "hf", 16.0, "t")
+    ts("GM WC RKz", "RKa", T.RK[:, :, 4], T.GM[:], T.WC[:, 0:1], A.mult)
+    ts("GM WC RKz", "RKb", T.RK[:, :, 5], T.GM[:], T.WC[:, 1:2], A.mult)
+    table("fs", 3, "VT3a VT3b")
+    lin("x3", "ge8", "b0", 255.0, A.mult, A.mult); lin("clb", "pm", 93.0, "x4", A.add, A.add); lin("crg", "pg", 8.0, "fs"); lin("wg", "x3", 1.0, 1.0)
+    spick("LBa", T.LB[:, 0:144], "XR", 144, "clb", "km")
+    ms("LBb", T.LB[:, 144:224], 0.0)
+    pick("RG", T.RG[:], "XR", 64, "crg", "wg")
+    pick("IDF", T.IDF[:], "XR", 128, "p")
+    cp("LN LNo", "LF", T.LF[:], T.LN[:])
+    for h2 in range(2):
+        pw = T["PW%d" % h2]
+        mm("LF PW%d" % h2, "B1", B[1][:, :, 2 * h2::4, :, 0:6], pw[:, 16:144], T.LF[:, :, 0::2], True, False)
+        mm("LF PW%d" % h2, "B1", B[1][:, :, 2 * h2::4, :, 0:6], pw[:, 0:128], T.LF[:, :, 1::2], False, True)
+    ms("OKz", T.OK[:], 0.0); ms("OF", T.OF[:], 1.0)
+    for y in ("YXa", "YXb", "RB"): ms(y + "z", T[y][:, 0:16], 0.0)
+    cp("B1", "O1a", T.O1a[:], B[1][:, :, 0::2, :, 0:6])
+    pick("IDH", T.IDH[:], "XR", 128, "p")
+    for k in range(2):
+        tt("ML%d IDF" % k, "MD", T.MD[:], T.ML[:, k, :], T.IDF[:, 0:96], A.mult)
+        red("MD", "cml%d" % k, C("ml%d" % k), T.MD[:], A.add)
+        for j in range(3):
+            ts("ML%d cml%d" % (k, k), "TT%d%d" % (k, j), T.TT[:, 3 * k + j, :], T.ML[:, k, :], C("ml%d" % k), A.subtract, float(16 * (k + 1) * (j - 1)), A.is_ge)
+
+    def claim_constants_v():
+        lin("x5", "ge8", -1.0, 1.0); lin("w8", "pm", 10.0, 1.0, A.is_lt, A.mult); lin("cla", "m1", 1.0, 8.0); lin("x7", "pm", 8.0, 1.0)
+        lin("x6", "x5", "b3", 0.0); lin("j1", "p", 1.0, 1025.0); lin("j0", "p", 1.0, 1024.0); lin("cpt", "t", 2.0, "x7"); lin("cr8", "ge8", 4.0, "x6")
+        ts("XR cp", "TB", T.TB[:], T.XR[:, 0:128], C("p"), A.is_le, 4096.0, A.mult)
+        cp("GM", "GH", T.GH[:], T.GM[:]); ms("XKz", T.XK[:], 0.0); ms("KOz", T.KO[:], 0.0)
+        pick("R8", T.R8[:], "XR", 8, "cr8", "w8")
+
+    def claim_constants_s():
+        spick("MT", T.MT[:], "X16", 128, "pm")
+        spick("LA0", T.LA0[:], "X16", 128, "cla", "w16"); spick("LB0", T.LB0[:], "X16", 128, "pm", "x5")
+        spick("SR", T.SR[:], "X16", 128, "pm")
+        spick("PT0", T.PT0[:], "XR", 130, "cpt", "nhf"); spick("PT1", T.PT1[:], "XR", 130, "cpt", "hf")
+        for j in range(4): act("ID", "ID4%d" % j, T.ID4[:, j, :], T.ID[:])
+        act("ID KOz", "KO", T.KO[:, :, 0:4, :], T.ID[:])
+
+    def own_kids():
+        for blk in range(4):
+            o = B[5 + blk // 2][:, 2 * (blk % 2):2 * (blk % 2) + 2]; k = "B%d" % (5 + blk // 2)
+            mm("KO HL", k, o, T.KO[:, :, :, blk], T.HL[:, 0:256], True, False)
+            mm("KO HL", k, o, T.KO[:, :, :, blk], T.HL[:, 256:512], False, True)
+
+    for r in range(8):
+        dma("y", "L Lo", "UP%d" % r, T.UP[r::8, :], T.L[64:128, 256 * r:256 * r + 256])
+    for gg in range(8):
+        dma("y", ks("UP%d", 8), "Q%d" % gg, T.Q[16 * gg:16 * gg + 16, 0:8192], T.UP[:])
+    QK, RS, OHK = ks("Q%d", 8), ks("R%d_", 16), ks("OH%d", 8)
+    for i in range(16):
+        r, j, b = i // 2, i % 2, i % 8
+        for u in range(2):
+            mm("L Lo LRz", "B%d" % b, B[b][:, 2 * u:2 * u + 2], T.LR[0:96, :, :, 2 * j + u::4], T.L[0:96, 256 * r:256 * r + 256])
+        o = T.R[:, 512 * i:512 * i + 512]
+        if i % 2: act("B%d cbias" % b, "R%d_" % i, o, B[b][:], AF.Relu, bias=C("bias"))
+        else: ts("B%d cbias" % b, "R%d_" % i, o, B[b][:], C("bias"), A.add, 0.0, A.max)
+    sm = lambda i: T.SM[0:96, i, :]
+    sn = lambda i: T.SN[:, i, :]
+    hit0, hit1 = T.EA[0:96, 3:256:4], T.EA[0:96, 259::4]
+
+    def step1(k, qs):
+        O1, G1 = T["O1" + "ab"[k]], T["G1" + "ab"[k]]
+        for q in qs:
+            gather(S1[k][q], RS + " O1" + "ab"[k], "G1%d%d" % (k, q), G1[:, 768 * q:768 * q + 768], T.R[:], O1[:, 48 * q:48 * q + 48])
+
+    def turn(k, c):
+        G1 = T["G1" + "ab"[k]]; b = (0, 7)[c]
+        for pp in range(16):
+            mm("WD G1%d%d G1%d%d" % (k, 2 * c, k, 2 * c + 1), "B%d" % b, B[b][:, 0:2, 0:3], T.WD[:, 15 - pp:143 - pp],
+               G1[:, 1536 * c + pp:1536 * (c + 1):16], pp == 0, pp == 15)
+        cp("B%d" % b, "O2%d" % c, T.O2[:, 96 * c:96 * c + 96], B[b][:, 0:2, 0:3])
+
+    def q_nodes(k):
+        G1 = T["G1" + "ab"[k]]
+        for q in range(4):
+            for gg in range(8):
+                mm("RQ G1%d%d" % (k, q), "B1", B[1][0:96, q, gg, :, 0:4], G1[:, 768 * q + 96 * gg:768 * q + 96 * gg + 96], T.RQ[:])
+
+    def step2(k, qs):
+        for q in qs:
+            gather(S2[k][q], RS + " O2%d" % (q // 2), "G2%d" % q, T.G2[:, 768 * q:768 * q + 768], T.R[:], T.O2[:, 48 * q:48 * q + 48])
+
+    def results(k):
+        for q in range(4):
+            for h in range(2):
+                for gg in range(8):
+                    a = 768 * q + 96 * gg + 48 * h
+                    mm("LUa LUb G2%d" % q, "B%d" % (2 + h), B[2 + h][32 * q:32 * q + 32, 0:3, gg], T.LU[:], T.G2[:, a:a + 48])
+        for h in (0, 1):
+            ts("B%d" % (2 + h), "YB%d" % h, T.YB[:, 3 * h:3 * h + 3], B[2 + h][:, 0:3], 2.0 ** -13, EQ, 15.0, A.mult)
+            act("B%d cb1" % (3 - h), "Y0%d" % (1 - h), T.Y0[:, 3 - 3 * h:6 - 3 * h], B[3 - h][:, 0:3], AF.Relu, bias=C("b1"))
+        for bb in range(6):
+            for j, y in enumerate(("Y0", "YB")):
+                mm("RKa RKb %s%d" % (y, bb // 3), "B0", B[0][:, :, 0::4, :, bb], T[y][:, bb], T.RK[:, :, 4:6], j == 0, j == 1)
+        H = T.HI
+        cp("B0", "HF", T.HF[:], B[0][:, :, 0::4, 0, 0:6])
+        tt("B0 HF", "H0", H[:, 0, :], B[0][:, :, 0::4, 1, 0:6], T.HF[:], A.add)
+        ts("H0", "H1", H[:, 1, :], H[:, 0, :], 8191, AND); ts("H0", "H2", H[:, 2, :], H[:, 0, :], 8190, AND); ts("H0", "H3", H[:, 3, :], H[:, 0, :], 1, AND)
+        cp("H1", "O30", T.O3[:, 0:48], H[:, 1, :])
+        tt("H2 H3", "H4", H[:, 4, :], H[:, 2, :], H[:, 3, :], A.subtract)
+        ts("H4", "O31", T.O3[:, 48:96], H[:, 4, :], 1.0, A.add)
+
+    def lookup(k):
+        def gathers(e):
+            for c in range(4):
+                if S3[k][c] == e:
+                    gather(e, QK + " O3%d" % (c // 2), "G3%d" % c, T.G3[:, 384 * c:384 * c + 384], T.Q[:, 0:8192], T.O3[:, 24 * c:24 * c + 24])
+        x = "YX" + "ab"[k]; YX = T[x]; G1 = T["G1" + "ab"[k]]; I = T.SI
+        for gg in range(8):
+            b = 2 + gg // 4; o = B[b][:, gg % 4, 0:6]
+            mm("ID Y00 Y01", "B%d" % b, o, T.ID[:], T.Y0[:, :, gg, :], True, False)
+            mm("ID YB0 YB1", "B%d" % b, o, T.ID[:], T.YB[:, :, gg, :], False, True)
+            if gg % 4 == 3: act("B%d" % b, x + str(b - 2), YX[:, 16 + 384 * (b - 2):400 + 384 * (b - 2)], B[b][:, :, 0:6])
+        for gg in range(8):
+            mm("RKa RKb " + x + str(gg // 4), "B4", B[4][0:96, :, gg], YX[:, 16 + 96 * gg:112 + 96 * gg], T.RK[:])
+        gathers("v")
+        act("B4", "KN", T.KN[0:96], B[4][0:96])
+        gathers("s")
+        if k == 0: claim_constants_s()
+        for par in range(2):
+            for s in range(8):
+                a = 768 * par + 96 * s
+                mm("RG G3%d" % (2 * par + s // 4), "B%d" % (5 + par), B[5 + par][0:96, s // 2, :, s % 2, :], T.G3[:, a:a + 96], T.RG[:])
+        for h in range(2):
+            for q in range(4):
+                mm("LBa LBb G1%d%d" % (k, q), "B%d" % (2 + h), B[2 + h][:, 0:3], T.LB[:, 96 - 32 * q:224 - 32 * q], G1[:, 768 * q + 384 * h:768 * q + 384 * h + 384], q == 0, False)
+        tt("KN", "I0", I[0:96, 0, :], T.KN[0:96, :, :, :, 4], T.KN[0:96, :, :, :, 5], A.add)
+        ts("I0", "I1", I[0:96, 1, :], I[0:96, 0, :], 10, SHR, 7, AND); ts("I0", "I2", I[0:96, 2, :], I[0:96, 0, :], 992, AND)
+        ts("I0", "I3", I[0:96, 3, :], I[0:96, 0, :], 31, AND); ts("I0", "I4", I[0:96, 4, :], I[0:96, 0, :], 1, AND)
+        ts("I1", "m0", sm(0), I[0:96, 1, :], 1.0, A.add); ts("I3", "m2", sm(2), I[0:96, 3, :], 1.0, A.add)
+        ts("I4", "m3", sm(3), I[0:96, 4, :], -2.0, A.mult, 1.0, A.add)
+        cp("I2", "m1", sm(1), I[0:96, 2, :])
+        for q in range(4): act("m1 FWz", "FWh%d" % q, T.FW[0:96, :, 2 * q:2 * q + 2, 8], T.SM[0:96, 1, 16 * q:16 * q + 16])
+        for par in range(2):
+            b = "B%d" % (5 + par)
+            tt(b + " KN", "EQ%d" % par, T.EQ[0:96, 256 * par:256 * par + 256], B[5 + par][0:96, :, :, :, 0:4], T.KN[0:96, :, :, :, 0:4], EQ)
+            ts(b, "m%d" % (6 + par), sm(6 + par), B[5 + par][0:96, :, :, :, 0], 0.0, A.is_lt)
+        scan("EQ0 EQ1 D1", "m4", T.EA[0:96, :], T.D1[0:96, :], T.EQ[0:96, :], A.max, A.mult)
+        tt("m6 m7", "m11", sm(11), sm(7), sm(6), A.max)
+        tt("m4", "m8", sm(8), hit1, hit0, A.is_gt)
+        tt("m11 m0", "m11", sm(11), sm(11), sm(0), A.mult)
+        tt("m4 m8", "m9", sm(9), sm(8), hit0, EQ)
+        tt("m11 m9", "m12", sm(12), sm(11), sm(9), A.mult)
+
+    def select1():
+        for t in range(4):
+            tt("B5 m4", "M0%d" % t, T.M0[0:96, :, t], B[5][0:96, :, :, :, 4 + t], hit0, A.mult)
+            tt("B1 m9", "MQ%d" % t, T.MQ[0:96, :, t], B[1][0:96, :, :, :, t], sm(9), A.mult)
+        for t in range(4):
+            tt("B6 m8", "B6", B[6][0:96, :, :, :, t], B[6][0:96, :, :, :, 4 + t], sm(8), A.mult)
+
+    def select2():
+        tt("B6 " + ks("M0%d", 4), "B6", B[6][0:96, :, :, :, 4:8], B[6][0:96, :, :, :, 0:4], T.M0[0:96], A.add)
+        tt("B6 " + ks("MQ%d", 4), "P", T.P[0:96], B[6][0:96, :, :, :, 4:8], T.MQ[0:96], A.add)
+
+    def count(k):
+        for o in range(8): ts("m12", "OH%d" % o, T.OH[0:96, :, :, :, o], sm(12), float(o + 1), EQ)
+        for gg in range(8): ts(OHK + " IC", "OI%d" % gg, T.OI[0:96, :, gg], T.OH[0:96, :, gg], T.IC[0:96, gg:gg + 1], A.mult)
+        tt("m6 m7", "m10", sm(10), sm(7), sm(6), A.is_gt); tt("m10 m3", "m10", sm(10), sm(10), sm(3), A.mult)
+        tt("m10 m2", "m13", sm(13), sm(10), sm(2), A.add)
+        for q in range(4): act("m13 FWz", "FWl%d" % q, T.FW[0:96, :, 2 * q:2 * q + 2, 9], T.SM[0:96, 13, 16 * q:16 * q + 16])
+        for hf in range(2):
+            for h2 in range(2):
+                j = 1 + h2 - hf
+                mm(OHK + " TT%d%d" % (k, j), "B7", B[7][0:96, :, :, hf, :], T.TT[0:96, 3 * k + j, :], T.OH[0:96, :, :, h2, :], h2 == 0, False)
+            z = [(r0, d, h2) for r0 in range(2) for d in range(1, 4) for h2 in range(2)]
+            for r0, d, h2 in z:
+                mm(OHK + " ON", "B7", B[7][0:96, :, 4 * r0 + d:4 * r0 + 4, hf, :], T.ON[0:96, 0:96], T.OH[0:96, :, 4 * r0:4 * r0 + 4 - d, h2, :], False, (r0, d, h2) == z[-1])
+        for gg in range(8):
+            h, a = gg // 4, 96 * (gg % 4)
+            for lo, hi in ((a, min(a + 96, (a // 128 + 1) * 128)), ((a // 128 + 1) * 128, a + 96)):
+                if hi > lo:
+                    mm(ks("FWh%d", 4) + " ID " + ks("FWl%d", 4), "B%d" % (2 + h), B[2 + h][:, lo // 128, (lo % 128) // 16:(lo % 128 + hi - lo) // 16],
+                       T.FW[0:96, gg], T.ID[0:96, (lo - a) // 16:(hi - a) // 16], False, gg % 4 == 3)
+        for h in range(2): act("B%d RBz" % (2 + h), "RB%d" % h, T.RB[:, 16 + 384 * h:400 + 384 * h], B[2 + h][:, 0:3])
+
+    def first16():
+        tt(OHK + " B7", "AA", T.AA[0:96, :], B[7][0:96], T.OH[0:96], A.mult)
+        scan("AA D0", "CS", T.CS[0:96, :], T.D0[0:96, :], T.AA[0:96, :], A.min, A.add)
+        for j in range(16): ts("CS OKz", "OK%d" % j, T.OK[0:96, 16 + j::32], T.CS[0:96, 7::8], float(j + 1), EQ)
+        for h in range(2): mm("TB " + ks("ID4%d", 4), "B%d" % (2 + h), B[2 + h][:], T.TB[:], T.ID4[:], True, False)
+        for q in range(4):
+            for r0 in range(2):
+                for a in range(4):
+                    for hf in range(2):
+                        c = 32 * (16 * q + 2 * (4 * r0 + a) + hf) + 16 * (1 - hf)
+                        mm(ks("OK%d", 16) + " " + ks("OI%d", 8), "B4", B[4][32 * q:32 * q + 32, 0, :, 0, r0], T.OK[0:96, c:c + 32],
+                           T.OI[0:96, q, 4 * r0 + a, hf, :], a + hf == 0, a + hf == 4)
+
+    def fetch(k):
+        x = "YX" + "ab"[k]
+        cp("B4", "OS", T.OS[:], B[4][:, 0, :, 0, 0:2])
+        gather("v", "OS RB0 RB1", "GB", T.GB[:], T.RB[:], T.OS[:])
+        gather("vs"[k], "OS %sz %s0 %s1" % (x, x, x), "GA", T.GA[:], T[x][:], T.OS[:])
+
+    def records(k):
+        n = "N3" + "ab"[k]; N3 = T[n]
+        for q in range(4):
+            p = slice(32 * q, 32 * q + 32)
+            for o in range(8): mm("GB R8", "B4", B[4][p, o // 2, 4 * (o % 2), 0, :], T.GB[p, 32 * o:32 * o + 32], T.R8[p, :])
+        cp("B4", n + "k", N3[:, :, 16:24], B[4][:, :, 0::4, 0, :])
+        ts(n + "k", "n0", sn(0), N3[:, :, 20], -1.0, A.mult)
+        for o in range(8):
+            ts(n + "k IDH", "DG%d" % o, T.DG[:, o, :], T.IDH[:], N3[:, o, 20:21], A.mult)
+            if o % 4 == 3: mm("OF " + ks("DG%d", range(o - 3, o + 1)), "B%d" % (2 + o // 4), B[2 + o // 4][:], T.OF[:], T.DG[:, o - 3:o + 1, :], False, True)
+        if k == 0: turn(1, 1)
+        for q in range(4):
+            p = slice(32 * q, 32 * q + 32)
+            for o in range(8): mm("GA MT", "B7", B[7][p, o // 2, 4 * (o % 2)], T.GA[p, 32 * o:32 * o + 32], T.MT[p, 0:16])
+        ts(n + "k", "n3", sn(3), N3[:, :, 20], 1.0, A.min)
+        ts(n + "k cj1", "n1", sn(1), N3[:, :, 20], C("j1"), A.subtract)
+        if k == 0:
+            tt(n + "k CG0", "n5", sn(5), N3[:, :, 20], T.CG[:, 0, :], A.subtract)
+            for q in (0, 2, 1, 3):
+                if q == 1: need("t", ("t", cnt["t"]))
+                p = slice(32 * q, 32 * q + 32); b = 5 + q // 2; o = B[b][:, 2 * (q % 2):2 * (q % 2) + 2]
+                mm("LA0 GA", "B%d" % b, o, T.LA0[p, :], T.GA[p, :], True, False)
+                mm("LB0 GB", "B%d" % b, o, T.LB0[p, :], T.GB[p, :], False, True)
+
+    def winners(k):
+        n = "N3" + "ab"[k]; N3 = T[n]
+        for o in range(8):
+            act("n0 B%d" % (2 + o // 4), "AB%d" % o, T.AB[:, o, :], B[2 + o // 4][:, o % 4], AF.Abs, bias=T.SN[:, 0, o:o + 1])
+            red("AB%d" % o, "n2%d" % o, T.SN[:, 2, o:o + 1], T.AB[:, o, :], A.min)
+        act("B7", n + "c", N3[:, :, 0:16], B[7][:, :, 0::4])
+        tt("n3 " + ks("n2%d", 8), "n3", sn(3), sn(2), sn(3), A.min)
+        if k == 0:
+            tt("n3 n5", "n6", sn(6), sn(3), sn(5), A.mult); tt("n6 CG1", "n7", sn(7), sn(6), T.CG[:, 1, :], A.add)
+            for r in range(8): ts("n7 GM", "XQ%d" % r, T.XQ[:, r // 2, :, r % 2], sn(7), T.GM[:, r:r + 1], A.mult)
+            mm("SR " + ks("XQ%d", 8), "B4", B[4][:, 0, 0:4], T.SR[:], T.XQ[:])
+        tt("n3 n1", "n4", sn(4), sn(3), sn(1), A.mult)
+        ts("n4 cj0 " + n + "k", n + "o", N3[:, :, 21], sn(4), C("j0"), A.add)
+        exchange(2 + k, "%sk %sc %so" % (n, n, n), "LW" + "ab"[k], lambda r: N3[:, r, :], T["LW" + "ab"[k]][:, me, :])
+        if k == 0:
+            for h in range(2): act("B%d" % (5 + h), "DQ%d" % h, T.DQ[:, 512 * h:512 * h + 512], B[5 + h][:])
+            cp("B4", "OQ", T.OQ[:], B[4][:, 0, 0:4])
+            cp("OQ DQ0 DQ1", QK, T.Q[:].indirect(T.OQ[:]), T.DQ[:])
+
+    def nodes_back():
+        for y in range(3):
+            for t in range(4): act("P", "OP%d%d" % (y, t), T.OP[32 * t:32 * t + 32, :, :, :, :, y], T.P[32 * y:32 * y + 32, :, t])
+        for y2 in range(3):
+            for x1 in range(2):
+                hf, y = divmod(2 * y2 + x1, 3); a = 4 * (y % 2) + hf; pt = T["PT%d" % x1]
+                for h2 in range(2):
+                    mm("PT%d " % x1 + ks("OP%d%%d" % y2, 4), "B1", B[1][:, :, 0::2, y // 2, a:a + 3:2],
+                       pt[:, 1 - h2:129 - h2], T.OP[:, :, h2, :, :, y2], h2 == 0, h2 == 1)
+        act("B1", "NPa", T.NP[:, :, 0:8], B[1][:, :, 0::2, 0, :]); act("B1", "NPb", T.NP[:, :, 8:12], B[1][:, :, 0::2, 1, 0:4])
+        exchange(4, "NPa NPb", "LP", lambda r: T.NP[:, 2 * r:2 * r + 2, :], T.LP[:, me, :])
+        dma("y", "NPa NPb", "yn", T.ynodes[16 * me:16 * me + 16, :], T.NP[:, 2 * me:2 * me + 2, :])
+
+    def settle(k):
+        l = "LW" + "ab"[k]; LW = T[l]; R = l + " " + l + "o"; n = "N3" + "ab"[k]
+        act("%sk %sc %so" % (n, n, n), l + "o", LW[:, me, :], T[n][:, me, :])
+        for gg in range(8): ts(R + " MF", "XO%d" % gg, T.XO[:, gg, :], T.MF[:], LW[:, gg, 21:22], A.mult)
+        act(R, "XC", T.XC[:], LW[:, :, 0:16]); act(R + " XKz", "XK", T.XK[:, :, 0:4], LW[:, :, 16:20])
+        mm("XC ID", "B5", B[5][:, 0], T.XC[:], T.ID[:])
+        mm("GH " + ks("XO%d", 8), "B0", B[0][:, 0, 0, 0, :], T.XO[:], T.GH[:])
+        mm("XK IDF", "B7", B[7][:, 0], T.XK[:], T.IDF[:])
+        act("B5", "DC", T.DC[:], B[5][:, 0]); act("B7", "DK", T.DK[:], B[7][:, 0])
+        cp("B0", "OO", T.OO[:], B[0][:, 0, 0, 0, :])
+        cp("OO DC CN", "CN", T.CN[:].indirect(T.OO[:]), T.DC[:])
+        cp("OO DK YK0 YK1", "YK0 YK1", T.YK[:].indirect(T.OO[:]), T.DK[:])
+
+    step1(0, range(4)); turn(0, 0); step2(0, [0, 1]); turn(0, 1); q_nodes(0); step2(0, [2, 3]); claim_constants_v()
+    results(0); lookup(0); count(0); select1(); select2()
+    for y in range(3):
+        for t in range(4): cp("P", "O1b%d%d" % (y, t), T.O1b[32 * t:32 * t + 32, y::3], T.P[32 * y:32 * y + 32, :, t])
+    lastw["O1b"] = [("v", cnt["v"], "v")]
+    step1(1, [0, 1]); first16(); step1(1, [2, 3]); fetch(0); turn(1, 0); step2(1, [0]); records(0); winners(0)
+    q_nodes(1); own_kids(); step2(1, [1, 2, 3])
+    act("B5", "YK0", T.YK[:, 0:512], B[5][:]); act("B6", "YK1", T.YK[:, 512:1024], B[6][:])
+    results(1); lookup(1)
+    count(1); first16(); select1(); fetch(1); records(1); select2(); winners(1); nodes_back(); settle(0); settle(1)
+    dma("s", "CN", "yc", T.ycells[:], T.CN[:, 0:1024])
+    for r in others: dma("y", "LP", "yn%d" % r, T.ynodes[16 * r:16 * r + 16, :], T.LP[:, r, :])
+    for t in range(4): dma("s", "YK0 YK1", "yk%d" % t, T.ykids[t::4, :], T.YK[t::16, 0:1024])
+    for s, n in total.items(): need("p", (s, n))

@@ -10,7 +10,7 @@ SB = {
     "Y0": ([6, 8, 16], B16), "YB": ([6, 8, 16], B16), "YXa": ([784], B16), "YXb": ([784], B16), "RB": ([784], B16),
     "HI": ([5, 48], I32), "HF": ([48], F32), "O3": ([96], U16), "G3": ([1536], B16), "KN": ([4, 8, 2, 8], F32), "EQ": ([512], B16), "EA": ([512], B16),
     "SM": ([14, 64], F32), "SI": ([5, 64], I32), "P": ([64, 4], F32), "M0": ([64, 4], F32), "MQ": ([64, 4], F32),
-    "OH": ([4, 8, 2, 8], B16), "AA": ([512], B16), "CS": ([512], B16), "OK": ([2064], F16), "OI": ([4, 8, 2, 8], F16), "OS": ([16], U16),
+    "OH": ([4, 8, 2, 8], B16), "AA": ([512], B16), "CS": ([512], B16), "OK": ([130, 16], F16), "OI": ([4, 8, 2, 8], F16), "OS": ([16], U16),
     "GA": ([256], B16), "GB": ([256], B16), "FW": ([8, 8, 16], B16), "N3a": ([8, 24], F32), "N3b": ([8, 24], F32),
     "DG": ([8, 128], F16), "AB": ([8, 128], B16), "SN": ([8, 8], F32), "DQ": ([1024], B16), "OQ": ([64], U16), "XQ": ([4, 8, 2], F32),
     "LWa": ([8, 24], F32), "LWb": ([8, 24], F32), "LP": ([8, 24], F32), "OP": ([8, 2, 2, 2, 3], F32), "NP": ([16, 12], F32),
@@ -29,10 +29,9 @@ SCRATCH["D"] = ("dram", [8, 128, 256], B16)
 SCRATCH["DN"] = ("dram", [8, 128, 24], I32)
 for _b in range(8):
     SCRATCH["B%d" % _b] = ("psum", [128, 4, 8, 2, 8], F32)
-SEMAPHORES = ["v", "s", "t", "p"] + ["d%d" % i for i in range(48)] + ["rl%d" % i for i in range(5)] + ["rr%d" % i for i in range(5)]
+SEMAPHORES = ["v", "s", "t", "p", "rn"] + ["d%d" % i for i in range(48)] + ["rl%d" % i for i in range(5)] + ["rr%d" % i for i in range(5)]
 S1 = ("svsv", "sssv")
 S2 = ("svsv", "ssss")
-S3 = ("vvvs", "vvvs")
 
 
 def rank_program(g, core, T, topo):
@@ -82,18 +81,20 @@ def rank_program(g, core, T, topo):
     far = [r for r in others if topo.die(T.cores[r]) != topo.die(core)]
     near = [r for r in others if r not in far]
 
-    def exchange(k, R, W, src, dst):
+    def exchange(k, R, W, src, dst, split=False):
         deps("p", R.split(), [])
         tr = []
         for r in others:
             c = T.cores[r]; en = topo.engines(core, c); rid, pid, _ = topo.addr(c)
             en = en[0::2][2 * far.index(r):] if r in far else en[1::2][2 * near.index(r):]
             tr.append(RemoteDMATransfer(dst_ids=[DstId(rid=rid, pnc=pid)], dma_engine_mask=(1 << en[0]) | (1 << en[1]),
-                                        remote_sem=T.sem["rr%d" % k], src=src(r), dst=dst))
+                                        remote_sem=T.sem["rn" if split and r in near else "rr%d" % k], src=src(r), dst=dst))
         g.remote_dma_fused(tr, local_sem=T.sem["rl%d" % k])
         total["rl%d" % k] = total["rr%d" % k] = 14
         mark(("rl%d" % k, 14, "dma"), R.split(), [])
-        lastw[W] = [("rr%d" % k, 14, "dma")]
+        if split:
+            total["rn"], total["rr%d" % k] = 2 * len(near), 2 * len(far); lastw[W + "n"] = [("rn", total["rn"], "dma")]
+        lastw[W] = [("rr%d" % k, total["rr%d" % k], "dma")]
 
     def ks(f, n): return " ".join(f % j for j in (range(n) if isinstance(n, int) else n))
     def mm(R, W, out, l, r, st=True, sp=True): op("t", R, W, lambda: PE.matmul(out, l, r, st, sp))
@@ -115,8 +116,8 @@ def rank_program(g, core, T, topo):
     dma("y", "", "KI", T.KI[:], T.kids[:])
     dma("s", "", "CN", T.CN[:, 0:1024], T.cells[:])
     dma("y", "", "DN", T.DN[:], T.nodes[:])
-    dma("s", "", "Dc", T.D[:, 0:64, :], T.cells[:])
     dma("y", "", "WI", T.WI[:], T.wt[:])
+    dma("s", "CN", "Dc", T.D[:, 0:64, :], T.CN[:, 0:1024])
     op("p", "", "PI", lambda: g.iota(T.PI[:], [[0, 1]], 0, 1))
     iota("XR", T.XR[:], [[1, 144]], 0)
     iota("X16", T.X16[:], [[0, 8], [1, 16]], 0)
@@ -125,9 +126,9 @@ def rank_program(g, core, T, topo):
     iota("VT2", T.VT[:, 2, :], [[8, 4], [1, 4]], 18)
     iota("VT3a", T.VT[:, 3, 0:8], [[0, 2], [1, 4]], 4)
     iota("VT3b", T.VT[:, 3, 8:16], [[1, 4], [0, 2]], 0)
+    exchange(0, "DN", "LN", lambda r: T.DN[r], T.LN[:, me, :])
     iota("ML0", T.ML[:, 0, :], [[32, 6], [1, 16]], 0)
     iota("ML1", T.ML[:, 1, :], [[16, 2], [64, 3], [1, 16]], 0)
-    exchange(0, "DN", "LN", lambda r: T.DN[r], T.LN[:, me, :])
     dma("y", "DN", "LNo", T.LN[:, me, :], T.DN[me])
 
     names = ["p", "b0", "pm", "pg", "hf", "t", "i4", "t2", "p8", "m1", "k11", "b3"]
@@ -155,14 +156,14 @@ def rank_program(g, core, T, topo):
 
     ts("KI", "KHa", T.KH[:, 0:256], T.KI[:], 8160, AND)
     ts("KI", "KHb", T.KH[:, 256:512], T.KI[:], 31, AND)
-    cp("KHa KHb", "HL", T.HL[:], T.KH[:])
-    dma("y", "HL", "Dh", T.D[:, 64:80, :], T.HL[:, 0:256])
-    dma("y", "HL", "Dl", T.D[:, 80:96, :], T.HL[:, 256:512])
+    cp("KHa", "HLa", T.HL[:, 0:256], T.KH[:, 0:256]); cp("KHb", "HLb", T.HL[:, 256:512], T.KH[:, 256:512])
+    dma("y", "HLa", "Dh", T.D[:, 64:80, :], T.HL[:, 0:256])
+    dma("y", "HLb", "Dl", T.D[:, 80:96, :], T.HL[:, 256:512])
     mm("PM CN", "B0", B[0][:], T.PM[:, 1:129], T.CN[:, 0:512], True, False)
     mm("PM CN", "B0", B[0][:], T.PM[:, 0:128], T.CN[:, 512:1024], False, True)
     act("B0", "PB", T.PB[:], B[0][:])
     dma("s", "PB", "Dp", T.D[:, 96:128, :], T.PB[:])
-    exchange(1, "Dc Dh Dl Dp", "L", lambda r: T.D[r], T.L[:, 256 * me:256 * me + 256])
+    exchange(1, "Dc Dh Dl Dp", "L", lambda r: T.D[r], T.L[:, 256 * me:256 * me + 256], True)
     dma("y", "Dc Dh Dl Dp", "Lo", T.L[:, 256 * me:256 * me + 256], T.D[me])
     iota("FWz", T.FW[:], [[0, 1024]], 0)
     iota("D1", T.D1[:], [[0, 128], [-1, 4]], 1)
@@ -223,22 +224,19 @@ def rank_program(g, core, T, topo):
     lin("ge8", "pm", 8.0, 1.0, A.is_ge, A.mult); lin("x4", "hf", 16.0, "t")
     ts("GM WC RKz", "RKa", T.RK[:, :, 4], T.GM[:], T.WC[:, 0:1], A.mult)
     ts("GM WC RKz", "RKb", T.RK[:, :, 5], T.GM[:], T.WC[:, 1:2], A.mult)
-    table("fs", 3, "VT3a VT3b")
-    lin("x3", "ge8", "b0", 255.0, A.mult, A.mult); lin("clb", "pm", 93.0, "x4", A.add, A.add); lin("crg", "pg", 8.0, "fs"); lin("wg", "x3", 1.0, 1.0)
-    spick("LBa", T.LB[:, 0:144], "XR", 144, "clb", "km")
-    ms("LBb", T.LB[:, 144:224], 0.0)
-    pick("RG", T.RG[:], "XR", 64, "crg", "wg")
-    pick("IDF", T.IDF[:], "XR", 128, "p")
     cp("LN LNo", "LF", T.LF[:], T.LN[:])
     for h2 in range(2):
         pw = T["PW%d" % h2]
         mm("LF PW%d" % h2, "B1", B[1][:, :, 2 * h2::4, :, 0:6], pw[:, 16:144], T.LF[:, :, 0::2], True, False)
         mm("LF PW%d" % h2, "B1", B[1][:, :, 2 * h2::4, :, 0:6], pw[:, 0:128], T.LF[:, :, 1::2], False, True)
-    ms("OKz", T.OK[:], 0.0); ms("OF", T.OF[:], 1.0)
-    for y in ("YXa", "YXb", "RB"): ms(y + "z", T[y][:, 0:16], 0.0)
+    table("fs", 3, "VT3a VT3b")
+    lin("x3", "ge8", "b0", 255.0, A.mult, A.mult); lin("clb", "pm", 93.0, "x4", A.add, A.add); lin("crg", "pg", 8.0, "fs"); lin("wg", "x3", 1.0, 1.0)
+    spick("LBa", T.LB[:, 0:144], "XR", 144, "clb", "km")
+    ms("LBb", T.LB[:, 144:224], 0.0)
+    pick("RG", T.RG[:], "XR", 64, "crg", "wg")
     cp("B1", "O1a", T.O1a[:], B[1][:, :, 0::2, :, 0:6])
-    pick("IDH", T.IDH[:], "XR", 128, "p")
-    for k in range(2):
+
+    def order(k):
         tt("ML%d IDF" % k, "MD", T.MD[:], T.ML[:, k, :], T.IDF[:, 0:96], A.mult)
         red("MD", "cml%d" % k, C("ml%d" % k), T.MD[:], A.add)
         for j in range(3):
@@ -248,7 +246,7 @@ def rank_program(g, core, T, topo):
         lin("x5", "ge8", -1.0, 1.0); lin("w8", "pm", 10.0, 1.0, A.is_lt, A.mult); lin("cla", "m1", 1.0, 8.0); lin("x7", "pm", 8.0, 1.0)
         lin("x6", "x5", "b3", 0.0); lin("j1", "p", 1.0, 1025.0); lin("j0", "p", 1.0, 1024.0); lin("cpt", "t", 2.0, "x7"); lin("cr8", "ge8", 4.0, "x6")
         ts("XR cp", "TB", T.TB[:], T.XR[:, 0:128], C("p"), A.is_le, 4096.0, A.mult)
-        cp("GM", "GH", T.GH[:], T.GM[:]); ms("XKz", T.XK[:], 0.0); ms("KOz", T.KO[:], 0.0)
+        cp("GM", "GH", T.GH[:], T.GM[:]); ms("OF", T.OF[:], 1.0); pick("IDH", T.IDH[:], "XR", 128, "p")
         pick("R8", T.R8[:], "XR", 8, "cr8", "w8")
 
     def claim_constants_s():
@@ -257,26 +255,31 @@ def rank_program(g, core, T, topo):
         spick("SR", T.SR[:], "X16", 128, "pm")
         spick("PT0", T.PT0[:], "XR", 130, "cpt", "nhf"); spick("PT1", T.PT1[:], "XR", 130, "cpt", "hf")
         for j in range(4): act("ID", "ID4%d" % j, T.ID4[:, j, :], T.ID[:])
-        act("ID KOz", "KO", T.KO[:, :, 0:4, :], T.ID[:])
 
     def own_kids():
         for blk in range(4):
-            o = B[5 + blk // 2][:, 2 * (blk % 2):2 * (blk % 2) + 2]; k = "B%d" % (5 + blk // 2)
-            mm("KO HL", k, o, T.KO[:, :, :, blk], T.HL[:, 0:256], True, False)
-            mm("KO HL", k, o, T.KO[:, :, :, blk], T.HL[:, 256:512], False, True)
+            b = 7 * (blk // 2); o = B[b][:, 2 * (blk % 2):2 * (blk % 2) + 2]
+            mm("KO HLa", "B%d" % b, o, T.KO[:, :, :, blk], T.HL[:, 0:256], True, False)
+            mm("KO HLb", "B%d" % b, o, T.KO[:, :, :, blk], T.HL[:, 256:512], False, True)
+        act("B0", "YK0", T.YK[:, 0:512], B[0][:]); act("B7", "YK1", T.YK[:, 512:1024], B[7][:])
 
-    for r in range(8):
-        dma("y", "L Lo", "UP%d" % r, T.UP[r::8, :], T.L[64:128, 256 * r:256 * r + 256])
-    for gg in range(8):
-        dma("y", ks("UP%d", 8), "Q%d" % gg, T.Q[16 * gg:16 * gg + 16, 0:8192], T.UP[:])
-    QK, RS, OHK = ks("Q%d", 8), ks("R%d_", 16), ks("OH%d", 8)
-    for i in range(16):
-        r, j, b = i // 2, i % 2, i % 8
+    came = lambda r: "Lo" if r == me else "Ln" if r in near else "L"
+    for r in [me] + near + far:
+        dma("y", came(r), "UP%d" % r, T.UP[64 * (r // 4) + r % 4:64 * (r // 4) + 64:4, :], T.L[64:128, 256 * r:256 * r + 256])
+    for h in (me // 4, 1 - me // 4):
+        for gg in range(8):
+            dma("y", ks("UP%d", range(4 * h, 4 * h + 4)), "Q%d" % (8 * h + gg), T.Q[16 * gg:16 * gg + 16, 4096 * h:4096 * h + 4096], T.UP[64 * h:64 * h + 64, :])
+    QK, RS, OHK = ks("Q%d", 16), ks("R%d_", 16), ks("OH%d", 8)
+    for n, i in enumerate(2 * r + j for r in [me] + near + far for j in range(2)):
+        r, j, b = i // 2, i % 2, n % 8
         for u in range(2):
-            mm("L Lo LRz", "B%d" % b, B[b][:, 2 * u:2 * u + 2], T.LR[0:96, :, :, 2 * j + u::4], T.L[0:96, 256 * r:256 * r + 256])
+            mm(came(r) + " LRz", "B%d" % b, B[b][:, 2 * u:2 * u + 2], T.LR[0:96, :, :, 2 * j + u::4], T.L[0:96, 256 * r:256 * r + 256])
         o = T.R[:, 512 * i:512 * i + 512]
         if i % 2: act("B%d cbias" % b, "R%d_" % i, o, B[b][:], AF.Relu, bias=C("bias"))
         else: ts("B%d cbias" % b, "R%d_" % i, o, B[b][:], C("bias"), A.add, 0.0, A.max)
+        if n == 1:
+            pick("IDF", T.IDF[:], "XR", 128, "p"); order(0); ms("OKz", T.OK[:, 0::2, :], 0.0)
+            for y in ("YXa", "YXb", "RB"): ms(y + "z", T[y][:, 0:16], 0.0)
     sm = lambda i: T.SM[0:96, i, :]
     sn = lambda i: T.SN[:, i, :]
     hit0, hit1 = T.EA[0:96, 3:256:4], T.EA[0:96, 259::4]
@@ -286,12 +289,12 @@ def rank_program(g, core, T, topo):
         for q in qs:
             gather(S1[k][q], RS + " O1" + "ab"[k], "G1%d%d" % (k, q), G1[:, 768 * q:768 * q + 768], T.R[:], O1[:, 48 * q:48 * q + 48])
 
-    def turn(k, c):
+    def turn(k, c, copy=True):
         G1 = T["G1" + "ab"[k]]; b = (0, 7)[c]
         for pp in range(16):
             mm("WD G1%d%d G1%d%d" % (k, 2 * c, k, 2 * c + 1), "B%d" % b, B[b][:, 0:2, 0:3], T.WD[:, 15 - pp:143 - pp],
                G1[:, 1536 * c + pp:1536 * (c + 1):16], pp == 0, pp == 15)
-        cp("B%d" % b, "O2%d" % c, T.O2[:, 96 * c:96 * c + 96], B[b][:, 0:2, 0:3])
+        if copy: cp("B%d" % b, "O2%d" % c, T.O2[:, 96 * c:96 * c + 96], B[b][:, 0:2, 0:3])
 
     def q_nodes(k):
         G1 = T["G1" + "ab"[k]]
@@ -315,6 +318,7 @@ def rank_program(g, core, T, topo):
         for bb in range(6):
             for j, y in enumerate(("Y0", "YB")):
                 mm("RKa RKb %s%d" % (y, bb // 3), "B0", B[0][:, :, 0::4, :, bb], T[y][:, bb], T.RK[:, :, 4:6], j == 0, j == 1)
+        if k == 0: ms("XKz", T.XK[:], 0.0); ms("KOz", T.KO[:], 0.0)
         H = T.HI
         cp("B0", "HF", T.HF[:], B[0][:, :, 0::4, 0, 0:6])
         tt("B0 HF", "H0", H[:, 0, :], B[0][:, :, 0::4, 1, 0:6], T.HF[:], A.add)
@@ -324,10 +328,8 @@ def rank_program(g, core, T, topo):
         ts("H4", "O31", T.O3[:, 48:96], H[:, 4, :], 1.0, A.add)
 
     def lookup(k):
-        def gathers(e):
-            for c in range(4):
-                if S3[k][c] == e:
-                    gather(e, QK + " O3%d" % (c // 2), "G3%d" % c, T.G3[:, 384 * c:384 * c + 384], T.Q[:, 0:8192], T.O3[:, 24 * c:24 * c + 24])
+        def look(e, c):
+            gather(e, QK + " O3%d" % (c // 2), "G3%d" % c, T.G3[:, 384 * c:384 * c + 384], T.Q[:, 0:8192], T.O3[:, 24 * c:24 * c + 24])
         x = "YX" + "ab"[k]; YX = T[x]; G1 = T["G1" + "ab"[k]]; I = T.SI
         for gg in range(8):
             b = 2 + gg // 4; o = B[b][:, gg % 4, 0:6]
@@ -336,10 +338,11 @@ def rank_program(g, core, T, topo):
             if gg % 4 == 3: act("B%d" % b, x + str(b - 2), YX[:, 16 + 384 * (b - 2):400 + 384 * (b - 2)], B[b][:, :, 0:6])
         for gg in range(8):
             mm("RKa RKb " + x + str(gg // 4), "B4", B[4][0:96, :, gg], YX[:, 16 + 96 * gg:112 + 96 * gg], T.RK[:])
-        gathers("v")
+        look("v", 0); look("v", 1); look("s", 2)
         act("B4", "KN", T.KN[0:96], B[4][0:96])
-        gathers("s")
-        if k == 0: claim_constants_s()
+        look("s", 3)
+        if k == 0: claim_constants_s(); act("ID KOz", "KO", T.KO[:, :, 0:4, :], T.ID[:])
+        else: own_kids()
         for par in range(2):
             for s in range(8):
                 a = 768 * par + 96 * s
@@ -356,14 +359,17 @@ def rank_program(g, core, T, topo):
         for q in range(4): act("m1 FWz", "FWh%d" % q, T.FW[0:96, :, 2 * q:2 * q + 2, 8], T.SM[0:96, 1, 16 * q:16 * q + 16])
         for par in range(2):
             b = "B%d" % (5 + par)
-            tt(b + " KN", "EQ%d" % par, T.EQ[0:96, 256 * par:256 * par + 256], B[5 + par][0:96, :, :, :, 0:4], T.KN[0:96, :, :, :, 0:4], EQ)
             ts(b, "m%d" % (6 + par), sm(6 + par), B[5 + par][0:96, :, :, :, 0], 0.0, A.is_lt)
-        scan("EQ0 EQ1 D1", "m4", T.EA[0:96, :], T.D1[0:96, :], T.EQ[0:96, :], A.max, A.mult)
+            tt(b + " KN", "EQ%d" % par, T.EQ[0:96, 256 * par:256 * par + 256], B[5 + par][0:96, :, :, :, 0:4], T.KN[0:96, :, :, :, 0:4], EQ)
         tt("m6 m7", "m11", sm(11), sm(7), sm(6), A.max)
-        tt("m4", "m8", sm(8), hit1, hit0, A.is_gt)
+        scan("EQ0 EQ1 D1", "m4", T.EA[0:96, :], T.D1[0:96, :], T.EQ[0:96, :], A.max, A.mult)
         tt("m11 m0", "m11", sm(11), sm(11), sm(0), A.mult)
+        tt("m4", "m8", sm(8), hit1, hit0, A.is_gt)
+        tt("m6 m7", "m10", sm(10), sm(7), sm(6), A.is_gt)
         tt("m4 m8", "m9", sm(9), sm(8), hit0, EQ)
+        tt("m10 m3", "m10", sm(10), sm(10), sm(3), A.mult)
         tt("m11 m9", "m12", sm(12), sm(11), sm(9), A.mult)
+        tt("m10 m2", "m13", sm(13), sm(10), sm(2), A.add)
 
     def select1():
         for t in range(4):
@@ -379,8 +385,6 @@ def rank_program(g, core, T, topo):
     def count(k):
         for o in range(8): ts("m12", "OH%d" % o, T.OH[0:96, :, :, :, o], sm(12), float(o + 1), EQ)
         for gg in range(8): ts(OHK + " IC", "OI%d" % gg, T.OI[0:96, :, gg], T.OH[0:96, :, gg], T.IC[0:96, gg:gg + 1], A.mult)
-        tt("m6 m7", "m10", sm(10), sm(7), sm(6), A.is_gt); tt("m10 m3", "m10", sm(10), sm(10), sm(3), A.mult)
-        tt("m10 m2", "m13", sm(13), sm(10), sm(2), A.add)
         for q in range(4): act("m13 FWz", "FWl%d" % q, T.FW[0:96, :, 2 * q:2 * q + 2, 9], T.SM[0:96, 13, 16 * q:16 * q + 16])
         for hf in range(2):
             for h2 in range(2):
@@ -400,14 +404,14 @@ def rank_program(g, core, T, topo):
     def first16():
         tt(OHK + " B7", "AA", T.AA[0:96, :], B[7][0:96], T.OH[0:96], A.mult)
         scan("AA D0", "CS", T.CS[0:96, :], T.D0[0:96, :], T.AA[0:96, :], A.min, A.add)
-        for j in range(16): ts("CS OKz", "OK%d" % j, T.OK[0:96, 16 + j::32], T.CS[0:96, 7::8], float(j + 1), EQ)
+        for j in range(16): ts("CS OKz", "OK%d" % j, T.OK[0:96, 1:128:2, j], T.CS[0:96, 7::8], float(j + 1), EQ)
         for h in range(2): mm("TB " + ks("ID4%d", 4), "B%d" % (2 + h), B[2 + h][:], T.TB[:], T.ID4[:], True, False)
         for q in range(4):
             for r0 in range(2):
                 for a in range(4):
                     for hf in range(2):
-                        c = 32 * (16 * q + 2 * (4 * r0 + a) + hf) + 16 * (1 - hf)
-                        mm(ks("OK%d", 16) + " " + ks("OI%d", 8), "B4", B[4][32 * q:32 * q + 32, 0, :, 0, r0], T.OK[0:96, c:c + 32],
+                        c = 2 * (16 * q + 2 * (4 * r0 + a) + hf) + 1 - hf
+                        mm(ks("OK%d", 16) + " " + ks("OI%d", 8), "B4", B[4][32 * q:32 * q + 32, 0, :, 0, r0], T.OK[0:96, c:c + 2, :],
                            T.OI[0:96, q, 4 * r0 + a, hf, :], a + hf == 0, a + hf == 4)
 
     def fetch(k):
@@ -415,6 +419,28 @@ def rank_program(g, core, T, topo):
         cp("B4", "OS", T.OS[:], B[4][:, 0, :, 0, 0:2])
         gather("v", "OS RB0 RB1", "GB", T.GB[:], T.RB[:], T.OS[:])
         gather("vs"[k], "OS %sz %s0 %s1" % (x, x, x), "GA", T.GA[:], T[x][:], T.OS[:])
+
+    def cells_turned():
+        for q in range(4):
+            p = slice(32 * q, 32 * q + 32)
+            for o in range(8): mm("GA MT", "B7", B[7][p, o // 2, 4 * (o % 2)], T.GA[p, 32 * o:32 * o + 32], T.MT[p, 0:16])
+
+    def nodes_moved():
+        for y in range(3):
+            for t in range(4): act("P", "OP%d%d" % (y, t), T.OP[32 * t:32 * t + 32, :, :, :, :, y], T.P[32 * y:32 * y + 32, :, t])
+
+    def nodes_turned():
+        for y2 in range(3):
+            for x1 in range(2):
+                hf, y = divmod(2 * y2 + x1, 3); a = 4 * (y % 2) + hf; pt = T["PT%d" % x1]
+                for h2 in range(2):
+                    mm("PT%d " % x1 + ks("OP%d%%d" % y2, 4), "B1", B[1][:, :, 0::2, y // 2, a:a + 3:2],
+                       pt[:, 1 - h2:129 - h2], T.OP[:, :, h2, :, :, y2], h2 == 0, h2 == 1)
+
+    def nodes_sent():
+        act("B1", "NPa", T.NP[:, :, 0:8], B[1][:, :, 0::2, 0, :]); act("B1", "NPb", T.NP[:, :, 8:12], B[1][:, :, 0::2, 1, 0:4])
+        exchange(4, "NPa NPb", "LP", lambda r: T.NP[:, 2 * r:2 * r + 2, :], T.LP[:, me, :])
+        dma("y", "NPa NPb", "yn", T.ynodes[16 * me:16 * me + 16, :], T.NP[:, 2 * me:2 * me + 2, :])
 
     def records(k):
         n = "N3" + "ab"[k]; N3 = T[n]
@@ -426,51 +452,40 @@ def rank_program(g, core, T, topo):
         for o in range(8):
             ts(n + "k IDH", "DG%d" % o, T.DG[:, o, :], T.IDH[:], N3[:, o, 20:21], A.mult)
             if o % 4 == 3: mm("OF " + ks("DG%d", range(o - 3, o + 1)), "B%d" % (2 + o // 4), B[2 + o // 4][:], T.OF[:], T.DG[:, o - 3:o + 1, :], False, True)
-        if k == 0: turn(1, 1)
-        for q in range(4):
-            p = slice(32 * q, 32 * q + 32)
-            for o in range(8): mm("GA MT", "B7", B[7][p, o // 2, 4 * (o % 2)], T.GA[p, 32 * o:32 * o + 32], T.MT[p, 0:16])
+        if k == 1: cells_turned(); nodes_turned()
         ts(n + "k", "n3", sn(3), N3[:, :, 20], 1.0, A.min)
         ts(n + "k cj1", "n1", sn(1), N3[:, :, 20], C("j1"), A.subtract)
         if k == 0:
             tt(n + "k CG0", "n5", sn(5), N3[:, :, 20], T.CG[:, 0, :], A.subtract)
+            order(1)
             for q in (0, 2, 1, 3):
                 if q == 1: need("t", ("t", cnt["t"]))
                 p = slice(32 * q, 32 * q + 32); b = 5 + q // 2; o = B[b][:, 2 * (q % 2):2 * (q % 2) + 2]
                 mm("LA0 GA", "B%d" % b, o, T.LA0[p, :], T.GA[p, :], True, False)
                 mm("LB0 GB", "B%d" % b, o, T.LB0[p, :], T.GB[p, :], False, True)
+            turn(1, 1, False)
 
     def winners(k):
         n = "N3" + "ab"[k]; N3 = T[n]
         for o in range(8):
             act("n0 B%d" % (2 + o // 4), "AB%d" % o, T.AB[:, o, :], B[2 + o // 4][:, o % 4], AF.Abs, bias=T.SN[:, 0, o:o + 1])
             red("AB%d" % o, "n2%d" % o, T.SN[:, 2, o:o + 1], T.AB[:, o, :], A.min)
-        act("B7", n + "c", N3[:, :, 0:16], B[7][:, :, 0::4])
+        if k == 1: act("B7", n + "c", N3[:, :, 0:16], B[7][:, :, 0::4])
         tt("n3 " + ks("n2%d", 8), "n3", sn(3), sn(2), sn(3), A.min)
         if k == 0:
             tt("n3 n5", "n6", sn(6), sn(3), sn(5), A.mult); tt("n6 CG1", "n7", sn(7), sn(6), T.CG[:, 1, :], A.add)
             for r in range(8): ts("n7 GM", "XQ%d" % r, T.XQ[:, r // 2, :, r % 2], sn(7), T.GM[:, r:r + 1], A.mult)
             mm("SR " + ks("XQ%d", 8), "B4", B[4][:, 0, 0:4], T.SR[:], T.XQ[:])
+            cp("B7", "O21", T.O2[:, 96:192], B[7][:, 0:2, 0:3])
         tt("n3 n1", "n4", sn(4), sn(3), sn(1), A.mult)
         ts("n4 cj0 " + n + "k", n + "o", N3[:, :, 21], sn(4), C("j0"), A.add)
-        exchange(2 + k, "%sk %sc %so" % (n, n, n), "LW" + "ab"[k], lambda r: N3[:, r, :], T["LW" + "ab"[k]][:, me, :])
         if k == 0:
             for h in range(2): act("B%d" % (5 + h), "DQ%d" % h, T.DQ[:, 512 * h:512 * h + 512], B[5 + h][:])
             cp("B4", "OQ", T.OQ[:], B[4][:, 0, 0:4])
             cp("OQ DQ0 DQ1", QK, T.Q[:].indirect(T.OQ[:]), T.DQ[:])
-
-    def nodes_back():
-        for y in range(3):
-            for t in range(4): act("P", "OP%d%d" % (y, t), T.OP[32 * t:32 * t + 32, :, :, :, :, y], T.P[32 * y:32 * y + 32, :, t])
-        for y2 in range(3):
-            for x1 in range(2):
-                hf, y = divmod(2 * y2 + x1, 3); a = 4 * (y % 2) + hf; pt = T["PT%d" % x1]
-                for h2 in range(2):
-                    mm("PT%d " % x1 + ks("OP%d%%d" % y2, 4), "B1", B[1][:, :, 0::2, y // 2, a:a + 3:2],
-                       pt[:, 1 - h2:129 - h2], T.OP[:, :, h2, :, :, y2], h2 == 0, h2 == 1)
-        act("B1", "NPa", T.NP[:, :, 0:8], B[1][:, :, 0::2, 0, :]); act("B1", "NPb", T.NP[:, :, 8:12], B[1][:, :, 0::2, 1, 0:4])
-        exchange(4, "NPa NPb", "LP", lambda r: T.NP[:, 2 * r:2 * r + 2, :], T.LP[:, me, :])
-        dma("y", "NPa NPb", "yn", T.ynodes[16 * me:16 * me + 16, :], T.NP[:, 2 * me:2 * me + 2, :])
+            cells_turned(); q_nodes(1); step2(1, [1, 2, 3])
+            act("B7", n + "c", N3[:, :, 0:16], B[7][:, :, 0::4])
+        exchange(2 + k, "%sk %sc %so" % (n, n, n), "LW" + "ab"[k], lambda r: N3[:, r, :], T["LW" + "ab"[k]][:, me, :])
 
     def settle(k):
         l = "LW" + "ab"[k]; LW = T[l]; R = l + " " + l + "o"; n = "N3" + "ab"[k]
@@ -478,8 +493,8 @@ def rank_program(g, core, T, topo):
         for gg in range(8): ts(R + " MF", "XO%d" % gg, T.XO[:, gg, :], T.MF[:], LW[:, gg, 21:22], A.mult)
         act(R, "XC", T.XC[:], LW[:, :, 0:16]); act(R + " XKz", "XK", T.XK[:, :, 0:4], LW[:, :, 16:20])
         mm("XC ID", "B5", B[5][:, 0], T.XC[:], T.ID[:])
-        mm("GH " + ks("XO%d", 8), "B0", B[0][:, 0, 0, 0, :], T.XO[:], T.GH[:])
         mm("XK IDF", "B7", B[7][:, 0], T.XK[:], T.IDF[:])
+        mm("GH " + ks("XO%d", 8), "B0", B[0][:, 0, 0, 0, :], T.XO[:], T.GH[:])
         act("B5", "DC", T.DC[:], B[5][:, 0]); act("B7", "DK", T.DK[:], B[7][:, 0])
         cp("B0", "OO", T.OO[:], B[0][:, 0, 0, 0, :])
         cp("OO DC CN", "CN", T.CN[:].indirect(T.OO[:]), T.DC[:])
@@ -491,11 +506,9 @@ def rank_program(g, core, T, topo):
         for t in range(4): cp("P", "O1b%d%d" % (y, t), T.O1b[32 * t:32 * t + 32, y::3], T.P[32 * y:32 * y + 32, :, t])
     lastw["O1b"] = [("v", cnt["v"], "v")]
     step1(1, [0, 1]); first16(); step1(1, [2, 3]); fetch(0); turn(1, 0); step2(1, [0]); records(0); winners(0)
-    q_nodes(1); own_kids(); step2(1, [1, 2, 3])
-    act("B5", "YK0", T.YK[:, 0:512], B[5][:]); act("B6", "YK1", T.YK[:, 512:1024], B[6][:])
     results(1); lookup(1)
-    count(1); first16(); select1(); fetch(1); records(1); select2(); winners(1); nodes_back(); settle(0); settle(1)
+    count(1); first16(); select1(); fetch(1); select2(); nodes_moved(); records(1); winners(1); nodes_sent(); settle(0); settle(1)
     dma("s", "CN", "yc", T.ycells[:], T.CN[:, 0:1024])
     for r in others: dma("y", "LP", "yn%d" % r, T.ynodes[16 * r:16 * r + 16, :], T.LP[:, r, :])
-    for t in range(4): dma("s", "YK0 YK1", "yk%d" % t, T.ykids[t::4, :], T.YK[t::16, 0:1024])
+    for t in range(4): dma("sy"[t % 2], "YK0 YK1", "yk%d" % t, T.ykids[t::4, :], T.YK[t::16, 0:1024])
     for s, n in total.items(): need("p", (s, n))

@@ -3,35 +3,77 @@ from concourse.mybir import AluOpType as A, AxisListType, ActivationFunctionType
 
 F32, B16, I32, F16, U16 = "float32", "bfloat16", "int32", "float16", "uint16"
 SB = {
-    "KI": ([256], I32), "KH": ([512], I32), "HL": ([512], B16), "CN": ([1152], B16), "YK": ([1152], F32), "PB": ([512], B16),
+    "KI": ([256], I32), "KH": ([512], I32), "HL": ([512], B16), "CN": ([1168], B16), "YK": ([1168], F32), "PB": ([512], B16),
     "WI": ([1], I32), "WH": ([2], I32), "WB": ([2], B16), "WC": ([2], F32),
-    "L": ([2048], B16), "LN": ([8, 24], I32), "LF": ([8, 24], F32), "UP": ([1024], B16), "R": ([8192], B16), "Q": ([9216], B16),
+    "L": ([2048], B16), "LN": ([8, 24], I32), "LF": ([8, 24], F32), "UP": ([1024], B16), "R": ([8192], B16), "Q": ([9248], B16),
     "O1a": ([192], U16), "O1b": ([192], U16), "G1a": ([3072], B16), "G1b": ([3072], B16), "O2": ([192], U16), "G2": ([3072], B16),
-    "Y0": ([6, 8, 16], B16), "YB": ([6, 8, 16], B16), "YXa": ([784], B16), "YXb": ([784], B16), "RB": ([784], B16),
-    "HI": ([5, 48], I32), "HF": ([48], F32), "O3": ([96], U16), "G3": ([1536], B16), "KN": ([4, 8, 2, 8], F32), "EQ": ([512], B16), "EA": ([512], B16),
-    "SM": ([14, 64], F32), "SI": ([5, 64], I32), "P": ([64, 4], F32), "M0": ([64, 4], F32), "MQ": ([64, 4], F32),
-    "OH": ([4, 8, 2, 8], B16), "AA": ([512], B16), "CS": ([512], B16), "OK": ([130, 16], F16), "OI": ([4, 8, 2, 8], F16), "OS": ([16], U16),
-    "GA": ([256], B16), "GB": ([256], B16), "FW": ([8, 8, 16], B16), "N3a": ([8, 24], F32), "N3b": ([8, 24], F32),
-    "DG": ([8, 128], F16), "AB": ([8, 128], B16), "SN": ([8, 8], F32), "DQ": ([1024], B16), "OQ": ([64], U16), "XQ": ([4, 8, 2], F32),
-    "LWa": ([8, 24], F32), "LWb": ([8, 24], F32), "LP": ([8, 24], F32), "OP": ([8, 2, 2, 2, 3], F32), "NP": ([16, 12], F32),
-    "XC": ([8, 16], B16), "XK": ([8, 16], F32), "XO": ([8, 16], F16), "DC": ([128], B16), "DK": ([128], F32), "OO": ([8], U16),
-    "PI": ([1], I32), "PJ": ([12], I32), "PF": ([64], F32), "XR": ([144], F32), "X16": ([128], F32), "VT": ([5, 16], F32), "VU": ([6, 16], F32),
-    "XT0": ([144], F32), "XT1": ([144], F32), "ID": ([8, 16], B16), "IDF": ([128], F32), "IDH": ([128], F16), "ID4": ([4, 128], B16),
-    "MT": ([128], B16), "MF": ([16], F32), "GM": ([8], F32), "GH": ([8], F16), "PM": ([130], B16),
+    "Y0": ([6, 8, 16], B16), "YB": ([6, 8, 16], B16), "YX": ([784], B16), "RB": ([784], B16), "YT": ([2, 384], B16),
+    "HI": ([5, 48], I32), "H16": ([128], B16), "O3": ([96], U16), "G3": ([1536], B16), "NZ": ([384], B16), "NS": ([384], B16), "HT": ([128], B16),
+    "SM": ([6, 64], F32), "SI": ([5, 64], I32), "P": ([64, 4], F32), "M0": ([64, 4], F32), "MQ": ([64, 4], F32),
+    "OH": ([4, 8, 2, 8], B16), "CS": ([512], F32), "OK": ([130, 16], F16), "OI": ([4, 8, 2, 8], F16), "OS": ([16], U16),
+    "GA": ([256], B16), "GB": ([256], B16), "FW0": ([8, 8, 16], B16), "FW1": ([8, 8, 16], B16), "FS": ([4, 8, 2, 3], B16),
+    "XC": ([8, 16], B16), "XK": ([8, 16], F32), "N3a": ([8, 24], F32), "N3b": ([8, 24], F32),
+    "AB": ([8, 128], B16), "SN": ([5, 8], F32), "CP": ([64], B16), "XQ": ([4, 8, 2], F32), "DQ": ([1024], B16), "OQ": ([64], U16),
+    "LWa": ([8, 24], F32), "LWb": ([8, 24], F32), "OP": ([8, 2, 2, 2, 3], F32), "NP": ([16, 12], F32),
+    "XO": ([8, 16], F32), "DC": ([128], B16), "DK": ([128], F32), "OO": ([8], U16),
+    "PI": ([1], I32), "PJ": ([13], I32), "PF": ([96], F32), "XR": ([144], F32), "X16": ([128], F32), "VT": ([7, 18], F32), "VU": ([12, 16], F32),
+    "XT0": ([144], F32), "XT1": ([144], F32), "ID": ([8, 16], B16), "IDF": ([128], F32),
+    "MT": ([128], B16), "MF": ([16], F32), "GM": ([8], F32), "PM": ([130], B16),
     "PW0": ([144], F32), "PW1": ([144], F32), "PT0": ([130], F32), "PT1": ([130], F32),
-    "KO": ([8, 16, 4], B16), "LR": ([8, 4, 16], B16), "WD": ([144], B16), "LU": ([32], B16), "RG": ([64], B16), "RK": ([8, 8], B16),
-    "RQ": ([8], B16), "LB": ([224], B16), "R8": ([8], B16), "LA0": ([128], B16), "LB0": ([128], B16), "SR": ([128], F32),
-    "SW": ([128], B16), "ML": ([2, 96], F32), "MD": ([96], F32), "TT": ([6, 96], B16), "ON": ([128], B16), "OF": ([128], F16),
-    "TB": ([128], B16), "D0": ([512], B16), "D1": ([512], B16), "IC": ([8], F32), "CG": ([2, 8], F32),
+    "KO": ([8, 16, 4], B16), "LR": ([8, 4, 16], B16), "WD": ([144], B16), "LU": ([32], B16), "RG": ([8, 8], B16), "RK": ([8, 8], B16), "RW": ([8, 2], B16),
+    "RQ": ([2, 8], B16), "R8": ([8], B16), "LA0": ([128], B16), "LB0": ([128], B16), "SR": ([128], F32),
+    "SW": ([128], B16), "ML": ([2, 96], F32), "MD": ([3, 96], F32), "TT": ([6, 96], B16), "ON": ([128], B16), "ZR": ([128], F32),
+    "LS": ([4, 128], B16), "TB": ([128], F32), "TC": ([128], F32), "W2": ([1], B16), "D0": ([64], B16),
+    "D1": ([384], B16), "IC": ([8], F32), "CK": ([8], F32), "CO": ([8], F32),
 }
 SCRATCH = {k: ("sbuf", [128] + s, d) for k, (s, d) in SB.items()}
 SCRATCH["D"] = ("dram", [8, 128, 256], B16)
 SCRATCH["DN"] = ("dram", [8, 128, 24], I32)
+SCRATCH["DP"] = ("dram", [8, 128, 24], F32)
 for _b in range(8):
-    SCRATCH["B%d" % _b] = ("psum", [128, 4, 8, 2, 8], F32)
+    SCRATCH["B%d" % _b] = ("psum", [128, 4, 8, 2, 8] if _b < 7 else [128, 8, 64], F32)
 SEMAPHORES = ["v", "s", "t", "p", "rn"] + ["d%d" % i for i in range(48)] + ["rl%d" % i for i in range(5)] + ["rr%d" % i for i in range(5)]
-S1 = ("svsv", "sssv")
-S2 = ("svsv", "ssss")
+CY, PC, HOP, SAME, GA_, SC_ = 0.83e-3, 0.47e-3, 0.17, 0.23, 1.45, 3.0
+TOL = 0.02
+FIX = {"s": 0.03, "vs": 0.015}
+URGE, SHY = {'D': 8, 'r': 4, 'd': 2, 'X': -8, 'dB4': 2, 'tR2': -2, 'tB0': -8, 'HH3': -0.5, 'GB0': 2, 'XB3': -8, 'rB2': -1, 'dB2': 4, 'lm2': -2, 'xB3': -4, 'G': -1, 'R': -2, 'oB4': -4, 'SCN': 2, 'RB2': -2, 'rB3': 0.5, 'tR5': -8}, {'kOI': 9, 'eDQ': 0.5, 'GG2': 0.5, 'eXQ': 9, 'tR1': -0.3, 'LG3': 0.2, 'tR6': 0.2, 'fFW': 0.5, 'gG2': -0.3}
+
+
+def schedule(ops):
+    n = len(ops); succ = [[] for _ in ops]; left = [len(o[3]) for o in ops]
+    for i, o in enumerate(ops):
+        for j, _ in o[3]: succ[j].append(i)
+    rest = [0.0] * n
+    for i in range(n - 1, -1, -1):
+        rest[i] = ops[i][1] + ops[i][2] + max([rest[j] + (HOP if dict(ops[j][3])[i] is not None else -ops[i][2]) for j in succ[i]] + [0.0])
+    for i in range(n): rest[i] += URGE.get(ops[i][7], 0.0) + URGE.get(ops[i][7][0], 0.0)
+    free, done, on, out, base = dict.fromkeys("vstpy", 0.0), [0.0] * n, [""] * n, [], {}
+    ready = [i for i in range(n) if not left[i]]
+    def can(i):
+        base[i] = []
+        for e in ops[i][0]:
+            s = 0.0
+            for j, hard in ops[i][3]:
+                if hard is None: s = max(s, done[j] - ops[j][2] - ops[j][1]); continue
+                if on[j] != e or ops[j][2] > 0: s = max(s, done[j] + HOP)
+                elif hard: s = max(s, done[j] + SAME)
+            base[i].append((s, e, SHY.get(ops[i][7], 0.0) if e == "v" else 0.0))
+    for i in ready: can(i)
+    while ready:
+        c = [min((max(s, free[e]) + d, max(s, free[e]), e, i) for s, e, d in base[i])[1:] for i in ready]
+        e = min(c)[1]; c = [z for z in c if z[1] == e]
+        c.sort(key=lambda z: -rest[z[2]])
+        best = c[0]
+        while True:
+            fit = [z for z in c if z[0] + ops[z[2]][1] <= best[0] + TOL and z is not best and z[0] < best[0]]
+            if not fit: break
+            best = fit[0]
+        s, e, i = best
+        free[e] = s + ops[i][1]; done[i] = free[e] + ops[i][2]; on[i] = e; out.append((i, e)); ready.remove(i)
+        for j in succ[i]:
+            left[j] -= 1
+            if not left[j]: ready.append(j); can(j)
+    return out
 
 
 def rank_program(g, core, T, topo):
@@ -40,106 +82,109 @@ def rank_program(g, core, T, topo):
         return
     QU = {"v": g.vector, "s": g.scalar, "t": g.tensor, "p": g, "y": g.sync}
     V, S, PE = g.vector, g.scalar, g.tensor
-    cnt = {"v": 0, "s": 0, "t": 0, "p": 0}
-    seen, lastw, reads, total = {}, {}, {}, {}
+    ops, lastw, reads, bank, part = [], {}, {}, {}, ["c"]
+
+    def op(es, R, W, fn, cost, lat=0.0, sig=None):
+        R, W = R.split(), W.split(); pre = {}; after = []
+        for k in R + W:
+            if k[0] == "B" and k[:2] in bank: pre.setdefault((bank[k[:2]], ""), False)
+        for k in W:
+            for j in lastw.get(k, []) + reads.get(k, []): pre[j] = pre.get(j, False) or es != "t"
+        for k in R:
+            if k[0] == "#": after += lastw.get(k, [])
+            else:
+                for j in lastw.get(k.strip("!"), []): pre[j] = pre.get(j, False) or es != "t" or k[0] == "!"
+        i = len(ops)
+        for k in W: lastw[k] = [(i, k if sig and k in sig else "")]; reads[k] = []
+        for k in R: reads.setdefault(k, []).append((i, ""))
+        for k in R + W:
+            if k[0] == "B": bank[k[:2]] = i
+        hard = {}
+        for (j, _), h in pre.items(): hard[j] = hard.get(j, False) or h
+        for j, _ in after: hard.setdefault(j, None)
+        ops.append([es, cost + FIX.get(es, 0.0), lat, sorted(hard.items()), fn, pre, sig, part[0] + W[0][:2]])
+
     nd = [0]
-
-    def need(e, tok):
-        if seen.get((e, tok[0]), 0) < tok[1]:
-            QU[e].wait_ge(T.sem[tok[0]], tok[1]); seen[(e, tok[0])] = tok[1]
-
-    def deps(e, R, W):
-        toks = []
-        for k in R:
-            toks += [tok for tok in lastw.get(k, []) if not (e == "t" and tok[2] == "t")]
-            if k[0] == "B":
-                toks += [tok for tok in reads.get(k, {}).values() if tok[2] != e]
-        for k in W:
-            toks += [tok for tok in lastw.get(k, []) + list(reads.get(k, {}).values()) if tok[2] != e]
-        for tok in sorted(toks, reverse=True): need(e, tok)
-
-    def mark(tok, R, W):
-        for k in W:
-            lastw[k] = [tok]; reads[k] = {}
-        for k in R:
-            reads.setdefault(k, {})[tok[0]] = tok
-
-    def op(e, R, W, fn):
-        R, W = R.split(), W.split()
-        deps(e, R, W)
-        fn().then_inc(T.sem[e], 1); cnt[e] += 1; total[e] = cnt[e]
-        mark((e, cnt[e], e), R, W)
-
-    def dma(e, R, W, out, in_):
-        R, W = R.split(), W.split()
-        deps(e, R, W)
+    def dma(e, R, W, out, in_, lat=1.1):
         s = "d%d" % nd[0]; nd[0] += 1
-        QU[e].dma_start(out, in_).then_inc(T.sem[s], 16); total[s] = 16
-        mark((s, 16, "dma"), R, W)
+        op(e, R, W, lambda q: QU[q].dma_start(out, in_).then_inc(T.sem[s], 16), 0.06, lat, {"": (s, 16)})
 
     others = [r for r in range(8) if r != me]
     far = [r for r in others if topo.die(T.cores[r]) != topo.die(core)]
     near = [r for r in others if r not in far]
 
-    def exchange(k, R, W, src, dst, split=False):
-        deps("p", R.split(), [])
+    def exchange(k, R, W, src, dst, split=False, cost=0.9, lat=2.8):
         tr = []
         for r in others:
             c = T.cores[r]; en = topo.engines(core, c); rid, pid, _ = topo.addr(c)
             en = en[0::2][2 * far.index(r):] if r in far else en[1::2][2 * near.index(r):]
             tr.append(RemoteDMATransfer(dst_ids=[DstId(rid=rid, pnc=pid)], dma_engine_mask=(1 << en[0]) | (1 << en[1]),
                                         remote_sem=T.sem["rn" if split and r in near else "rr%d" % k], src=src(r), dst=dst))
-        g.remote_dma_fused(tr, local_sem=T.sem["rl%d" % k])
-        total["rl%d" % k] = total["rr%d" % k] = 14
-        mark(("rl%d" % k, 14, "dma"), R.split(), [])
-        if split:
-            total["rn"], total["rr%d" % k] = 2 * len(near), 2 * len(far); lastw[W + "n"] = [("rn", total["rn"], "dma")]
-        lastw[W] = [("rr%d" % k, total["rr%d" % k], "dma")]
+        sig = {"": ("rl%d" % k, 14), W: ("rr%d" % k, 2 * len(far) if split else 14)}
+        if split: sig[W + "n"] = ("rn", 2 * len(near))
+        op("p", R + " #%d" % min(k - 1, 2), " ".join(sig) + " #%d" % k, lambda q: g.remote_dma_fused(tr, local_sem=T.sem["rl%d" % k]), cost, lat, sig)
 
+    def size(a):
+        n = 1
+        for d in a.shape[1:]: n *= d
+        return n
+    def cyc(*a): return CY * max(64, size(a[0]) * (0.5 if all("16" in str(z.dtype) for z in a) else 1))
     def ks(f, n): return " ".join(f % j for j in (range(n) if isinstance(n, int) else n))
-    def mm(R, W, out, l, r, st=True, sp=True): op("t", R, W, lambda: PE.matmul(out, l, r, st, sp))
-    def cp(R, W, o, i): op("v", R, W, lambda: V.tensor_copy(o, i))
-    def tt(R, W, o, a, b, f): op("v", R, W, lambda: V.tensor_tensor(o, a, b, f))
+    def mm(R, W, out, l, r, st=True, sp=True):
+        op("t", R, W, lambda q: PE.matmul(out, l, r, st, sp), PC * max(min(64, size(l)), size(r)) * (4 if "32" in str(l.dtype) else 1))
+    def cp(R, W, o, i): op("v", R, W, lambda q: V.tensor_copy(o, i), cyc(o, i))
+    def tt(R, W, o, a, b, f): op("v", R, W, lambda q: V.tensor_tensor(o, a, b, f), CY * max(64, size(o) * (1 if "B" in [k[0] for k in R.split()] else 2)))
     def ts(R, W, o, a, s1, f0, s2=None, f1=None):
-        op("v", R, W, (lambda: V.tensor_scalar(o, a, s1, None, f0)) if f1 is None else (lambda: V.tensor_scalar(o, a, s1, s2, f0, f1)))
-    def ms(W, o, c, R=""): op("v", R, W, lambda: V.memset(o, c))
-    def act(R, W, o, i, f=AF.Identity, **k): op("s", R, W, lambda: S.activation(o, i, f, **k))
-    def red(R, W, o, i, f): op("v", R, W, lambda: V.tensor_reduce(o, i, AxisListType.X, f))
-    def scan(R, W, o, a, b, f0, f1): op("v", R, W, lambda: V.tensor_tensor_scan(o, a, b, 0.0, f0, f1))
-    def iota(W, o, pat, base, cm=0): op("p", "", W, lambda: g.iota(o, pat, base, cm, allow_small_or_imprecise_dtypes=True))
-    def gather(e, R, W, o, win, off):
-        if e == "v": cp(R, W, o, win.indirect(off))
-        else: act(R, W, o, win.indirect(off))
+        op("v", R, W, (lambda q: V.tensor_scalar(o, a, s1, None, f0)) if f1 is None else (lambda q: V.tensor_scalar(o, a, s1, s2, f0, f1)), cyc(o, a))
+    def ms(W, o, c, R=""): op("v", R, W, lambda q: V.memset(o, c), cyc(o))
+    def act(R, W, o, i, f=AF.Identity, **k): op("s", R, W, lambda q: S.activation(o, i, f, **k), CY * max(64, size(o)))
+    def red(R, W, o, i, f): op("v", R, W, lambda q: V.tensor_reduce(o, i, AxisListType.X, f), CY * 64)
+    def scan(R, W, o, a, b, f0, f1): op("v", R, W, lambda q: V.tensor_tensor_scan(o, a, b, 0.0, f0, f1), cyc(o, a, b))
+    def iota(W, o, pat, base, cm=0): op("p", "", W, lambda q: g.iota(o, pat, base, cm, allow_small_or_imprecise_dtypes=True), 0.13 + 2 * CY * size(o))
+    def move(R, W, o, i, es="vs", cost=None):
+        op(es, R, W, lambda q: V.tensor_copy(o, i) if q == "v" else S.activation(o, i, AF.Identity), cost or CY * max(64, size(o)))
+    def scale(R, W, o, i, c, es="vs"):
+        op(es, R, W, lambda q: V.tensor_scalar(o, i, c, None, A.mult) if q == "v" else S.activation(o, i, AF.Identity, scale=c), CY * max(64, size(o)))
+    def relu(R, W, o, i, c):
+        op("vs", R, W, lambda q: V.tensor_scalar(o, i, c, 0.0, A.add, A.max) if q == "v" else S.activation(o, i, AF.Relu, bias=c), CY * max(64, size(o)))
+    def gather(R, W, o, win, off): move(R, W, o, win.indirect(off), "vs", 0.03 + CY * GA_ * size(o))
+    def scatter(R, W, win, off, i): op("v", R, W, lambda q: V.tensor_copy(win.indirect(off), i), 0.05 + CY * SC_ * size(i))
     B = [T["B%d" % b] for b in range(8)]
+    half = lambda b, u: B[b][:, 2 * u:2 * u + 2] if b < 7 else B[b][:, 4 * u:4 * u + 4]
     SHR, AND, EQ = A.arith_shift_right, A.bitwise_and, A.is_equal
 
+    dma("y", "", "DN", T.DN[:], T.nodes[:])
     dma("y", "", "KI", T.KI[:], T.kids[:])
     dma("s", "", "CN", T.CN[:, 0:1024], T.cells[:])
-    dma("y", "", "DN", T.DN[:], T.nodes[:])
     dma("y", "", "WI", T.WI[:], T.wt[:])
     dma("s", "CN", "Dc", T.D[:, 0:64, :], T.CN[:, 0:1024])
-    op("p", "", "PI", lambda: g.iota(T.PI[:], [[0, 1]], 0, 1))
+    op("p", "", "PI", lambda q: g.iota(T.PI[:], [[0, 1]], 0, 1), 0.13)
     iota("XR", T.XR[:], [[1, 144]], 0)
     iota("X16", T.X16[:], [[0, 8], [1, 16]], 0)
     iota("VT1a", T.VT[:, 1, 0:12], [[8, 3], [1, 4]], 9)
     iota("VT1b", T.VT[:, 1, 12:16], [[8, 2], [1, 2]], 18)
-    iota("VT2", T.VT[:, 2, :], [[8, 4], [1, 4]], 18)
+    iota("VT2", T.VT[:, 2, 0:16], [[8, 4], [1, 4]], 18)
     iota("VT3a", T.VT[:, 3, 0:8], [[0, 2], [1, 4]], 4)
-    iota("VT3b", T.VT[:, 3, 8:16], [[1, 4], [0, 2]], 0)
-    exchange(0, "DN", "LN", lambda r: T.DN[r], T.LN[:, me, :])
+    iota("VT3b", T.VT[:, 3, 8:17], [[1, 3], [0, 3]], 0)
+    iota("VT5", T.VT[:, 5, :], [[1, 3], [0, 6]], 0)
     iota("ML0", T.ML[:, 0, :], [[32, 6], [1, 16]], 0)
     iota("ML1", T.ML[:, 1, :], [[16, 2], [64, 3], [1, 16]], 0)
+    iota("IC", T.IC[:], [[96, 8]], 16, 1)
+    iota("CK", T.CK[:], [[-1023, 8]], 7168, 8)
+    iota("CQ", T.CP[:], [[0, 4], [1, 8], [0, 2]], 0)
+    iota("CO", T.CO[:], [[1023, 8]], -1024)
+    exchange(0, "DN", "LN", lambda r: T.DN[r], T.LN[:, me, :], cost=2.0)
     dma("y", "DN", "LNo", T.LN[:, me, :], T.DN[me])
 
-    names = ["p", "b0", "pm", "pg", "hf", "t", "i4", "t2", "p8", "m1", "k11", "b3"]
-    rule = [(0, 127), (0, 1), (0, 15), (4, 7), (4, 1), (5, 3), (2, 3), (1, 3), (3, 15), (1, 7), (0, 11), (0, 3)]
+    names = ["p", "b0", "pm", "pg", "hf", "t", "i4", "t2", "p8", "m1", "k11", "b3", "o7"]
+    rule = [(0, 127), (0, 1), (0, 15), (4, 7), (4, 1), (5, 3), (2, 3), (1, 3), (3, 15), (1, 7), (0, 11), (0, 3), (0, 7)]
     col = {}
     def C(n):
         if n not in col: col[n] = len(col)
         return T.PF[:, col[n]:col[n] + 1]
     for j, (sh, an) in enumerate(rule):
         ts("PI", "PJ%d" % j, T.PJ[:, j:j + 1], T.PI[:], sh, SHR, an, AND); C(names[j])
-    cp(ks("PJ%d", 12), ks("c%s", names), T.PF[:, 0:12], T.PJ[:])
+    cp(ks("PJ%d", 13), ks("c%s", names), T.PF[:, 0:13], T.PJ[:])
     def lin(n, a, x, y, f0=A.mult, f1=A.add):
         ts(ks("c%s", [z for z in (a, x, y) if isinstance(z, str)]), "c" + n, C(n), C(a), C(x) if isinstance(x, str) else x, f0, C(y) if isinstance(y, str) else y, f1)
     def pick(W, o, rk, n, c, w="one"):
@@ -149,41 +194,37 @@ def rank_program(g, core, T, topo):
         k = "XT%d" % xt[0]; xt[0] ^= 1
         act(rk + " c" + c, k, T[k][:, 0:n], T[rk][:, 0:n], AF.Abs, scale=-1.0, bias=C(c))
         act(k + " c" + w, W, o, T[k][:, 0:n], AF.Relu, scale=-65536.0, bias=C(w))
-    ms("cone", C("one"), 1.0); ms("cb1", C("b1"), -(1.0 + 2.0 ** -11))
+    for n, c in (("one", 1.0), ("b1", -(1.0 + 2.0 ** -11)), ("b128", -128.0), ("b2", -2.0 ** -13), ("b15", 15.0)): ms("c" + n, C(n), c)
     lin("w16", "b0", 15.0, 1.0); lin("cpm", "p", 1.0, "b0", A.add, A.subtract)
     pick("PM", T.PM[:], "XR", 130, "cpm", "w16")
     pick("ID", T.ID[:], "XR", 128, "p")
 
     ts("KI", "KHa", T.KH[:, 0:256], T.KI[:], 8160, AND)
+    cp("KHa", "HLa", T.HL[:, 0:256], T.KH[:, 0:256])
     ts("KI", "KHb", T.KH[:, 256:512], T.KI[:], 31, AND)
-    cp("KHa", "HLa", T.HL[:, 0:256], T.KH[:, 0:256]); cp("KHb", "HLb", T.HL[:, 256:512], T.KH[:, 256:512])
+    cp("KHb", "HLb", T.HL[:, 256:512], T.KH[:, 256:512])
     dma("y", "HLa", "Dh", T.D[:, 64:80, :], T.HL[:, 0:256])
     dma("y", "HLb", "Dl", T.D[:, 80:96, :], T.HL[:, 256:512])
     mm("PM CN", "B0", B[0][:], T.PM[:, 1:129], T.CN[:, 0:512], True, False)
     mm("PM CN", "B0", B[0][:], T.PM[:, 0:128], T.CN[:, 512:1024], False, True)
     act("B0", "PB", T.PB[:], B[0][:])
     dma("s", "PB", "Dp", T.D[:, 96:128, :], T.PB[:])
-    exchange(1, "Dc Dh Dl Dp", "L", lambda r: T.D[r], T.L[:, 256 * me:256 * me + 256], True)
+    exchange(1, "Dc Dh Dl Dp", "L", lambda r: T.D[r], T.L[:, 256 * me:256 * me + 256], True, lat=3.6)
     dma("y", "Dc Dh Dl Dp", "Lo", T.L[:, 256 * me:256 * me + 256], T.D[me])
-    iota("FWz", T.FW[:], [[0, 1024]], 0)
-    iota("D1", T.D1[:], [[0, 128], [-1, 4]], 1)
-    iota("D0", T.D0[:], [[0, 64], [4096, 8]], 0)
-    iota("ON", T.ON[:], [[0, 128]], 1)
-    iota("IC", T.IC[:], [[96, 8]], 16, 1)
-    iota("CG0", T.CG[:, 0, :], [[-896, 8]], 8193, 1)
-    iota("CG1", T.CG[:, 1, :], [[128, 8]], 8192, 1)
 
-    ms("LR", T.LR[:], 0.0)
+    ms("LR", T.LR[:], 0.0); ms("OKz", T.OK[:, 0::2, :], 0.0); ms("ON", T.ON[:], 1.0); ms("KOz", T.KO[:], 0.0)
+    ms("FWz0", T.FW0[:, :, :, 11:16], 0.0); ms("FWz1", T.FW1[:, :, :, 11:16], 0.0)
+    ms("D0z", T.D0[:], 0.0); ms("D0", T.D0[:, 0::8], 4096.0, "D0z"); ms("D1z", T.D1[:], 1.0); ms("D1", T.D1[:, 0::3], 0.0, "D1z")
     for t in range(4):
         t1, t0 = t >> 1, t & 1
         b = 4 * (5 - 4 * t1 - t0); vr, vc = 2 - 2 * t1, 2 - 2 * t0
-        act("ID LR", "LRa%d" % t, T.LR[:, 2 * t, 0:3, 0:12], T.ID[:, b // 16:b // 16 + 3, b % 16:b % 16 + 12])
-        act("ID LR", "LRb%d" % t, T.LR[:, 2 * t, 3, :], T.ID[:, vr:vr + 2, 4 * vc:4 * vc + 8])
-        act("ID LR", "LRc%d" % t, T.LR[:, 2 * t, 0:2, 12:16], T.ID[:, 4:6, 4 * (3 - t):4 * (3 - t) + 4])
-    act(ks("LRa%d", 4) + " " + ks("LRb%d", 4) + " " + ks("LRc%d", 4), "LRz", T.LR[:, 1::2], T.LR[:, 0::2])
+        move("ID LR", "LRa%d" % t, T.LR[:, 2 * t, 0:3, 0:12], T.ID[:, b // 16:b // 16 + 3, b % 16:b % 16 + 12])
+        move("ID LR", "LRb%d" % t, T.LR[:, 2 * t, 3, :], T.ID[:, vr:vr + 2, 4 * vc:4 * vc + 8])
+        move("ID LR", "LRc%d" % t, T.LR[:, 2 * t, 0:2, 12:16], T.ID[:, 4:6, 4 * (3 - t):4 * (3 - t) + 4])
+    move(ks("LRa%d", 4) + " " + ks("LRb%d", 4) + " " + ks("LRc%d", 4), "LRz", T.LR[:, 1::2], T.LR[:, 0::2])
     pick("MF", T.MF[:], "X16", 16, "pm")
     def table(n, row, R):
-        tt(R + " MF", "VU%d" % row, T.VU[:, row, :], T.VT[:, row, :], T.MF[:], A.mult)
+        tt(R + " MF", "VU%d" % row, T.VU[:, row, :], T.VT[:, row, 0:16], T.MF[:], A.mult)
         red("VU%d" % row, "c" + n, C(n), T.VU[:, row, :], A.add)
     ms("VT0", T.VT[:, 0, :], 0.0)
     for a in range(3): ms("VT0%d" % a, T.VT[:, 0, 4 * a:4 * a + 3], 1.0, "VT0")
@@ -192,323 +233,311 @@ def rank_program(g, core, T, topo):
     spick("PW0", T.PW0[:], "XR", 144, "cpw", "nb0"); spick("PW1", T.PW1[:], "XR", 144, "cpw", "b0")
     lin("km", "k11", 3.0, 1.0, EQ, A.mult); lin("cwd", "pg", 16.0, 15.0); lin("crq", "hf", 4.0, "t")
     spick("WD", T.WD[:], "XR", 144, "cwd", "km")
-    pick("RQ", T.RQ[:], "XR", 8, "crq", "km")
+    lin("kh", "pm", 3.0, 1.0, EQ, A.mult)
+    for u in range(2):
+        ts("XR ccrq ckm", "RQa%d" % u, T.RQ[:, u, 0:4], T.XR[:, 4 * u:4 * u + 4], C("crq"), EQ, C("km"), A.mult)
+        ts("XR ccrq ckh", "RQb%d" % u, T.RQ[:, u, 4:8], T.XR[:, 4 * u:4 * u + 4], C("crq"), EQ, C("kh"), A.mult)
     table("pos0", 1, "VT1a VT1b")
-    for t in range(4): ms("tau%d" % t, T.PF[32 * t:32 * t + 32, 63:64], float(8 * (t >> 1) + (t & 1)))
-    ts("chm " + ks("tau%d", 4), "cx2", C("x2"), C("hm"), 2.0, A.add, T.PF[:, 63:64], A.mult)
+    lin("tl", "t", 2.0, 6.0, A.is_ge, A.mult); lin("tau", "t", 1.0, "tl")
+    lin("x2", "hm", 2.0, "tau", A.add, A.mult)
     lin("hw", "hm", 2.0 ** -14, 0.0); lin("vw", "pm", 12.0, 1.0, A.is_ge, A.mult); lin("nhf", "hf", -1.0, 1.0); lin("pos", "x2", 1.0, "pos0")
     U = lambda i: T.VU[:, i, :]
-    ts("VT2 cpos", "VU2", U(2), T.VT[:, 2, :], C("pos"), A.subtract)
-    lin("mine", "pg", float(me), 1.0, EQ, A.mult)
+    ts("VT2 cpos", "VU2", U(2), T.VT[:, 2, 0:16], C("pos"), A.subtract)
     tt("VU2", "VU2", U(2), U(2), U(2), A.mult)
+    ts("VU2 chw", "VU7", U(7), U(2), 1.0, EQ, C("hw"), A.mult)
+    ts("VU2", "VU8", U(8), U(2), 49.0, A.is_ge)
+    ts("VU2 chw", "VU9", U(9), U(2), 81.0, A.is_le, C("hw"), A.mult)
+    ts("VU2 cvw", "VU10", U(10), U(2), 0.0, EQ, C("vw"), A.mult)
+    tt("VU8 VU9", "VU8", U(8), U(8), U(9), A.mult)
+    tt("VU7 VU10", "VU7", U(7), U(7), U(10), A.add)
+    tt("VU7 VU8", "VU7", U(7), U(7), U(8), A.add)
+    ts("VU7 cnhf", "LUa", T.LU[:, 0:16], U(7), C("nhf"), A.mult)
+    ts("VU7 chf", "LUb", T.LU[:, 16:32], U(7), C("hf"), A.mult)
+    lin("mine", "pg", float(me), 1.0, EQ, A.mult)
     spick("SW", T.SW[:], "X16", 128, "pm", "mine")
     pick("GM", T.GM[:], "XR", 8, "pg")
-    ts("VU2 chw", "VU0", U(0), U(2), 1.0, EQ, C("hw"), A.mult)
-    ts("VU2", "VU1", U(1), U(2), 49.0, A.is_ge)
-    ts("VU2 chw", "VU4", U(4), U(2), 81.0, A.is_le, C("hw"), A.mult)
-    ts("VU2 cvw", "VU5", U(5), U(2), 0.0, EQ, C("vw"), A.mult)
     ts("WI", "WHa", T.WH[:, 0:1], T.WI[:], 8160, AND); ts("WI", "WHb", T.WH[:, 1:2], T.WI[:], 31, AND)
-    tt("VU1 VU4", "VU1", U(1), U(1), U(4), A.mult)
-    tt("VU0 VU5", "VU0", U(0), U(0), U(5), A.add)
     cp("WHa WHb", "WB", T.WB[:], T.WH[:])
     mm("SW WB", "B0", B[0][:, 0, 0, 0, 0:2], T.SW[:], T.WB[:])
-    ms("VT4", T.VT[:, 4, :], 1.0)
-    tt("VU0 VU1", "VU0", U(0), U(0), U(1), A.add)
-    for j in range(1, 4): ms("VT4%d" % j, T.VT[:, 4, j::4], 16.0 ** j, "VT4")
-    ts("VU0 cnhf", "LUa", T.LU[:, 0:16], U(0), C("nhf"), A.mult)
-    ts("VU0 chf", "LUb", T.LU[:, 16:32], U(0), C("hf"), A.mult)
-    lin("crk", "pg", 8.0, "i4")
-    table("wk", 4, "VT41 VT42 VT43")
     cp("B0", "WC", T.WC[:], B[0][:, 0, 0, 0, 0:2])
+    for j in range(6): ms("VT4%d" % j, T.VT[:, 4, j::6], -16.0 ** j)
+    table("wk", 4, ks("VT4%d", 6)); table("i6", 5, "VT5")
+    lin("crk", "pg", 8.0, "i6")
     pick("RKz", T.RK[:], "XR", 64, "crk", "wk")
-    lin("ge8", "pm", 8.0, 1.0, A.is_ge, A.mult); lin("x4", "hf", 16.0, "t")
-    ts("GM WC RKz", "RKa", T.RK[:, :, 4], T.GM[:], T.WC[:, 0:1], A.mult)
-    ts("GM WC RKz", "RKb", T.RK[:, :, 5], T.GM[:], T.WC[:, 1:2], A.mult)
+    lin("ge8", "pm", 8.0, 1.0, A.is_ge, A.mult)
+    ts("GM WC", "RKa", T.RW[:, :, 0], T.GM[:], T.WC[:, 0:1], A.mult)
+    ts("GM WC", "RKb", T.RW[:, :, 1], T.GM[:], T.WC[:, 1:2], A.mult)
+    ms("VT6", T.VT[:, 6, :], 1.0)
+    for j in (1, 2): ms("VT6%d" % j, T.VT[:, 6, 8 + j::3], 256.0 ** j, "VT6")
+    table("fs", 3, "VT3a VT3b"); table("wg", 6, "VT61 VT62")
+    lin("crg", "pg", 8.0, "fs"); lin("is8", "pm", 8.0, 1.0, EQ, A.mult)
+    pick("RGz", T.RG[:], "XR", 64, "crg", "wg")
+    ts("GM cis8 RGz", "RG", T.RG[:, :, 3], T.GM[:], C("is8"), A.mult)
+    pick("IDF", T.IDF[:], "XR", 128, "p")
+    ts("IDF", "MD2", T.MD[:, 2, :], T.IDF[:, 0:96], -1024.0, A.mult)
+    for k in range(2):
+        tt("ML%d IDF" % k, "MD0", T.MD[:, 0, :], T.ML[:, k, :], T.IDF[:, 0:96], A.mult)
+        red("MD0", "cml%d" % k, C("ml%d" % k), T.MD[:, 0, :], A.add)
+        for j in (0, 2):
+            ts("ML%d cml%d" % (k, k), "TT%d%d" % (k, j), T.TT[:, 3 * k + j, :], T.ML[:, k, :], C("ml%d" % k), A.subtract, float(16 * (k + 1) * (j - 1)), A.is_ge)
+        ts("ML%d cml%d" % (k, k), "MD1", T.MD[:, 1, :], T.ML[:, k, :], C("ml%d" % k), A.is_gt)
+        tt("MD1 MD2", "TT%d1" % k, T.TT[:, 3 * k + 1, :], T.MD[:, 1, :], T.MD[:, 2, :], A.add)
+    ms("N3az", T.N3a[:, :, 20:24], 0.0); ms("N3bz", T.N3b[:, :, 20:24], 0.0); lin("jq", "p", 8.0, 8192.0); ms("ZR", T.ZR[:], 0.0); ms("YXz", T.YX[:, 0:16], 0.0); ms("XKz", T.XK[:], 0.0)
+    lin("k8", "is8", 1024.0, 0.0)
+    ts("MF ck8", "RBz", T.RB[:, 0:16], T.MF[:], 0.0, A.mult, C("k8"), A.add)
+    lin("x5", "ge8", -1.0, 1.0); lin("w8", "pm", 11.0, 1.0, A.is_lt, A.mult); lin("cla", "m1", 1.0, 8.0); lin("x7", "pm", 8.0, 1.0)
+    lin("x6", "x5", "b3", 0.0); lin("j1", "p", 1.0, 2049.0); lin("cpt", "t", 2.0, "x7"); lin("cr8", "ge8", 4.0, "x6"); lin("ws", "ge8", "w8", 0.0)
+    ms("TBa", T.TB[:], 0.5); ms("TBb", T.TB[:, 0:1], 2.0 ** 63, "TBa")
+    op("v", "TBb ZR", "TC", lambda q: V.tensor_tensor_scan(T.TC[:], T.TB[:], T.ZR[:], 1.0, A.mult, A.add), CY * 128)
+    tt("TC IDF", "TC", T.TC[:], T.TC[:], T.IDF[:], A.mult); red("TC", "cw2", C("w2"), T.TC[:], A.add)
+    cp("cw2", "W2", T.W2[:], C("w2")); lin("w3", "w2", 2.5, 0.0)
+    ts("CQ", "CP", T.CP[:], T.CP[:], 2.0 ** -7, A.mult)
+    pick("R8", T.R8[:], "XR", 8, "cr8", "w8")
+    for q in range(4):
+        lin("lq%d" % q, "t", float(q), "ws", EQ, A.mult)
+        scale("ON clq%d" % q, "LS%d" % q, T.LS[:, q, :], T.ON[:], C("lq%d" % q))
+    spick("MT", T.MT[:], "X16", 128, "pm")
+    move("MT", "SR", T.SR[:], T.MT[:])
+    spick("LA0", T.LA0[:], "X16", 128, "cla", "w16"); spick("LB0", T.LB0[:], "X16", 128, "pm", "x5")
+    spick("PT0", T.PT0[:], "XR", 130, "cpt", "nhf"); spick("PT1", T.PT1[:], "XR", 130, "cpt", "hf")
+    move("ID KOz", "KO", T.KO[:, :, 8:12, :], T.ID[:])
+    for blk in range(4):
+        b = 6 + blk // 2; o = half(b, blk % 2)
+        mm("KO HLa", "B%d" % b, o, T.KO[:, :, :, blk], T.HL[:, 0:256], True, False)
+        mm("KO HLb", "B%d" % b, o, T.KO[:, :, :, blk], T.HL[:, 256:512], False, True)
+    move("B6", "YK0", T.YK[:, 0:512], B[6][:]); move("B7", "YK1", T.YK[:, 512:1024], B[7][:])
     cp("LN LNo", "LF", T.LF[:], T.LN[:])
     for h2 in range(2):
         pw = T["PW%d" % h2]
-        mm("LF PW%d" % h2, "B1", B[1][:, :, 2 * h2::4, :, 0:6], pw[:, 16:144], T.LF[:, :, 0::2], True, False)
-        mm("LF PW%d" % h2, "B1", B[1][:, :, 2 * h2::4, :, 0:6], pw[:, 0:128], T.LF[:, :, 1::2], False, True)
-    table("fs", 3, "VT3a VT3b")
-    lin("x3", "ge8", "b0", 255.0, A.mult, A.mult); lin("clb", "pm", 93.0, "x4", A.add, A.add); lin("crg", "pg", 8.0, "fs"); lin("wg", "x3", 1.0, 1.0)
-    spick("LBa", T.LB[:, 0:144], "XR", 144, "clb", "km")
-    ms("LBb", T.LB[:, 144:224], 0.0)
-    pick("RG", T.RG[:], "XR", 64, "crg", "wg")
-    cp("B1", "O1a", T.O1a[:], B[1][:, :, 0::2, :, 0:6])
+        mm("LF PW%d" % h2, "B5", B[5][:, :, 2 * h2::4, :, 0:6], pw[:, 16:144], T.LF[:, :, 0::2], True, False)
+        mm("LF PW%d" % h2, "B5", B[5][:, :, 2 * h2::4, :, 0:6], pw[:, 0:128], T.LF[:, :, 1::2], False, True)
+    cp("B5", "O1a", T.O1a[:], B[5][:, :, 0::2, :, 0:6])
 
-    def order(k):
-        tt("ML%d IDF" % k, "MD", T.MD[:], T.ML[:, k, :], T.IDF[:, 0:96], A.mult)
-        red("MD", "cml%d" % k, C("ml%d" % k), T.MD[:], A.add)
-        for j in range(3):
-            ts("ML%d cml%d" % (k, k), "TT%d%d" % (k, j), T.TT[:, 3 * k + j, :], T.ML[:, k, :], C("ml%d" % k), A.subtract, float(16 * (k + 1) * (j - 1)), A.is_ge)
-
-    def claim_constants_v():
-        lin("x5", "ge8", -1.0, 1.0); lin("w8", "pm", 10.0, 1.0, A.is_lt, A.mult); lin("cla", "m1", 1.0, 8.0); lin("x7", "pm", 8.0, 1.0)
-        lin("x6", "x5", "b3", 0.0); lin("j1", "p", 1.0, 1025.0); lin("j0", "p", 1.0, 1024.0); lin("cpt", "t", 2.0, "x7"); lin("cr8", "ge8", 4.0, "x6")
-        ts("XR cp", "TB", T.TB[:], T.XR[:, 0:128], C("p"), A.is_le, 4096.0, A.mult)
-        cp("GM", "GH", T.GH[:], T.GM[:]); ms("OF", T.OF[:], 1.0); pick("IDH", T.IDH[:], "XR", 128, "p")
-        pick("R8", T.R8[:], "XR", 8, "cr8", "w8")
-
-    def claim_constants_s():
-        spick("MT", T.MT[:], "X16", 128, "pm")
-        spick("LA0", T.LA0[:], "X16", 128, "cla", "w16"); spick("LB0", T.LB0[:], "X16", 128, "pm", "x5")
-        spick("SR", T.SR[:], "X16", 128, "pm")
-        spick("PT0", T.PT0[:], "XR", 130, "cpt", "nhf"); spick("PT1", T.PT1[:], "XR", 130, "cpt", "hf")
-        for j in range(4): act("ID", "ID4%d" % j, T.ID4[:, j, :], T.ID[:])
-
-    def own_kids():
-        for blk in range(4):
-            b = 7 * (blk // 2); o = B[b][:, 2 * (blk % 2):2 * (blk % 2) + 2]
-            mm("KO HLa", "B%d" % b, o, T.KO[:, :, :, blk], T.HL[:, 0:256], True, False)
-            mm("KO HLb", "B%d" % b, o, T.KO[:, :, :, blk], T.HL[:, 256:512], False, True)
-        act("B0", "YK0", T.YK[:, 0:512], B[0][:]); act("B7", "YK1", T.YK[:, 512:1024], B[7][:])
-
+    part[0] = "t"
     came = lambda r: "Lo" if r == me else "Ln" if r in near else "L"
     for r in [me] + near + far:
         dma("y", came(r), "UP%d" % r, T.UP[64 * (r // 4) + r % 4:64 * (r // 4) + 64:4, :], T.L[64:128, 256 * r:256 * r + 256])
-    for h in (me // 4, 1 - me // 4):
+    for n, h in enumerate((me // 4, 1 - me // 4)):
         for gg in range(8):
-            dma("y", ks("UP%d", range(4 * h, 4 * h + 4)), "Q%d" % (8 * h + gg), T.Q[16 * gg:16 * gg + 16, 4096 * h:4096 * h + 4096], T.UP[64 * h:64 * h + 64, :])
+            dma("y", ks("UP%d", range(4 * h, 4 * h + 4)), "Q%d" % (8 * h + gg), T.Q[16 * gg:16 * gg + 16, 4096 * h:4096 * h + 4096], T.UP[64 * h:64 * h + 64, :],
+                1.2 + 0.15 * (8 * n + gg))
     QK, RS, OHK = ks("Q%d", 16), ks("R%d_", 16), ks("OH%d", 8)
     for n, i in enumerate(2 * r + j for r in [me] + near + far for j in range(2)):
         r, j, b = i // 2, i % 2, n % 8
         for u in range(2):
-            mm(came(r) + " LRz", "B%d" % b, B[b][:, 2 * u:2 * u + 2], T.LR[0:96, :, :, 2 * j + u::4], T.L[0:96, 256 * r:256 * r + 256])
-        o = T.R[:, 512 * i:512 * i + 512]
-        if i % 2: act("B%d cbias" % b, "R%d_" % i, o, B[b][:], AF.Relu, bias=C("bias"))
-        else: ts("B%d cbias" % b, "R%d_" % i, o, B[b][:], C("bias"), A.add, 0.0, A.max)
-        if n == 1:
-            pick("IDF", T.IDF[:], "XR", 128, "p"); order(0); ms("OKz", T.OK[:, 0::2, :], 0.0)
-            for y in ("YXa", "YXb", "RB"): ms(y + "z", T[y][:, 0:16], 0.0)
+            mm(came(r) + " LRz", "B%d" % b, half(b, u), T.LR[0:96, :, :, 2 * j + u::4], T.L[0:96, 256 * r:256 * r + 256])
+        relu("B%d cbias" % b, "R%d_" % i, T.R[:, 512 * i:512 * i + 512], B[b][:], C("bias"))
     sm = lambda i: T.SM[0:96, i, :]
-    sn = lambda i: T.SN[:, i, :]
-    hit0, hit1 = T.EA[0:96, 3:256:4], T.EA[0:96, 259::4]
+    pf = lambda f: B[4][0:96, :, :, :, f]
+    hit0, hit1 = T.HT[0:96, 0:64], T.HT[0:96, 64:128]
 
-    def step1(k, qs):
-        O1, G1 = T["O1" + "ab"[k]], T["G1" + "ab"[k]]
-        for q in qs:
-            gather(S1[k][q], RS + " O1" + "ab"[k], "G1%d%d" % (k, q), G1[:, 768 * q:768 * q + 768], T.R[:], O1[:, 48 * q:48 * q + 48])
-
-    def turn(k, c, copy=True):
-        G1 = T["G1" + "ab"[k]]; b = (0, 7)[c]
-        for pp in range(16):
-            mm("WD G1%d%d G1%d%d" % (k, 2 * c, k, 2 * c + 1), "B%d" % b, B[b][:, 0:2, 0:3], T.WD[:, 15 - pp:143 - pp],
-               G1[:, 1536 * c + pp:1536 * (c + 1):16], pp == 0, pp == 15)
-        if copy: cp("B%d" % b, "O2%d" % c, T.O2[:, 96 * c:96 * c + 96], B[b][:, 0:2, 0:3])
-
-    def q_nodes(k):
-        G1 = T["G1" + "ab"[k]]
+    def grandchildren(k):
+        part[0] = "gG"[k]; O1, G1 = T["O1" + "ab"[k]], T["G1" + "ab"[k]]; O1K = "O1a" if k == 0 else ks("O1b%d", 12)
+        for a in range(8): gather(RS + " " + O1K, "G1%d%d" % (k, a), G1[:, 384 * a:384 * a + 384], T.R[:], O1[:, 24 * a:24 * a + 24])
+        for c in range(2):
+            for pp in range(16):
+                mm("WD " + ks("G1%d%%d" % k, range(4 * c, 4 * c + 4)), "B0", B[0][:, 2 * c:2 * c + 2, 0:3], T.WD[:, 15 - pp:143 - pp],
+                   G1[:, 1536 * c + pp:1536 * (c + 1):16], pp == 0, pp == 15)
+            cp("B0", "O2%d" % c, T.O2[:, 96 * c:96 * c + 96], B[0][:, 2 * c:2 * c + 2, 0:3])
+        for a in range(8): gather(RS + " O2%d" % (a // 4), "G2%d" % a, T.G2[:, 384 * a:384 * a + 384], T.R[:], T.O2[:, 24 * a:24 * a + 24])
         for q in range(4):
             for gg in range(8):
-                mm("RQ G1%d%d" % (k, q), "B1", B[1][0:96, q, gg, :, 0:4], G1[:, 768 * q + 96 * gg:768 * q + 96 * gg + 96], T.RQ[:])
-
-    def step2(k, qs):
-        for q in qs:
-            gather(S2[k][q], RS + " O2%d" % (q // 2), "G2%d" % q, T.G2[:, 768 * q:768 * q + 768], T.R[:], T.O2[:, 48 * q:48 * q + 48])
+                mm("RQa0 RQa1 RQb0 RQb1 G1%d%d" % (k, 2 * q + gg // 4), "B1", B[1][0:96, q, gg], G1[:, 768 * q + 96 * gg:768 * q + 96 * gg + 96], T.RQ[:])
+        for q in range(4):
+            FW = T["FW%d" % k]
+            move("B1", "FH%d%d" % (k, q), FW[0:96, :, 2 * q:2 * q + 2, 0:4], B[1][0:96, q, :, :, 4:8])
+            tt("B1 FH%d%d" % (k, q), "FL%d%d" % (k, q), FW[0:96, :, 2 * q:2 * q + 2, 4:8], B[1][0:96, q, :, :, 0:4], FW[0:96, :, 2 * q:2 * q + 2, 0:4], A.subtract)
 
     def results(k):
+        part[0] = "rR"[k]
         for q in range(4):
-            for h in range(2):
-                for gg in range(8):
+            for gg in range(8):
+                for h in range(2):
                     a = 768 * q + 96 * gg + 48 * h
-                    mm("LUa LUb G2%d" % q, "B%d" % (2 + h), B[2 + h][32 * q:32 * q + 32, 0:3, gg], T.LU[:], T.G2[:, a:a + 48])
+                    mm("LUa LUb G2%d" % (2 * q + gg // 4), "B%d" % (2 + h), B[2 + h][32 * q:32 * q + 32, 0:3, gg], T.LU[:], T.G2[:, a:a + 48])
         for h in (0, 1):
-            ts("B%d" % (2 + h), "YB%d" % h, T.YB[:, 3 * h:3 * h + 3], B[2 + h][:, 0:3], 2.0 ** -13, EQ, 15.0, A.mult)
+            if k == 0: ts("B%d" % (2 + h), "YB%d" % h, T.YB[:, 3 * h:3 * h + 3], B[2 + h][:, 0:3], 2.0 ** -13, EQ, 15.0, A.mult)
+            else: act("B%d cb2" % (3 - h), "YT%d" % h, T.YT[:, h, :], B[3 - h][:, 0:3], AF.Abs, bias=C("b2"))
             act("B%d cb1" % (3 - h), "Y0%d" % (1 - h), T.Y0[:, 3 - 3 * h:6 - 3 * h], B[3 - h][:, 0:3], AF.Relu, bias=C("b1"))
+            if k == 1: act("YT%d cb15" % h, "YB%d" % (1 - h), T.YB[:, 3 - 3 * h:6 - 3 * h], T.YT[:, h, :], AF.Relu, scale=-15.0 * 2 ** 14, bias=C("b15"))
         for bb in range(6):
-            for j, y in enumerate(("Y0", "YB")):
-                mm("RKa RKb %s%d" % (y, bb // 3), "B0", B[0][:, :, 0::4, :, bb], T[y][:, bb], T.RK[:, :, 4:6], j == 0, j == 1)
-        if k == 0: ms("XKz", T.XK[:], 0.0); ms("KOz", T.KO[:], 0.0)
-        H = T.HI
-        cp("B0", "HF", T.HF[:], B[0][:, :, 0::4, 0, 0:6])
-        tt("B0 HF", "H0", H[:, 0, :], B[0][:, :, 0::4, 1, 0:6], T.HF[:], A.add)
+            for j in range(4):
+                y = ("Y0", "YB")[j // 2]
+                mm("RKa RKb %s%d" % (y, bb // 3), "B0", B[0][:, 0, :, 0, bb], T[y][:, bb], T.RW[:, :, j % 2], j == 0, j == 3)
+        part[0] = "xX"[k]
+        for gg in range(8):
+            b = 2 + gg // 4; o = B[b][:, gg % 4, 0:6]
+            mm("ID Y00 Y01", "B%d" % b, o, T.ID[:], T.Y0[:, :, gg, :], True, False)
+            mm("ID YB0 YB1", "B%d" % b, o, T.ID[:], T.YB[:, :, gg, :], False, True)
+            if gg % 4 == 3: move("B%d" % b, "YX%d" % (b - 2), T.YX[:, 16 + 384 * (b - 2):400 + 384 * (b - 2)], B[b][:, :, 0:6])
+        part[0] = "hH"[k]; H = T.HI
+        cp("B0", "H0", H[:, 0, :], B[0][:, 0, :, 0, 0:6])
         ts("H0", "H1", H[:, 1, :], H[:, 0, :], 8191, AND); ts("H0", "H2", H[:, 2, :], H[:, 0, :], 8190, AND); ts("H0", "H3", H[:, 3, :], H[:, 0, :], 1, AND)
         cp("H1", "O30", T.O3[:, 0:48], H[:, 1, :])
         tt("H2 H3", "H4", H[:, 4, :], H[:, 2, :], H[:, 3, :], A.subtract)
         ts("H4", "O31", T.O3[:, 48:96], H[:, 4, :], 1.0, A.add)
 
     def lookup(k):
-        def look(e, c):
-            gather(e, QK + " O3%d" % (c // 2), "G3%d" % c, T.G3[:, 384 * c:384 * c + 384], T.Q[:, 0:8192], T.O3[:, 24 * c:24 * c + 24])
-        x = "YX" + "ab"[k]; YX = T[x]; G1 = T["G1" + "ab"[k]]; I = T.SI
-        for gg in range(8):
-            b = 2 + gg // 4; o = B[b][:, gg % 4, 0:6]
-            mm("ID Y00 Y01", "B%d" % b, o, T.ID[:], T.Y0[:, :, gg, :], True, False)
-            mm("ID YB0 YB1", "B%d" % b, o, T.ID[:], T.YB[:, :, gg, :], False, True)
-            if gg % 4 == 3: act("B%d" % b, x + str(b - 2), YX[:, 16 + 384 * (b - 2):400 + 384 * (b - 2)], B[b][:, :, 0:6])
-        for gg in range(8):
-            mm("RKa RKb " + x + str(gg // 4), "B4", B[4][0:96, :, gg], YX[:, 16 + 96 * gg:112 + 96 * gg], T.RK[:])
-        look("v", 0); look("v", 1); look("s", 2)
-        act("B4", "KN", T.KN[0:96], B[4][0:96])
-        look("s", 3)
-        if k == 0: claim_constants_s(); act("ID KOz", "KO", T.KO[:, :, 0:4, :], T.ID[:])
-        else: own_kids()
-        for par in range(2):
-            for s in range(8):
-                a = 768 * par + 96 * s
-                mm("RG G3%d" % (2 * par + s // 4), "B%d" % (5 + par), B[5 + par][0:96, s // 2, :, s % 2, :], T.G3[:, a:a + 96], T.RG[:])
-        for h in range(2):
-            for q in range(4):
-                mm("LBa LBb G1%d%d" % (k, q), "B%d" % (2 + h), B[2 + h][:, 0:3], T.LB[:, 96 - 32 * q:224 - 32 * q], G1[:, 768 * q + 384 * h:768 * q + 384 * h + 384], q == 0, False)
-        tt("KN", "I0", I[0:96, 0, :], T.KN[0:96, :, :, :, 4], T.KN[0:96, :, :, :, 5], A.add)
-        ts("I0", "I1", I[0:96, 1, :], I[0:96, 0, :], 10, SHR, 7, AND); ts("I0", "I2", I[0:96, 2, :], I[0:96, 0, :], 992, AND)
-        ts("I0", "I3", I[0:96, 3, :], I[0:96, 0, :], 31, AND); ts("I0", "I4", I[0:96, 4, :], I[0:96, 0, :], 1, AND)
-        ts("I1", "m0", sm(0), I[0:96, 1, :], 1.0, A.add); ts("I3", "m2", sm(2), I[0:96, 3, :], 1.0, A.add)
-        ts("I4", "m3", sm(3), I[0:96, 4, :], -2.0, A.mult, 1.0, A.add)
-        cp("I2", "m1", sm(1), I[0:96, 2, :])
-        for q in range(4): act("m1 FWz", "FWh%d" % q, T.FW[0:96, :, 2 * q:2 * q + 2, 8], T.SM[0:96, 1, 16 * q:16 * q + 16])
+        part[0] = "lL"[k]; I = T.SI
+        for c in range(4): gather(QK + " O3%d" % (c // 2), "G3%d" % c, T.G3[:, 384 * c:384 * c + 384], T.Q[:, 0:8192], T.O3[:, 24 * c:24 * c + 24])
         for par in range(2):
             b = "B%d" % (5 + par)
-            ts(b, "m%d" % (6 + par), sm(6 + par), B[5 + par][0:96, :, :, :, 0], 0.0, A.is_lt)
-            tt(b + " KN", "EQ%d" % par, T.EQ[0:96, 256 * par:256 * par + 256], B[5 + par][0:96, :, :, :, 0:4], T.KN[0:96, :, :, :, 0:4], EQ)
-        tt("m6 m7", "m11", sm(11), sm(7), sm(6), A.max)
-        scan("EQ0 EQ1 D1", "m4", T.EA[0:96, :], T.D1[0:96, :], T.EQ[0:96, :], A.max, A.mult)
-        tt("m11 m0", "m11", sm(11), sm(11), sm(0), A.mult)
-        tt("m4", "m8", sm(8), hit1, hit0, A.is_gt)
-        tt("m6 m7", "m10", sm(10), sm(7), sm(6), A.is_gt)
-        tt("m4 m8", "m9", sm(9), sm(8), hit0, EQ)
-        tt("m10 m3", "m10", sm(10), sm(10), sm(3), A.mult)
-        tt("m11 m9", "m12", sm(12), sm(11), sm(9), A.mult)
-        tt("m10 m2", "m13", sm(13), sm(10), sm(2), A.add)
-
-    def select1():
+            for gg in range(8):
+                mm("RKz YX%d" % (gg // 4), b, B[5 + par][0:96, :, gg], T.YX[:, 16 + 96 * gg:112 + 96 * gg], T.RK[:], gg == 0, False)
+            for s in range(8):
+                a = 768 * par + 96 * s
+                mm("RG G3%d" % (2 * par + s // 4), b, B[5 + par][0:96, s // 2, :, s % 2, :], T.G3[:, a:a + 96], T.RG[:], False, s == 7)
+        for gg in range(8):
+            for j in range(2): mm("RKa RKb YX%d" % (gg // 4), "B4", B[4][0:96, :, gg, :, 0], T.YX[:, 16 + 96 * gg:112 + 96 * gg], T.RW[:, :, j], j == 0, j == 1)
+        cp("B4", "I0", I[0:96, 0, :], pf(0))
+        ts("I0", "I1", I[0:96, 1, :], I[0:96, 0, :], 10, SHR, 7, AND)
+        ts("I0", "I2", I[0:96, 2, :], I[0:96, 0, :], 992, AND); ts("I0", "I3", I[0:96, 3, :], I[0:96, 0, :], 31, AND); ts("I0", "I4", I[0:96, 4, :], I[0:96, 0, :], 1, AND)
+        ts("B5", "NZ0", T.NZ[0:96, 0:192], B[5][0:96, :, :, :, 0:3], 0.0, A.not_equal)
+        ts("B5", "B4e", pf(2), B[5][0:96, :, :, :, 3], 0.0, A.is_lt, 8.0, A.mult)
+        act("B6", "NZ1", T.NZ[0:96, 192:384], B[6][0:96, :, :, :, 0:3], AF.Abs)
+        act("B6 cb128", "m1", sm(1), B[6][0:96, :, :, :, 3], AF.Relu, scale=-8.0, bias=C("b128")[0:96])
+        scan("NZ0 NZ1 D1", "NS", T.NS[0:96, :], T.D1[0:96, :], T.NZ[0:96, :], A.mult, A.add)
+        ts("NS", "HT", T.HT[0:96, :], T.NS[0:96, 2::3], 0.0, EQ)
+        tt("HT", "m2", sm(2), hit1, hit0, A.is_gt)
+        tt("HT m2", "m3", sm(3), sm(2), hit0, EQ)
+        part[0] = "oO"[k]
+        ts("NS", "H16", T.H16[0:96, :], T.NS[0:96, 2::3], 0.0, EQ, 16.0, A.mult)
+        tt("B4e m1", "B4a", pf(3), pf(2), sm(1), A.max)
+        tt("B4a I1", "B4c", pf(4), I[0:96, 1, :], pf(3), A.subtract)
+        tt("B4c H16", "B4d", pf(6), pf(4), T.H16[0:96, 0:64], A.add)
+        tt("B4d H16", "m4", sm(4), pf(6), T.H16[0:96, 64:128], A.add)
+        for o in range(8): ts("m4", "OH%d" % o, T.OH[0:96, :, :, :, o], sm(4), float(o - 8), EQ)
+        part[0] = "fF"[k]
+        ts("I4", "m5", sm(5), I[0:96, 4, :], -2.0, A.mult, 1.0, A.add)
+        tt("B4e m1", "B4f", pf(5), sm(1), pf(2), A.is_gt)
+        tt("B4f m5", "FS2", T.FS[0:96, :, :, :, 2], pf(5), sm(5), A.mult)
+        cp("I2", "FS0", T.FS[0:96, :, :, :, 0], I[0:96, 2, :]); cp("I3", "FS1", T.FS[0:96, :, :, :, 1], I[0:96, 3, :])
+        for q in range(4): move("FS0 FS1 FS2", "FW%d%d" % (k, q), T["FW%d" % k][0:96, :, 2 * q:2 * q + 2, 8:11], T.FS[0:96, q])
+        part[0] = "nN"[k]
         for t in range(4):
-            tt("B5 m4", "M0%d" % t, T.M0[0:96, :, t], B[5][0:96, :, :, :, 4 + t], hit0, A.mult)
-            tt("B1 m9", "MQ%d" % t, T.MQ[0:96, :, t], B[1][0:96, :, :, :, t], sm(9), A.mult)
-        for t in range(4):
-            tt("B6 m8", "B6", B[6][0:96, :, :, :, t], B[6][0:96, :, :, :, 4 + t], sm(8), A.mult)
-
-    def select2():
-        tt("B6 " + ks("M0%d", 4), "B6", B[6][0:96, :, :, :, 4:8], B[6][0:96, :, :, :, 0:4], T.M0[0:96], A.add)
+            tt("B5 HT", "M0%d" % t, T.M0[0:96, :, t], B[5][0:96, :, :, :, 4 + t], hit0, A.mult)
+            tt("B1 m3", "MQ%d" % t, T.MQ[0:96, :, t], B[1][0:96, :, :, :, t], sm(3), A.mult)
+            tt("B6 m2", "B6%d" % t, B[6][0:96, :, :, :, t], B[6][0:96, :, :, :, 4 + t], sm(2), A.mult)
+        tt(ks("B6%d", 4) + " " + ks("M0%d", 4), "B6", B[6][0:96, :, :, :, 4:8], B[6][0:96, :, :, :, 0:4], T.M0[0:96], A.add)
         tt("B6 " + ks("MQ%d", 4), "P", T.P[0:96], B[6][0:96, :, :, :, 4:8], T.MQ[0:96], A.add)
 
-    def count(k):
-        for o in range(8): ts("m12", "OH%d" % o, T.OH[0:96, :, :, :, o], sm(12), float(o + 1), EQ)
-        for gg in range(8): ts(OHK + " IC", "OI%d" % gg, T.OI[0:96, :, gg], T.OH[0:96, :, gg], T.IC[0:96, gg:gg + 1], A.mult)
-        for q in range(4): act("m13 FWz", "FWl%d" % q, T.FW[0:96, :, 2 * q:2 * q + 2, 9], T.SM[0:96, 13, 16 * q:16 * q + 16])
+    def claims(k):
+        part[0] = "kK"[k]; n = "N3" + "ab"[k]; N3 = T[n]
+        for gg in range(8): scale(OHK + " IC", "OI%d" % gg, T.OI[0:96, :, gg], T.OH[0:96, :, gg], T.IC[0:96, gg:gg + 1])
         for hf in range(2):
             for h2 in range(2):
                 j = 1 + h2 - hf
-                mm(OHK + " TT%d%d" % (k, j), "B7", B[7][0:96, :, :, hf, :], T.TT[0:96, 3 * k + j, :], T.OH[0:96, :, :, h2, :], h2 == 0, False)
-            z = [(r0, d, h2) for r0 in range(2) for d in range(1, 4) for h2 in range(2)]
-            for r0, d, h2 in z:
-                mm(OHK + " ON", "B7", B[7][0:96, :, 4 * r0 + d:4 * r0 + 4, hf, :], T.ON[0:96, 0:96], T.OH[0:96, :, 4 * r0:4 * r0 + 4 - d, h2, :], False, (r0, d, h2) == z[-1])
+                mm(OHK + " TT%d%d" % (k, j), "B7", B[7][0:96, hf::2, :], T.TT[0:96, 3 * k + j, :], T.OH[0:96, :, :, h2, :], hf + h2 == 0, False)
+        z = [(hf, r0, d, h2) for hf in range(2) for r0 in range(2) for d in range(1, 4) for h2 in range(2)]
+        for hf, r0, d, h2 in z:
+            mm(OHK + " ON", "B7", B[7][0:96, hf::2, 8 * (4 * r0 + d):8 * (4 * r0 + 4)], T.ON[0:96, 0:96], T.OH[0:96, :, 4 * r0:4 * r0 + 4 - d, h2, :], False, (hf, r0, d, h2) == z[-1])
         for gg in range(8):
             h, a = gg // 4, 96 * (gg % 4)
             for lo, hi in ((a, min(a + 96, (a // 128 + 1) * 128)), ((a // 128 + 1) * 128, a + 96)):
                 if hi > lo:
-                    mm(ks("FWh%d", 4) + " ID " + ks("FWl%d", 4), "B%d" % (2 + h), B[2 + h][:, lo // 128, (lo % 128) // 16:(lo % 128 + hi - lo) // 16],
-                       T.FW[0:96, gg], T.ID[0:96, (lo - a) // 16:(hi - a) // 16], False, gg % 4 == 3)
-        for h in range(2): act("B%d RBz" % (2 + h), "RB%d" % h, T.RB[:, 16 + 384 * h:400 + 384 * h], B[2 + h][:, 0:3])
-
-    def first16():
-        tt(OHK + " B7", "AA", T.AA[0:96, :], B[7][0:96], T.OH[0:96], A.mult)
-        scan("AA D0", "CS", T.CS[0:96, :], T.D0[0:96, :], T.AA[0:96, :], A.min, A.add)
-        for j in range(16): ts("CS OKz", "OK%d" % j, T.OK[0:96, 1:128:2, j], T.CS[0:96, 7::8], float(j + 1), EQ)
-        for h in range(2): mm("TB " + ks("ID4%d", 4), "B%d" % (2 + h), B[2 + h][:], T.TB[:], T.ID4[:], True, False)
+                    mm(ks("FW%d%%d" % k, 4) + " " + ks("FL%d%%d" % k, 4) + " ID FWz%d" % k, "B%d" % (2 + h), B[2 + h][:, lo // 128, (lo % 128) // 16:(lo % 128 + hi - lo) // 16],
+                       T["FW%d" % k][0:96, gg], T.ID[0:96, (lo - a) // 16:(hi - a) // 16])
+        for h in range(2):
+            move("B%d RBz" % (2 + h), "RB%d" % h, T.RB[:, 16 + 384 * h:400 + 384 * h], B[2 + h][:, 0:3])
+        for i in range(8): scan("B7 D0", "CS%d" % i, T.CS[0:96, 64 * i:64 * i + 64], T.D0[0:96, :], B[7][0:96, i, :], A.add, A.min)
+        for j in range(16): ts(ks("CS%d", 8) + " OKz", "OK%d" % j, T.OK[0:96, 1:128:2, j], T.CS[0:96, 7::8], float(j - 1024), EQ)
         for q in range(4):
             for r0 in range(2):
-                for a in range(4):
-                    for hf in range(2):
-                        c = 2 * (16 * q + 2 * (4 * r0 + a) + hf) + 1 - hf
-                        mm(ks("OK%d", 16) + " " + ks("OI%d", 8), "B4", B[4][32 * q:32 * q + 32, 0, :, 0, r0], T.OK[0:96, c:c + 2, :],
-                           T.OI[0:96, q, 4 * r0 + a, hf, :], a + hf == 0, a + hf == 4)
-
-    def fetch(k):
-        x = "YX" + "ab"[k]
+                for hf in (1, 0):
+                    for a in range(4):
+                        c = 2 * (16 * q + 8 * hf + 4 * r0 + a) + 1 - hf
+                        mm(ks("OK%d", 16) + " " + ks("OI%d", 8), "B4", B[4][32 * q:32 * q + 16 + 16 * hf, 0, :, 0, r0], T.OK[0:96, c:c + 1 + hf, :],
+                           T.OI[0:96, q, 4 * r0 + a, hf, :], (hf, a) == (1, 0), (hf, a) == (0, 3))
         cp("B4", "OS", T.OS[:], B[4][:, 0, :, 0, 0:2])
-        gather("v", "OS RB0 RB1", "GB", T.GB[:], T.RB[:], T.OS[:])
-        gather("vs"[k], "OS %sz %s0 %s1" % (x, x, x), "GA", T.GA[:], T[x][:], T.OS[:])
-
-    def cells_turned():
+        gather("OS RB0 RB1", "GB", T.GB[:], T.RB[:], T.OS[:])
+        gather("OS YXz YX0 YX1", "GA", T.GA[:], T.YX[:], T.OS[:])
+        part[0] = "dD"[k]
         for q in range(4):
             p = slice(32 * q, 32 * q + 32)
-            for o in range(8): mm("GA MT", "B7", B[7][p, o // 2, 4 * (o % 2)], T.GA[p, 32 * o:32 * o + 32], T.MT[p, 0:16])
+            for o in range(8): mm("GB R8", "B4", B[4][p, o // 2, 4 * (o % 2), 0, :], T.GB[p, 32 * o:32 * o + 32], T.R8[p, :])
+        for h in range(2):
+            for q in range(4):
+                mm("GB LS%d" % q, "B%d" % (2 + h), B[2 + h][:, :, 2 * q:2 * q + 2], T.LS[:, q, :], T.GB[:, 128 * h:128 * h + 128])
+        bs = "B7" if k == 0 else "B0"; sums = B[7][:, 0, 0:8] if k == 0 else B[0][:, 0, 0, 0, :]
+        for o in range(8):
+            ts("B4 B%d" % (2 + o // 4), "AB%d" % o, T.AB[:, o, :], B[2 + o // 4][:, o % 4], B[4][:, o // 2, 4 * (o % 2), 0, 4:5], EQ)
+            mm("W2 AB%d" % o, bs, B[7][:, 0, o:o + 1] if k == 0 else B[0][:, 0, 0, 0, o:o + 1], T.AB[:, o, :], T.W2[:])
+        move("B4 " + n + "z", n + "k", N3[:, :, 16:21], B[4][:, :, 0::4, 0, 0:5])
+        if k == 0: ts(bs + " cjq cw3", "nq", T.SN[:, 1, :], sums, C("w3"), A.is_ge, C("jq"), A.mult)
+        ts(bs + " cj1 cw3", "n0", T.SN[:, 0, :], sums, C("w3"), A.is_ge, C("j1"), A.mult)
+        tt("n0 %sk %sz" % (n, n), n + "o", N3[:, :, 21], T.SN[:, 0, :], N3[:, :, 20], A.max)
+        part[0] = "zZ"[k]
+        for q in range(4):
+            p = slice(32 * q, 32 * q + 32)
+            for o in range(8): mm("GA MT", "B7", B[7][p, o, 0:16], T.GA[p, 32 * o:32 * o + 32], T.MT[p, 0:16])
+        l = "LW" + "ab"[k]
+        move("B7", n + "c", N3[:, :, 0:16], B[7][:, :, 0:16])
+        exchange(2 + k, "%sk %sc %so" % (n, n, n), l, lambda r: N3[:, r, :], T[l][:, me, :])
+        move("%sk %sc %so" % (n, n, n), l + "o", T[l][:, me, :], N3[:, me, :])
 
-    def nodes_moved():
+    def enter():
+        part[0] = "e"
+        for q in (0, 2, 1, 3):
+            p = slice(32 * q, 32 * q + 32); b = 5 + q // 2; o = B[b][:, 2 * (q % 2):2 * (q % 2) + 2]
+            mm("LB0 GB" + (" !F%d" % (q - 1) if q % 2 else ""), "B%d" % b, o, T.LB0[p, :], T.GB[p, :], True, False)
+            mm("LA0 GA", "B%d F%d" % (b, q), o, T.LA0[p, :], T.GA[p, :], False, True)
+        for h in range(2): move("B%d" % (5 + h), "DQ%d" % h, T.DQ[:, 512 * h:512 * h + 512], B[5 + h][:])
+        ts("N3ak", "n2", T.SN[:, 2, :], T.N3a[:, :, 20], 2048.0, A.is_ge)
+        tt("N3ak CO", "n3", T.SN[:, 3, :], T.N3a[:, :, 20], T.CO[:], A.add)
+        tt("n2 CK", "n2", T.SN[:, 2, :], T.SN[:, 2, :], T.CK[:], A.mult)
+        tt("n2 n3", "n3", T.SN[:, 3, :], T.SN[:, 3, :], T.SN[:, 2, :], A.add)
+        tt("nq n3", "n4", T.SN[:, 4, :], T.SN[:, 3, :], T.SN[:, 1, :], A.max)
+        for s in range(8): scale("n4 GM", "XQ%d" % s, T.XQ[:, s // 2, :, s % 2], T.SN[:, 4, :], T.GM[:, s:s + 1])
+        mm("ON CP", "B4", B[4][:, 0, 0:4], T.ON[:], T.CP[:], True, False)
+        mm("SR " + ks("XQ%d", 8), "B4", B[4][:, 0, 0:4], T.SR[:], T.XQ[:], False, True)
+        cp("B4", "OQ", T.OQ[:], B[4][:, 0, 0:4])
+        scatter("OQ DQ0 DQ1", QK, T.Q[:], T.OQ[:], T.DQ[:])
+
+    def pointers():
+        part[0] = "p"
         for y in range(3):
-            for t in range(4): act("P", "OP%d%d" % (y, t), T.OP[32 * t:32 * t + 32, :, :, :, :, y], T.P[32 * y:32 * y + 32, :, t])
-
-    def nodes_turned():
+            for t in range(4): move("P", "OP%d%d" % (y, t), T.OP[32 * t:32 * t + 32, :, :, :, :, y], T.P[32 * y:32 * y + 32, :, t])
         for y2 in range(3):
             for x1 in range(2):
                 hf, y = divmod(2 * y2 + x1, 3); a = 4 * (y % 2) + hf; pt = T["PT%d" % x1]
                 for h2 in range(2):
                     mm("PT%d " % x1 + ks("OP%d%%d" % y2, 4), "B1", B[1][:, :, 0::2, y // 2, a:a + 3:2],
                        pt[:, 1 - h2:129 - h2], T.OP[:, :, h2, :, :, y2], h2 == 0, h2 == 1)
-
-    def nodes_sent():
-        act("B1", "NPa", T.NP[:, :, 0:8], B[1][:, :, 0::2, 0, :]); act("B1", "NPb", T.NP[:, :, 8:12], B[1][:, :, 0::2, 1, 0:4])
-        exchange(4, "NPa NPb", "LP", lambda r: T.NP[:, 2 * r:2 * r + 2, :], T.LP[:, me, :])
+        move("B1", "NPa", T.NP[:, :, 0:8], B[1][:, :, 0::2, 0, :]); move("B1", "NPb", T.NP[:, :, 8:12], B[1][:, :, 0::2, 1, 0:4])
+        exchange(4, "NPa NPb", "DP", lambda r: T.NP[:, 2 * r:2 * r + 2, :], T.DP[me])
         dma("y", "NPa NPb", "yn", T.ynodes[16 * me:16 * me + 16, :], T.NP[:, 2 * me:2 * me + 2, :])
+        if me > 0: dma("y", "DP", "yn0", T.ynodes[0:16 * me, :], T.DP[0:me])
+        if me < 7: dma("y", "DP", "yn1", T.ynodes[16 * me + 16:128, :], T.DP[me + 1:8])
 
-    def records(k):
-        n = "N3" + "ab"[k]; N3 = T[n]
-        for q in range(4):
-            p = slice(32 * q, 32 * q + 32)
-            for o in range(8): mm("GB R8", "B4", B[4][p, o // 2, 4 * (o % 2), 0, :], T.GB[p, 32 * o:32 * o + 32], T.R8[p, :])
-        cp("B4", n + "k", N3[:, :, 16:24], B[4][:, :, 0::4, 0, :])
-        ts(n + "k", "n0", sn(0), N3[:, :, 20], -1.0, A.mult)
-        for o in range(8):
-            ts(n + "k IDH", "DG%d" % o, T.DG[:, o, :], T.IDH[:], N3[:, o, 20:21], A.mult)
-            if o % 4 == 3: mm("OF " + ks("DG%d", range(o - 3, o + 1)), "B%d" % (2 + o // 4), B[2 + o // 4][:], T.OF[:], T.DG[:, o - 3:o + 1, :], False, True)
-        if k == 1: cells_turned(); nodes_turned()
-        ts(n + "k", "n3", sn(3), N3[:, :, 20], 1.0, A.min)
-        ts(n + "k cj1", "n1", sn(1), N3[:, :, 20], C("j1"), A.subtract)
-        if k == 0:
-            tt(n + "k CG0", "n5", sn(5), N3[:, :, 20], T.CG[:, 0, :], A.subtract)
-            order(1)
-            for q in (0, 2, 1, 3):
-                if q == 1: need("t", ("t", cnt["t"]))
-                p = slice(32 * q, 32 * q + 32); b = 5 + q // 2; o = B[b][:, 2 * (q % 2):2 * (q % 2) + 2]
-                mm("LA0 GA", "B%d" % b, o, T.LA0[p, :], T.GA[p, :], True, False)
-                mm("LB0 GB", "B%d" % b, o, T.LB0[p, :], T.GB[p, :], False, True)
-            turn(1, 1, False)
+    def settle(k, b):
+        part[0] = "sS"[k]; l = "LW" + "ab"[k]; LW = T[l]; R = l + " " + l + "o #3"
+        move(R, "XC", T.XC[:], LW[:, :, 0:16]); move(R + " XKz", "XK", T.XK[:, :, 8:12], LW[:, :, 16:20])
+        mm("XC ID", "B%d" % b[0], B[b[0]][:, 0], T.XC[:], T.ID[:])
+        mm("XK IDF", "B%d" % b[1], B[b[1]][:, 0], T.XK[:], T.IDF[:])
+        for gg in range(8): scale(R + " MF", "XO%d" % gg, T.XO[:, gg, :], T.MF[:], LW[:, gg, 21:22])
+        mm("GM " + ks("XO%d", 8), "B0", B[0][:, 0, 0, 0, :], T.XO[:], T.GM[:])
+        move("B%d" % b[0], "DC", T.DC[:], B[b[0]][:, 0]); move("B%d" % b[1], "DK", T.DK[:], B[b[1]][:, 0])
+        ts("B0", "OO", T.OO[:], B[0][:, 0, 0, 0, :], -1024.0, A.add)
+        scatter("OO DC CN", "CN", T.CN[:], T.OO[:], T.DC[:])
+        scatter("OO DK YK0 YK1", "YK0 YK1", T.YK[:], T.OO[:], T.DK[:])
 
-    def winners(k):
-        n = "N3" + "ab"[k]; N3 = T[n]
-        for o in range(8):
-            act("n0 B%d" % (2 + o // 4), "AB%d" % o, T.AB[:, o, :], B[2 + o // 4][:, o % 4], AF.Abs, bias=T.SN[:, 0, o:o + 1])
-            red("AB%d" % o, "n2%d" % o, T.SN[:, 2, o:o + 1], T.AB[:, o, :], A.min)
-        if k == 1: act("B7", n + "c", N3[:, :, 0:16], B[7][:, :, 0::4])
-        tt("n3 " + ks("n2%d", 8), "n3", sn(3), sn(2), sn(3), A.min)
-        if k == 0:
-            tt("n3 n5", "n6", sn(6), sn(3), sn(5), A.mult); tt("n6 CG1", "n7", sn(7), sn(6), T.CG[:, 1, :], A.add)
-            for r in range(8): ts("n7 GM", "XQ%d" % r, T.XQ[:, r // 2, :, r % 2], sn(7), T.GM[:, r:r + 1], A.mult)
-            mm("SR " + ks("XQ%d", 8), "B4", B[4][:, 0, 0:4], T.SR[:], T.XQ[:])
-            cp("B7", "O21", T.O2[:, 96:192], B[7][:, 0:2, 0:3])
-        tt("n3 n1", "n4", sn(4), sn(3), sn(1), A.mult)
-        ts("n4 cj0 " + n + "k", n + "o", N3[:, :, 21], sn(4), C("j0"), A.add)
-        if k == 0:
-            for h in range(2): act("B%d" % (5 + h), "DQ%d" % h, T.DQ[:, 512 * h:512 * h + 512], B[5 + h][:])
-            cp("B4", "OQ", T.OQ[:], B[4][:, 0, 0:4])
-            cp("OQ DQ0 DQ1", QK, T.Q[:].indirect(T.OQ[:]), T.DQ[:])
-            cells_turned(); q_nodes(1); step2(1, [1, 2, 3])
-            act("B7", n + "c", N3[:, :, 0:16], B[7][:, :, 0::4])
-        exchange(2 + k, "%sk %sc %so" % (n, n, n), "LW" + "ab"[k], lambda r: N3[:, r, :], T["LW" + "ab"[k]][:, me, :])
-
-    def settle(k):
-        l = "LW" + "ab"[k]; LW = T[l]; R = l + " " + l + "o"; n = "N3" + "ab"[k]
-        act("%sk %sc %so" % (n, n, n), l + "o", LW[:, me, :], T[n][:, me, :])
-        for gg in range(8): ts(R + " MF", "XO%d" % gg, T.XO[:, gg, :], T.MF[:], LW[:, gg, 21:22], A.mult)
-        act(R, "XC", T.XC[:], LW[:, :, 0:16]); act(R + " XKz", "XK", T.XK[:, :, 0:4], LW[:, :, 16:20])
-        mm("XC ID", "B5", B[5][:, 0], T.XC[:], T.ID[:])
-        mm("XK IDF", "B7", B[7][:, 0], T.XK[:], T.IDF[:])
-        mm("GH " + ks("XO%d", 8), "B0", B[0][:, 0, 0, 0, :], T.XO[:], T.GH[:])
-        act("B5", "DC", T.DC[:], B[5][:, 0]); act("B7", "DK", T.DK[:], B[7][:, 0])
-        cp("B0", "OO", T.OO[:], B[0][:, 0, 0, 0, :])
-        cp("OO DC CN", "CN", T.CN[:].indirect(T.OO[:]), T.DC[:])
-        cp("OO DK YK0 YK1", "YK0 YK1", T.YK[:].indirect(T.OO[:]), T.DK[:])
-
-    step1(0, range(4)); turn(0, 0); step2(0, [0, 1]); turn(0, 1); q_nodes(0); step2(0, [2, 3]); claim_constants_v()
-    results(0); lookup(0); count(0); select1(); select2()
+    grandchildren(0); results(0); lookup(0)
     for y in range(3):
-        for t in range(4): cp("P", "O1b%d%d" % (y, t), T.O1b[32 * t:32 * t + 32, y::3], T.P[32 * y:32 * y + 32, :, t])
-    lastw["O1b"] = [("v", cnt["v"], "v")]
-    step1(1, [0, 1]); first16(); step1(1, [2, 3]); fetch(0); turn(1, 0); step2(1, [0]); records(0); winners(0)
-    results(1); lookup(1)
-    count(1); first16(); select1(); fetch(1); select2(); nodes_moved(); records(1); winners(1); nodes_sent(); settle(0); settle(1)
+        for t in range(4): cp("P", "O1b%d" % (4 * y + t), T.O1b[32 * t:32 * t + 32, y::3], T.P[32 * y:32 * y + 32, :, t])
+    grandchildren(1); claims(0); enter(); results(1); lookup(1); claims(1); pointers(); settle(0, (5, 6)); settle(1, (5, 6))
     dma("s", "CN", "yc", T.ycells[:], T.CN[:, 0:1024])
-    for r in others: dma("y", "LP", "yn%d" % r, T.ynodes[16 * r:16 * r + 16, :], T.LP[:, r, :])
-    for t in range(4): dma("sy"[t % 2], "YK0 YK1", "yk%d" % t, T.ykids[t::4, :], T.YK[t::16, 0:1024])
-    for s, n in total.items(): need("p", (s, n))
+    for t in range(4): dma("sy"[t % 2], "YK0 YK1", "yk%d" % t, T.ykids[t::4, :], T.YK[8 + t::16, 0:1024])
+
+    cnt, seen, tok, total = {"v": 0, "s": 0, "t": 0, "p": 0}, {}, {}, {}
+    def need(e, s, n):
+        if seen.get((e, s), 0) < n:
+            QU[e].wait_ge(T.sem[s], n); seen[(e, s)] = n
+    for i, e in schedule(ops):
+        pre, sig = ops[i][5], ops[i][6]
+        w = [ops[j][6][k] if ops[j][6] else tok[j] for (j, k), hard in pre.items() if ops[j][6] or hard or tok[j][0] != e]
+        for s, n in sorted(w, reverse=True): need(e, s, n)
+        call = ops[i][4](e)
+        if sig: total.update(sig.values())
+        else:
+            call.then_inc(T.sem[e], 1); cnt[e] += 1; tok[i] = (e, cnt[e]); total[e] = cnt[e]
+    for s, n in total.items(): need("p", s, n)

from concourse.bass import DstId, RemoteDMATransfer
from concourse.mybir import AluOpType as A, AxisListType, ActivationFunctionType as AF

F32, B16, I32, F16, U16 = "float32", "bfloat16", "int32", "float16", "uint16"
SB = {
    "KI": ([256], I32), "KH": ([512], I32), "HL": ([512], B16), "CN": ([1168], B16), "YK": ([1168], F32), "PB": ([512], B16),
    "WI": ([1], I32), "WH": ([2], I32), "WB": ([2], B16), "WC": ([2], F32),
    "L": ([2048], B16), "LN": ([8, 24], I32), "LF": ([8, 24], F32), "UP": ([1024], B16), "R": ([8192], B16), "Q": ([9248], B16),
    "O1a": ([192], U16), "O1b": ([192], U16), "G1a": ([3072], B16), "G1b": ([3072], B16), "O2": ([192], U16), "G2": ([3072], B16),
    "Y0": ([6, 8, 16], B16), "YB": ([6, 8, 16], B16), "YX": ([784], B16), "RB": ([784], B16), "YT": ([2, 384], B16),
    "HI": ([5, 48], I32), "H16": ([128], B16), "O3": ([96], U16), "G3": ([1536], B16), "NZ": ([384], B16), "NS": ([384], B16), "HT": ([128], B16),
    "SM": ([6, 64], F32), "SI": ([5, 64], I32), "P": ([64, 4], F32), "M0": ([64, 4], F32), "MQ": ([64, 4], F32),
    "OH": ([4, 8, 2, 8], B16), "CS": ([512], F32), "OK": ([130, 16], F16), "OI": ([4, 8, 2, 8], F16), "OS": ([16], U16),
    "GA": ([256], B16), "GB": ([256], B16), "FW0": ([8, 8, 16], B16), "FW1": ([8, 8, 16], B16), "FS": ([4, 8, 2, 3], B16),
    "XC": ([8, 16], B16), "XK": ([8, 16], F32), "N3a": ([8, 24], F32), "N3b": ([8, 24], F32),
    "AB": ([8, 128], B16), "SN": ([5, 8], F32), "CP": ([64], B16), "XQ": ([4, 8, 2], F32), "DQ": ([1024], B16), "OQ": ([64], U16),
    "LWa": ([8, 24], F32), "LWb": ([8, 24], F32), "OP": ([8, 2, 2, 2, 3], F32), "NP": ([16, 12], F32),
    "XO": ([8, 16], F32), "DC": ([128], B16), "DK": ([128], F32), "OO": ([8], U16),
    "PI": ([1], I32), "PJ": ([13], I32), "PF": ([96], F32), "XR": ([144], F32), "X16": ([128], F32), "VT": ([7, 18], F32), "VU": ([12, 16], F32),
    "XT0": ([144], F32), "XT1": ([144], F32), "ID": ([8, 16], B16), "IDF": ([128], F32),
    "MT": ([128], B16), "MF": ([16], F32), "GM": ([8], F32), "PM": ([130], B16),
    "PW0": ([144], F32), "PW1": ([144], F32), "PT0": ([130], F32), "PT1": ([130], F32),
    "KO": ([8, 16, 4], B16), "LR": ([8, 4, 16], B16), "WD": ([144], B16), "LU": ([32], B16), "RG": ([8, 8], B16), "RK": ([8, 8], B16), "RW": ([8, 2], B16),
    "RQ": ([2, 8], B16), "R8": ([8], B16), "LA0": ([128], B16), "LB0": ([128], B16), "SR": ([128], F32),
    "SW": ([128], B16), "ML": ([2, 96], F32), "MD": ([3, 96], F32), "TT": ([6, 96], B16), "ON": ([128], B16), "ZR": ([128], F32),
    "LS": ([4, 128], B16), "TB": ([128], F32), "TC": ([128], F32), "W2": ([1], B16), "D0": ([64], B16),
    "D1": ([384], B16), "IC": ([8], F32), "CK": ([8], F32), "CO": ([8], F32),
}
SCRATCH = {k: ("sbuf", [128] + s, d) for k, (s, d) in SB.items()}
SCRATCH["D"] = ("dram", [8, 128, 256], B16)
SCRATCH["DN"] = ("dram", [8, 128, 24], I32)
SCRATCH["DP"] = ("dram", [8, 128, 24], F32)
for _b in range(8):
    SCRATCH["B%d" % _b] = ("psum", [128, 4, 8, 2, 8] if _b < 7 else [128, 8, 64], F32)
SEMAPHORES = ["v", "s", "t", "p", "rn"] + ["d%d" % i for i in range(48)] + ["rl%d" % i for i in range(5)] + ["rr%d" % i for i in range(5)]
CY, PC, HOP, SAME, GA_, SC_ = 0.83e-3, 0.47e-3, 0.17, 0.23, 1.45, 3.0
TOL = 0.02
FIX = {"s": 0.03, "vs": 0.015}
URGE, SHY = {'D': 8, 'r': 4, 'd': 2, 'X': -8, 'dB4': 2, 'tR2': -2, 'tB0': -8, 'HH3': -0.5, 'GB0': 2, 'XB3': -8, 'rB2': -1, 'dB2': 4, 'lm2': -2, 'xB3': -4, 'G': -1, 'R': -2, 'oB4': -4, 'SCN': 2, 'RB2': -2, 'rB3': 0.5, 'tR5': -8}, {'kOI': 9, 'eDQ': 0.5, 'GG2': 0.5, 'eXQ': 9, 'tR1': -0.3, 'LG3': 0.2, 'tR6': 0.2, 'fFW': 0.5, 'gG2': -0.3}


def schedule(ops):
    n = len(ops); succ = [[] for _ in ops]; left = [len(o[3]) for o in ops]
    for i, o in enumerate(ops):
        for j, _ in o[3]: succ[j].append(i)
    rest = [0.0] * n
    for i in range(n - 1, -1, -1):
        rest[i] = ops[i][1] + ops[i][2] + max([rest[j] + (HOP if dict(ops[j][3])[i] is not None else -ops[i][2]) for j in succ[i]] + [0.0])
    for i in range(n): rest[i] += URGE.get(ops[i][7], 0.0) + URGE.get(ops[i][7][0], 0.0)
    free, done, on, out, base = dict.fromkeys("vstpy", 0.0), [0.0] * n, [""] * n, [], {}
    ready = [i for i in range(n) if not left[i]]
    def can(i):
        base[i] = []
        for e in ops[i][0]:
            s = 0.0
            for j, hard in ops[i][3]:
                if hard is None: s = max(s, done[j] - ops[j][2] - ops[j][1]); continue
                if on[j] != e or ops[j][2] > 0: s = max(s, done[j] + HOP)
                elif hard: s = max(s, done[j] + SAME)
            base[i].append((s, e, SHY.get(ops[i][7], 0.0) if e == "v" else 0.0))
    for i in ready: can(i)
    while ready:
        c = [min((max(s, free[e]) + d, max(s, free[e]), e, i) for s, e, d in base[i])[1:] for i in ready]
        e = min(c)[1]; c = [z for z in c if z[1] == e]
        c.sort(key=lambda z: -rest[z[2]])
        best = c[0]
        while True:
            fit = [z for z in c if z[0] + ops[z[2]][1] <= best[0] + TOL and z is not best and z[0] < best[0]]
            if not fit: break
            best = fit[0]
        s, e, i = best
        free[e] = s + ops[i][1]; done[i] = free[e] + ops[i][2]; on[i] = e; out.append((i, e)); ready.remove(i)
        for j in succ[i]:
            left[j] -= 1
            if not left[j]: ready.append(j); can(j)
    return out


def rank_program(g, core, T, topo):
    me = T.rank_of(core)
    if me is None:
        return
    QU = {"v": g.vector, "s": g.scalar, "t": g.tensor, "p": g, "y": g.sync}
    V, S, PE = g.vector, g.scalar, g.tensor
    ops, lastw, reads, bank, part = [], {}, {}, {}, ["c"]

    def op(es, R, W, fn, cost, lat=0.0, sig=None):
        R, W = R.split(), W.split(); pre = {}; after = []
        for k in R + W:
            if k[0] == "B" and k[:2] in bank: pre.setdefault((bank[k[:2]], ""), False)
        for k in W:
            for j in lastw.get(k, []) + reads.get(k, []): pre[j] = pre.get(j, False) or es != "t"
        for k in R:
            if k[0] == "#": after += lastw.get(k, [])
            else:
                for j in lastw.get(k.strip("!"), []): pre[j] = pre.get(j, False) or es != "t" or k[0] == "!"
        i = len(ops)
        for k in W: lastw[k] = [(i, k if sig and k in sig else "")]; reads[k] = []
        for k in R: reads.setdefault(k, []).append((i, ""))
        for k in R + W:
            if k[0] == "B": bank[k[:2]] = i
        hard = {}
        for (j, _), h in pre.items(): hard[j] = hard.get(j, False) or h
        for j, _ in after: hard.setdefault(j, None)
        ops.append([es, cost + FIX.get(es, 0.0), lat, sorted(hard.items()), fn, pre, sig, part[0] + W[0][:2]])

    nd = [0]
    def dma(e, R, W, out, in_, lat=1.1):
        s = "d%d" % nd[0]; nd[0] += 1
        op(e, R, W, lambda q: QU[q].dma_start(out, in_).then_inc(T.sem[s], 16), 0.06, lat, {"": (s, 16)})

    others = [r for r in range(8) if r != me]
    far = [r for r in others if topo.die(T.cores[r]) != topo.die(core)]
    near = [r for r in others if r not in far]

    def exchange(k, R, W, src, dst, split=False, cost=0.9, lat=2.8):
        tr = []
        for r in others:
            c = T.cores[r]; en = topo.engines(core, c); rid, pid, _ = topo.addr(c)
            en = en[0::2][2 * far.index(r):] if r in far else en[1::2][2 * near.index(r):]
            tr.append(RemoteDMATransfer(dst_ids=[DstId(rid=rid, pnc=pid)], dma_engine_mask=(1 << en[0]) | (1 << en[1]),
                                        remote_sem=T.sem["rn" if split and r in near else "rr%d" % k], src=src(r), dst=dst))
        sig = {"": ("rl%d" % k, 14), W: ("rr%d" % k, 2 * len(far) if split else 14)}
        if split: sig[W + "n"] = ("rn", 2 * len(near))
        op("p", R + " #%d" % min(k - 1, 2), " ".join(sig) + " #%d" % k, lambda q: g.remote_dma_fused(tr, local_sem=T.sem["rl%d" % k]), cost, lat, sig)

    def size(a):
        n = 1
        for d in a.shape[1:]: n *= d
        return n
    def cyc(*a): return CY * max(64, size(a[0]) * (0.5 if all("16" in str(z.dtype) for z in a) else 1))
    def ks(f, n): return " ".join(f % j for j in (range(n) if isinstance(n, int) else n))
    def mm(R, W, out, l, r, st=True, sp=True):
        op("t", R, W, lambda q: PE.matmul(out, l, r, st, sp), PC * max(min(64, size(l)), size(r)) * (4 if "32" in str(l.dtype) else 1))
    def cp(R, W, o, i): op("v", R, W, lambda q: V.tensor_copy(o, i), cyc(o, i))
    def tt(R, W, o, a, b, f): op("v", R, W, lambda q: V.tensor_tensor(o, a, b, f), CY * max(64, size(o) * (1 if "B" in [k[0] for k in R.split()] else 2)))
    def ts(R, W, o, a, s1, f0, s2=None, f1=None):
        op("v", R, W, (lambda q: V.tensor_scalar(o, a, s1, None, f0)) if f1 is None else (lambda q: V.tensor_scalar(o, a, s1, s2, f0, f1)), cyc(o, a))
    def ms(W, o, c, R=""): op("v", R, W, lambda q: V.memset(o, c), cyc(o))
    def act(R, W, o, i, f=AF.Identity, **k): op("s", R, W, lambda q: S.activation(o, i, f, **k), CY * max(64, size(o)))
    def red(R, W, o, i, f): op("v", R, W, lambda q: V.tensor_reduce(o, i, AxisListType.X, f), CY * 64)
    def scan(R, W, o, a, b, f0, f1): op("v", R, W, lambda q: V.tensor_tensor_scan(o, a, b, 0.0, f0, f1), cyc(o, a, b))
    def iota(W, o, pat, base, cm=0): op("p", "", W, lambda q: g.iota(o, pat, base, cm, allow_small_or_imprecise_dtypes=True), 0.13 + 2 * CY * size(o))
    def move(R, W, o, i, es="vs", cost=None):
        op(es, R, W, lambda q: V.tensor_copy(o, i) if q == "v" else S.activation(o, i, AF.Identity), cost or CY * max(64, size(o)))
    def scale(R, W, o, i, c, es="vs"):
        op(es, R, W, lambda q: V.tensor_scalar(o, i, c, None, A.mult) if q == "v" else S.activation(o, i, AF.Identity, scale=c), CY * max(64, size(o)))
    def relu(R, W, o, i, c):
        op("vs", R, W, lambda q: V.tensor_scalar(o, i, c, 0.0, A.add, A.max) if q == "v" else S.activation(o, i, AF.Relu, bias=c), CY * max(64, size(o)))
    def gather(R, W, o, win, off): move(R, W, o, win.indirect(off), "vs", 0.03 + CY * GA_ * size(o))
    def scatter(R, W, win, off, i): op("v", R, W, lambda q: V.tensor_copy(win.indirect(off), i), 0.05 + CY * SC_ * size(i))
    B = [T["B%d" % b] for b in range(8)]
    half = lambda b, u: B[b][:, 2 * u:2 * u + 2] if b < 7 else B[b][:, 4 * u:4 * u + 4]
    SHR, AND, EQ = A.arith_shift_right, A.bitwise_and, A.is_equal

    dma("y", "", "DN", T.DN[:], T.nodes[:])
    dma("y", "", "KI", T.KI[:], T.kids[:])
    dma("s", "", "CN", T.CN[:, 0:1024], T.cells[:])
    dma("y", "", "WI", T.WI[:], T.wt[:])
    dma("s", "CN", "Dc", T.D[:, 0:64, :], T.CN[:, 0:1024])
    op("p", "", "PI", lambda q: g.iota(T.PI[:], [[0, 1]], 0, 1), 0.13)
    iota("XR", T.XR[:], [[1, 144]], 0)
    iota("X16", T.X16[:], [[0, 8], [1, 16]], 0)
    iota("VT1a", T.VT[:, 1, 0:12], [[8, 3], [1, 4]], 9)
    iota("VT1b", T.VT[:, 1, 12:16], [[8, 2], [1, 2]], 18)
    iota("VT2", T.VT[:, 2, 0:16], [[8, 4], [1, 4]], 18)
    iota("VT3a", T.VT[:, 3, 0:8], [[0, 2], [1, 4]], 4)
    iota("VT3b", T.VT[:, 3, 8:17], [[1, 3], [0, 3]], 0)
    iota("VT5", T.VT[:, 5, :], [[1, 3], [0, 6]], 0)
    iota("ML0", T.ML[:, 0, :], [[32, 6], [1, 16]], 0)
    iota("ML1", T.ML[:, 1, :], [[16, 2], [64, 3], [1, 16]], 0)
    iota("IC", T.IC[:], [[96, 8]], 16, 1)
    iota("CK", T.CK[:], [[-1023, 8]], 7168, 8)
    iota("CQ", T.CP[:], [[0, 4], [1, 8], [0, 2]], 0)
    iota("CO", T.CO[:], [[1023, 8]], -1024)
    exchange(0, "DN", "LN", lambda r: T.DN[r], T.LN[:, me, :], cost=2.0)
    dma("y", "DN", "LNo", T.LN[:, me, :], T.DN[me])

    names = ["p", "b0", "pm", "pg", "hf", "t", "i4", "t2", "p8", "m1", "k11", "b3", "o7"]
    rule = [(0, 127), (0, 1), (0, 15), (4, 7), (4, 1), (5, 3), (2, 3), (1, 3), (3, 15), (1, 7), (0, 11), (0, 3), (0, 7)]
    col = {}
    def C(n):
        if n not in col: col[n] = len(col)
        return T.PF[:, col[n]:col[n] + 1]
    for j, (sh, an) in enumerate(rule):
        ts("PI", "PJ%d" % j, T.PJ[:, j:j + 1], T.PI[:], sh, SHR, an, AND); C(names[j])
    cp(ks("PJ%d", 13), ks("c%s", names), T.PF[:, 0:13], T.PJ[:])
    def lin(n, a, x, y, f0=A.mult, f1=A.add):
        ts(ks("c%s", [z for z in (a, x, y) if isinstance(z, str)]), "c" + n, C(n), C(a), C(x) if isinstance(x, str) else x, f0, C(y) if isinstance(y, str) else y, f1)
    def pick(W, o, rk, n, c, w="one"):
        ts("%s c%s c%s" % (rk, c, w), W, o, T[rk][:, 0:n], C(c), EQ, C(w), A.mult)
    xt = [0]
    def spick(W, o, rk, n, c, w="one"):
        k = "XT%d" % xt[0]; xt[0] ^= 1
        act(rk + " c" + c, k, T[k][:, 0:n], T[rk][:, 0:n], AF.Abs, scale=-1.0, bias=C(c))
        act(k + " c" + w, W, o, T[k][:, 0:n], AF.Relu, scale=-65536.0, bias=C(w))
    for n, c in (("one", 1.0), ("b1", -(1.0 + 2.0 ** -11)), ("b128", -128.0), ("b2", -2.0 ** -13), ("b15", 15.0)): ms("c" + n, C(n), c)
    lin("w16", "b0", 15.0, 1.0); lin("cpm", "p", 1.0, "b0", A.add, A.subtract)
    pick("PM", T.PM[:], "XR", 130, "cpm", "w16")
    pick("ID", T.ID[:], "XR", 128, "p")

    ts("KI", "KHa", T.KH[:, 0:256], T.KI[:], 8160, AND)
    cp("KHa", "HLa", T.HL[:, 0:256], T.KH[:, 0:256])
    ts("KI", "KHb", T.KH[:, 256:512], T.KI[:], 31, AND)
    cp("KHb", "HLb", T.HL[:, 256:512], T.KH[:, 256:512])
    dma("y", "HLa", "Dh", T.D[:, 64:80, :], T.HL[:, 0:256])
    dma("y", "HLb", "Dl", T.D[:, 80:96, :], T.HL[:, 256:512])
    mm("PM CN", "B0", B[0][:], T.PM[:, 1:129], T.CN[:, 0:512], True, False)
    mm("PM CN", "B0", B[0][:], T.PM[:, 0:128], T.CN[:, 512:1024], False, True)
    act("B0", "PB", T.PB[:], B[0][:])
    dma("s", "PB", "Dp", T.D[:, 96:128, :], T.PB[:])
    exchange(1, "Dc Dh Dl Dp", "L", lambda r: T.D[r], T.L[:, 256 * me:256 * me + 256], True, lat=3.6)
    dma("y", "Dc Dh Dl Dp", "Lo", T.L[:, 256 * me:256 * me + 256], T.D[me])

    ms("LR", T.LR[:], 0.0); ms("OKz", T.OK[:, 0::2, :], 0.0); ms("ON", T.ON[:], 1.0); ms("KOz", T.KO[:], 0.0)
    ms("FWz0", T.FW0[:, :, :, 11:16], 0.0); ms("FWz1", T.FW1[:, :, :, 11:16], 0.0)
    ms("D0z", T.D0[:], 0.0); ms("D0", T.D0[:, 0::8], 4096.0, "D0z"); ms("D1z", T.D1[:], 1.0); ms("D1", T.D1[:, 0::3], 0.0, "D1z")
    for t in range(4):
        t1, t0 = t >> 1, t & 1
        b = 4 * (5 - 4 * t1 - t0); vr, vc = 2 - 2 * t1, 2 - 2 * t0
        move("ID LR", "LRa%d" % t, T.LR[:, 2 * t, 0:3, 0:12], T.ID[:, b // 16:b // 16 + 3, b % 16:b % 16 + 12])
        move("ID LR", "LRb%d" % t, T.LR[:, 2 * t, 3, :], T.ID[:, vr:vr + 2, 4 * vc:4 * vc + 8])
        move("ID LR", "LRc%d" % t, T.LR[:, 2 * t, 0:2, 12:16], T.ID[:, 4:6, 4 * (3 - t):4 * (3 - t) + 4])
    move(ks("LRa%d", 4) + " " + ks("LRb%d", 4) + " " + ks("LRc%d", 4), "LRz", T.LR[:, 1::2], T.LR[:, 0::2])
    pick("MF", T.MF[:], "X16", 16, "pm")
    def table(n, row, R):
        tt(R + " MF", "VU%d" % row, T.VU[:, row, :], T.VT[:, row, 0:16], T.MF[:], A.mult)
        red("VU%d" % row, "c" + n, C(n), T.VU[:, row, :], A.add)
    ms("VT0", T.VT[:, 0, :], 0.0)
    for a in range(3): ms("VT0%d" % a, T.VT[:, 0, 4 * a:4 * a + 3], 1.0, "VT0")
    table("hm", 0, ks("VT0%d", 3))
    lin("x1", "t2", 32.0, 16.0); lin("nb0", "b0", -1.0, 1.0); lin("bias", "hm", -14.0, 0.0); lin("cpw", "x1", 1.0, "p8")
    spick("PW0", T.PW0[:], "XR", 144, "cpw", "nb0"); spick("PW1", T.PW1[:], "XR", 144, "cpw", "b0")
    lin("km", "k11", 3.0, 1.0, EQ, A.mult); lin("cwd", "pg", 16.0, 15.0); lin("crq", "hf", 4.0, "t")
    spick("WD", T.WD[:], "XR", 144, "cwd", "km")
    lin("kh", "pm", 3.0, 1.0, EQ, A.mult)
    for u in range(2):
        ts("XR ccrq ckm", "RQa%d" % u, T.RQ[:, u, 0:4], T.XR[:, 4 * u:4 * u + 4], C("crq"), EQ, C("km"), A.mult)
        ts("XR ccrq ckh", "RQb%d" % u, T.RQ[:, u, 4:8], T.XR[:, 4 * u:4 * u + 4], C("crq"), EQ, C("kh"), A.mult)
    table("pos0", 1, "VT1a VT1b")
    lin("tl", "t", 2.0, 6.0, A.is_ge, A.mult); lin("tau", "t", 1.0, "tl")
    lin("x2", "hm", 2.0, "tau", A.add, A.mult)
    lin("hw", "hm", 2.0 ** -14, 0.0); lin("vw", "pm", 12.0, 1.0, A.is_ge, A.mult); lin("nhf", "hf", -1.0, 1.0); lin("pos", "x2", 1.0, "pos0")
    U = lambda i: T.VU[:, i, :]
    ts("VT2 cpos", "VU2", U(2), T.VT[:, 2, 0:16], C("pos"), A.subtract)
    tt("VU2", "VU2", U(2), U(2), U(2), A.mult)
    ts("VU2 chw", "VU7", U(7), U(2), 1.0, EQ, C("hw"), A.mult)
    ts("VU2", "VU8", U(8), U(2), 49.0, A.is_ge)
    ts("VU2 chw", "VU9", U(9), U(2), 81.0, A.is_le, C("hw"), A.mult)
    ts("VU2 cvw", "VU10", U(10), U(2), 0.0, EQ, C("vw"), A.mult)
    tt("VU8 VU9", "VU8", U(8), U(8), U(9), A.mult)
    tt("VU7 VU10", "VU7", U(7), U(7), U(10), A.add)
    tt("VU7 VU8", "VU7", U(7), U(7), U(8), A.add)
    ts("VU7 cnhf", "LUa", T.LU[:, 0:16], U(7), C("nhf"), A.mult)
    ts("VU7 chf", "LUb", T.LU[:, 16:32], U(7), C("hf"), A.mult)
    lin("mine", "pg", float(me), 1.0, EQ, A.mult)
    spick("SW", T.SW[:], "X16", 128, "pm", "mine")
    pick("GM", T.GM[:], "XR", 8, "pg")
    ts("WI", "WHa", T.WH[:, 0:1], T.WI[:], 8160, AND); ts("WI", "WHb", T.WH[:, 1:2], T.WI[:], 31, AND)
    cp("WHa WHb", "WB", T.WB[:], T.WH[:])
    mm("SW WB", "B0", B[0][:, 0, 0, 0, 0:2], T.SW[:], T.WB[:])
    cp("B0", "WC", T.WC[:], B[0][:, 0, 0, 0, 0:2])
    for j in range(6): ms("VT4%d" % j, T.VT[:, 4, j::6], -16.0 ** j)
    table("wk", 4, ks("VT4%d", 6)); table("i6", 5, "VT5")
    lin("crk", "pg", 8.0, "i6")
    pick("RKz", T.RK[:], "XR", 64, "crk", "wk")
    lin("ge8", "pm", 8.0, 1.0, A.is_ge, A.mult)
    ts("GM WC", "RKa", T.RW[:, :, 0], T.GM[:], T.WC[:, 0:1], A.mult)
    ts("GM WC", "RKb", T.RW[:, :, 1], T.GM[:], T.WC[:, 1:2], A.mult)
    ms("VT6", T.VT[:, 6, :], 1.0)
    for j in (1, 2): ms("VT6%d" % j, T.VT[:, 6, 8 + j::3], 256.0 ** j, "VT6")
    table("fs", 3, "VT3a VT3b"); table("wg", 6, "VT61 VT62")
    lin("crg", "pg", 8.0, "fs"); lin("is8", "pm", 8.0, 1.0, EQ, A.mult)
    pick("RGz", T.RG[:], "XR", 64, "crg", "wg")
    ts("GM cis8 RGz", "RG", T.RG[:, :, 3], T.GM[:], C("is8"), A.mult)
    pick("IDF", T.IDF[:], "XR", 128, "p")
    ts("IDF", "MD2", T.MD[:, 2, :], T.IDF[:, 0:96], -1024.0, A.mult)
    for k in range(2):
        tt("ML%d IDF" % k, "MD0", T.MD[:, 0, :], T.ML[:, k, :], T.IDF[:, 0:96], A.mult)
        red("MD0", "cml%d" % k, C("ml%d" % k), T.MD[:, 0, :], A.add)
        for j in (0, 2):
            ts("ML%d cml%d" % (k, k), "TT%d%d" % (k, j), T.TT[:, 3 * k + j, :], T.ML[:, k, :], C("ml%d" % k), A.subtract, float(16 * (k + 1) * (j - 1)), A.is_ge)
        ts("ML%d cml%d" % (k, k), "MD1", T.MD[:, 1, :], T.ML[:, k, :], C("ml%d" % k), A.is_gt)
        tt("MD1 MD2", "TT%d1" % k, T.TT[:, 3 * k + 1, :], T.MD[:, 1, :], T.MD[:, 2, :], A.add)
    ms("N3az", T.N3a[:, :, 20:24], 0.0); ms("N3bz", T.N3b[:, :, 20:24], 0.0); lin("jq", "p", 8.0, 8192.0); ms("ZR", T.ZR[:], 0.0); ms("YXz", T.YX[:, 0:16], 0.0); ms("XKz", T.XK[:], 0.0)
    lin("k8", "is8", 1024.0, 0.0)
    ts("MF ck8", "RBz", T.RB[:, 0:16], T.MF[:], 0.0, A.mult, C("k8"), A.add)
    lin("x5", "ge8", -1.0, 1.0); lin("w8", "pm", 11.0, 1.0, A.is_lt, A.mult); lin("cla", "m1", 1.0, 8.0); lin("x7", "pm", 8.0, 1.0)
    lin("x6", "x5", "b3", 0.0); lin("j1", "p", 1.0, 2049.0); lin("cpt", "t", 2.0, "x7"); lin("cr8", "ge8", 4.0, "x6"); lin("ws", "ge8", "w8", 0.0)
    ms("TBa", T.TB[:], 0.5); ms("TBb", T.TB[:, 0:1], 2.0 ** 63, "TBa")
    op("v", "TBb ZR", "TC", lambda q: V.tensor_tensor_scan(T.TC[:], T.TB[:], T.ZR[:], 1.0, A.mult, A.add), CY * 128)
    tt("TC IDF", "TC", T.TC[:], T.TC[:], T.IDF[:], A.mult); red("TC", "cw2", C("w2"), T.TC[:], A.add)
    cp("cw2", "W2", T.W2[:], C("w2")); lin("w3", "w2", 2.5, 0.0)
    ts("CQ", "CP", T.CP[:], T.CP[:], 2.0 ** -7, A.mult)
    pick("R8", T.R8[:], "XR", 8, "cr8", "w8")
    for q in range(4):
        lin("lq%d" % q, "t", float(q), "ws", EQ, A.mult)
        scale("ON clq%d" % q, "LS%d" % q, T.LS[:, q, :], T.ON[:], C("lq%d" % q))
    spick("MT", T.MT[:], "X16", 128, "pm")
    move("MT", "SR", T.SR[:], T.MT[:])
    spick("LA0", T.LA0[:], "X16", 128, "cla", "w16"); spick("LB0", T.LB0[:], "X16", 128, "pm", "x5")
    spick("PT0", T.PT0[:], "XR", 130, "cpt", "nhf"); spick("PT1", T.PT1[:], "XR", 130, "cpt", "hf")
    move("ID KOz", "KO", T.KO[:, :, 8:12, :], T.ID[:])
    for blk in range(4):
        b = 6 + blk // 2; o = half(b, blk % 2)
        mm("KO HLa", "B%d" % b, o, T.KO[:, :, :, blk], T.HL[:, 0:256], True, False)
        mm("KO HLb", "B%d" % b, o, T.KO[:, :, :, blk], T.HL[:, 256:512], False, True)
    move("B6", "YK0", T.YK[:, 0:512], B[6][:]); move("B7", "YK1", T.YK[:, 512:1024], B[7][:])
    cp("LN LNo", "LF", T.LF[:], T.LN[:])
    for h2 in range(2):
        pw = T["PW%d" % h2]
        mm("LF PW%d" % h2, "B5", B[5][:, :, 2 * h2::4, :, 0:6], pw[:, 16:144], T.LF[:, :, 0::2], True, False)
        mm("LF PW%d" % h2, "B5", B[5][:, :, 2 * h2::4, :, 0:6], pw[:, 0:128], T.LF[:, :, 1::2], False, True)
    cp("B5", "O1a", T.O1a[:], B[5][:, :, 0::2, :, 0:6])

    part[0] = "t"
    came = lambda r: "Lo" if r == me else "Ln" if r in near else "L"
    for r in [me] + near + far:
        dma("y", came(r), "UP%d" % r, T.UP[64 * (r // 4) + r % 4:64 * (r // 4) + 64:4, :], T.L[64:128, 256 * r:256 * r + 256])
    for n, h in enumerate((me // 4, 1 - me // 4)):
        for gg in range(8):
            dma("y", ks("UP%d", range(4 * h, 4 * h + 4)), "Q%d" % (8 * h + gg), T.Q[16 * gg:16 * gg + 16, 4096 * h:4096 * h + 4096], T.UP[64 * h:64 * h + 64, :],
                1.2 + 0.15 * (8 * n + gg))
    QK, RS, OHK = ks("Q%d", 16), ks("R%d_", 16), ks("OH%d", 8)
    for n, i in enumerate(2 * r + j for r in [me] + near + far for j in range(2)):
        r, j, b = i // 2, i % 2, n % 8
        for u in range(2):
            mm(came(r) + " LRz", "B%d" % b, half(b, u), T.LR[0:96, :, :, 2 * j + u::4], T.L[0:96, 256 * r:256 * r + 256])
        relu("B%d cbias" % b, "R%d_" % i, T.R[:, 512 * i:512 * i + 512], B[b][:], C("bias"))
    sm = lambda i: T.SM[0:96, i, :]
    pf = lambda f: B[4][0:96, :, :, :, f]
    hit0, hit1 = T.HT[0:96, 0:64], T.HT[0:96, 64:128]

    def grandchildren(k):
        part[0] = "gG"[k]; O1, G1 = T["O1" + "ab"[k]], T["G1" + "ab"[k]]; O1K = "O1a" if k == 0 else ks("O1b%d", 12)
        for a in range(8): gather(RS + " " + O1K, "G1%d%d" % (k, a), G1[:, 384 * a:384 * a + 384], T.R[:], O1[:, 24 * a:24 * a + 24])
        for c in range(2):
            for pp in range(16):
                mm("WD " + ks("G1%d%%d" % k, range(4 * c, 4 * c + 4)), "B0", B[0][:, 2 * c:2 * c + 2, 0:3], T.WD[:, 15 - pp:143 - pp],
                   G1[:, 1536 * c + pp:1536 * (c + 1):16], pp == 0, pp == 15)
            cp("B0", "O2%d" % c, T.O2[:, 96 * c:96 * c + 96], B[0][:, 2 * c:2 * c + 2, 0:3])
        for a in range(8): gather(RS + " O2%d" % (a // 4), "G2%d" % a, T.G2[:, 384 * a:384 * a + 384], T.R[:], T.O2[:, 24 * a:24 * a + 24])
        for q in range(4):
            for gg in range(8):
                mm("RQa0 RQa1 RQb0 RQb1 G1%d%d" % (k, 2 * q + gg // 4), "B1", B[1][0:96, q, gg], G1[:, 768 * q + 96 * gg:768 * q + 96 * gg + 96], T.RQ[:])
        for q in range(4):
            FW = T["FW%d" % k]
            move("B1", "FH%d%d" % (k, q), FW[0:96, :, 2 * q:2 * q + 2, 0:4], B[1][0:96, q, :, :, 4:8])
            tt("B1 FH%d%d" % (k, q), "FL%d%d" % (k, q), FW[0:96, :, 2 * q:2 * q + 2, 4:8], B[1][0:96, q, :, :, 0:4], FW[0:96, :, 2 * q:2 * q + 2, 0:4], A.subtract)

    def results(k):
        part[0] = "rR"[k]
        for q in range(4):
            for gg in range(8):
                for h in range(2):
                    a = 768 * q + 96 * gg + 48 * h
                    mm("LUa LUb G2%d" % (2 * q + gg // 4), "B%d" % (2 + h), B[2 + h][32 * q:32 * q + 32, 0:3, gg], T.LU[:], T.G2[:, a:a + 48])
        for h in (0, 1):
            if k == 0: ts("B%d" % (2 + h), "YB%d" % h, T.YB[:, 3 * h:3 * h + 3], B[2 + h][:, 0:3], 2.0 ** -13, EQ, 15.0, A.mult)
            else: act("B%d cb2" % (3 - h), "YT%d" % h, T.YT[:, h, :], B[3 - h][:, 0:3], AF.Abs, bias=C("b2"))
            act("B%d cb1" % (3 - h), "Y0%d" % (1 - h), T.Y0[:, 3 - 3 * h:6 - 3 * h], B[3 - h][:, 0:3], AF.Relu, bias=C("b1"))
            if k == 1: act("YT%d cb15" % h, "YB%d" % (1 - h), T.YB[:, 3 - 3 * h:6 - 3 * h], T.YT[:, h, :], AF.Relu, scale=-15.0 * 2 ** 14, bias=C("b15"))
        for bb in range(6):
            for j in range(4):
                y = ("Y0", "YB")[j // 2]
                mm("RKa RKb %s%d" % (y, bb // 3), "B0", B[0][:, 0, :, 0, bb], T[y][:, bb], T.RW[:, :, j % 2], j == 0, j == 3)
        part[0] = "xX"[k]
        for gg in range(8):
            b = 2 + gg // 4; o = B[b][:, gg % 4, 0:6]
            mm("ID Y00 Y01", "B%d" % b, o, T.ID[:], T.Y0[:, :, gg, :], True, False)
            mm("ID YB0 YB1", "B%d" % b, o, T.ID[:], T.YB[:, :, gg, :], False, True)
            if gg % 4 == 3: move("B%d" % b, "YX%d" % (b - 2), T.YX[:, 16 + 384 * (b - 2):400 + 384 * (b - 2)], B[b][:, :, 0:6])
        part[0] = "hH"[k]; H = T.HI
        cp("B0", "H0", H[:, 0, :], B[0][:, 0, :, 0, 0:6])
        ts("H0", "H1", H[:, 1, :], H[:, 0, :], 8191, AND); ts("H0", "H2", H[:, 2, :], H[:, 0, :], 8190, AND); ts("H0", "H3", H[:, 3, :], H[:, 0, :], 1, AND)
        cp("H1", "O30", T.O3[:, 0:48], H[:, 1, :])
        tt("H2 H3", "H4", H[:, 4, :], H[:, 2, :], H[:, 3, :], A.subtract)
        ts("H4", "O31", T.O3[:, 48:96], H[:, 4, :], 1.0, A.add)

    def lookup(k):
        part[0] = "lL"[k]; I = T.SI
        for c in range(4): gather(QK + " O3%d" % (c // 2), "G3%d" % c, T.G3[:, 384 * c:384 * c + 384], T.Q[:, 0:8192], T.O3[:, 24 * c:24 * c + 24])
        for par in range(2):
            b = "B%d" % (5 + par)
            for gg in range(8):
                mm("RKz YX%d" % (gg // 4), b, B[5 + par][0:96, :, gg], T.YX[:, 16 + 96 * gg:112 + 96 * gg], T.RK[:], gg == 0, False)
            for s in range(8):
                a = 768 * par + 96 * s
                mm("RG G3%d" % (2 * par + s // 4), b, B[5 + par][0:96, s // 2, :, s % 2, :], T.G3[:, a:a + 96], T.RG[:], False, s == 7)
        for gg in range(8):
            for j in range(2): mm("RKa RKb YX%d" % (gg // 4), "B4", B[4][0:96, :, gg, :, 0], T.YX[:, 16 + 96 * gg:112 + 96 * gg], T.RW[:, :, j], j == 0, j == 1)
        cp("B4", "I0", I[0:96, 0, :], pf(0))
        ts("I0", "I1", I[0:96, 1, :], I[0:96, 0, :], 10, SHR, 7, AND)
        ts("I0", "I2", I[0:96, 2, :], I[0:96, 0, :], 992, AND); ts("I0", "I3", I[0:96, 3, :], I[0:96, 0, :], 31, AND); ts("I0", "I4", I[0:96, 4, :], I[0:96, 0, :], 1, AND)
        ts("B5", "NZ0", T.NZ[0:96, 0:192], B[5][0:96, :, :, :, 0:3], 0.0, A.not_equal)
        ts("B5", "B4e", pf(2), B[5][0:96, :, :, :, 3], 0.0, A.is_lt, 8.0, A.mult)
        act("B6", "NZ1", T.NZ[0:96, 192:384], B[6][0:96, :, :, :, 0:3], AF.Abs)
        act("B6 cb128", "m1", sm(1), B[6][0:96, :, :, :, 3], AF.Relu, scale=-8.0, bias=C("b128")[0:96])
        scan("NZ0 NZ1 D1", "NS", T.NS[0:96, :], T.D1[0:96, :], T.NZ[0:96, :], A.mult, A.add)
        ts("NS", "HT", T.HT[0:96, :], T.NS[0:96, 2::3], 0.0, EQ)
        tt("HT", "m2", sm(2), hit1, hit0, A.is_gt)
        tt("HT m2", "m3", sm(3), sm(2), hit0, EQ)
        part[0] = "oO"[k]
        ts("NS", "H16", T.H16[0:96, :], T.NS[0:96, 2::3], 0.0, EQ, 16.0, A.mult)
        tt("B4e m1", "B4a", pf(3), pf(2), sm(1), A.max)
        tt("B4a I1", "B4c", pf(4), I[0:96, 1, :], pf(3), A.subtract)
        tt("B4c H16", "B4d", pf(6), pf(4), T.H16[0:96, 0:64], A.add)
        tt("B4d H16", "m4", sm(4), pf(6), T.H16[0:96, 64:128], A.add)
        for o in range(8): ts("m4", "OH%d" % o, T.OH[0:96, :, :, :, o], sm(4), float(o - 8), EQ)
        part[0] = "fF"[k]
        ts("I4", "m5", sm(5), I[0:96, 4, :], -2.0, A.mult, 1.0, A.add)
        tt("B4e m1", "B4f", pf(5), sm(1), pf(2), A.is_gt)
        tt("B4f m5", "FS2", T.FS[0:96, :, :, :, 2], pf(5), sm(5), A.mult)
        cp("I2", "FS0", T.FS[0:96, :, :, :, 0], I[0:96, 2, :]); cp("I3", "FS1", T.FS[0:96, :, :, :, 1], I[0:96, 3, :])
        for q in range(4): move("FS0 FS1 FS2", "FW%d%d" % (k, q), T["FW%d" % k][0:96, :, 2 * q:2 * q + 2, 8:11], T.FS[0:96, q])
        part[0] = "nN"[k]
        for t in range(4):
            tt("B5 HT", "M0%d" % t, T.M0[0:96, :, t], B[5][0:96, :, :, :, 4 + t], hit0, A.mult)
            tt("B1 m3", "MQ%d" % t, T.MQ[0:96, :, t], B[1][0:96, :, :, :, t], sm(3), A.mult)
            tt("B6 m2", "B6%d" % t, B[6][0:96, :, :, :, t], B[6][0:96, :, :, :, 4 + t], sm(2), A.mult)
        tt(ks("B6%d", 4) + " " + ks("M0%d", 4), "B6", B[6][0:96, :, :, :, 4:8], B[6][0:96, :, :, :, 0:4], T.M0[0:96], A.add)
        tt("B6 " + ks("MQ%d", 4), "P", T.P[0:96], B[6][0:96, :, :, :, 4:8], T.MQ[0:96], A.add)

    def claims(k):
        part[0] = "kK"[k]; n = "N3" + "ab"[k]; N3 = T[n]
        for gg in range(8): scale(OHK + " IC", "OI%d" % gg, T.OI[0:96, :, gg], T.OH[0:96, :, gg], T.IC[0:96, gg:gg + 1])
        for hf in range(2):
            for h2 in range(2):
                j = 1 + h2 - hf
                mm(OHK + " TT%d%d" % (k, j), "B7", B[7][0:96, hf::2, :], T.TT[0:96, 3 * k + j, :], T.OH[0:96, :, :, h2, :], hf + h2 == 0, False)
        z = [(hf, r0, d, h2) for hf in range(2) for r0 in range(2) for d in range(1, 4) for h2 in range(2)]
        for hf, r0, d, h2 in z:
            mm(OHK + " ON", "B7", B[7][0:96, hf::2, 8 * (4 * r0 + d):8 * (4 * r0 + 4)], T.ON[0:96, 0:96], T.OH[0:96, :, 4 * r0:4 * r0 + 4 - d, h2, :], False, (hf, r0, d, h2) == z[-1])
        for gg in range(8):
            h, a = gg // 4, 96 * (gg % 4)
            for lo, hi in ((a, min(a + 96, (a // 128 + 1) * 128)), ((a // 128 + 1) * 128, a + 96)):
                if hi > lo:
                    mm(ks("FW%d%%d" % k, 4) + " " + ks("FL%d%%d" % k, 4) + " ID FWz%d" % k, "B%d" % (2 + h), B[2 + h][:, lo // 128, (lo % 128) // 16:(lo % 128 + hi - lo) // 16],
                       T["FW%d" % k][0:96, gg], T.ID[0:96, (lo - a) // 16:(hi - a) // 16])
        for h in range(2):
            move("B%d RBz" % (2 + h), "RB%d" % h, T.RB[:, 16 + 384 * h:400 + 384 * h], B[2 + h][:, 0:3])
        for i in range(8): scan("B7 D0", "CS%d" % i, T.CS[0:96, 64 * i:64 * i + 64], T.D0[0:96, :], B[7][0:96, i, :], A.add, A.min)
        for j in range(16): ts(ks("CS%d", 8) + " OKz", "OK%d" % j, T.OK[0:96, 1:128:2, j], T.CS[0:96, 7::8], float(j - 1024), EQ)
        for q in range(4):
            for r0 in range(2):
                for hf in (1, 0):
                    for a in range(4):
                        c = 2 * (16 * q + 8 * hf + 4 * r0 + a) + 1 - hf
                        mm(ks("OK%d", 16) + " " + ks("OI%d", 8), "B4", B[4][32 * q:32 * q + 16 + 16 * hf, 0, :, 0, r0], T.OK[0:96, c:c + 1 + hf, :],
                           T.OI[0:96, q, 4 * r0 + a, hf, :], (hf, a) == (1, 0), (hf, a) == (0, 3))
        cp("B4", "OS", T.OS[:], B[4][:, 0, :, 0, 0:2])
        gather("OS RB0 RB1", "GB", T.GB[:], T.RB[:], T.OS[:])
        gather("OS YXz YX0 YX1", "GA", T.GA[:], T.YX[:], T.OS[:])
        part[0] = "dD"[k]
        for q in range(4):
            p = slice(32 * q, 32 * q + 32)
            for o in range(8): mm("GB R8", "B4", B[4][p, o // 2, 4 * (o % 2), 0, :], T.GB[p, 32 * o:32 * o + 32], T.R8[p, :])
        for h in range(2):
            for q in range(4):
                mm("GB LS%d" % q, "B%d" % (2 + h), B[2 + h][:, :, 2 * q:2 * q + 2], T.LS[:, q, :], T.GB[:, 128 * h:128 * h + 128])
        bs = "B7" if k == 0 else "B0"; sums = B[7][:, 0, 0:8] if k == 0 else B[0][:, 0, 0, 0, :]
        for o in range(8):
            ts("B4 B%d" % (2 + o // 4), "AB%d" % o, T.AB[:, o, :], B[2 + o // 4][:, o % 4], B[4][:, o // 2, 4 * (o % 2), 0, 4:5], EQ)
            mm("W2 AB%d" % o, bs, B[7][:, 0, o:o + 1] if k == 0 else B[0][:, 0, 0, 0, o:o + 1], T.AB[:, o, :], T.W2[:])
        move("B4 " + n + "z", n + "k", N3[:, :, 16:21], B[4][:, :, 0::4, 0, 0:5])
        if k == 0: ts(bs + " cjq cw3", "nq", T.SN[:, 1, :], sums, C("w3"), A.is_ge, C("jq"), A.mult)
        ts(bs + " cj1 cw3", "n0", T.SN[:, 0, :], sums, C("w3"), A.is_ge, C("j1"), A.mult)
        tt("n0 %sk %sz" % (n, n), n + "o", N3[:, :, 21], T.SN[:, 0, :], N3[:, :, 20], A.max)
        part[0] = "zZ"[k]
        for q in range(4):
            p = slice(32 * q, 32 * q + 32)
            for o in range(8): mm("GA MT", "B7", B[7][p, o, 0:16], T.GA[p, 32 * o:32 * o + 32], T.MT[p, 0:16])
        l = "LW" + "ab"[k]
        move("B7", n + "c", N3[:, :, 0:16], B[7][:, :, 0:16])
        exchange(2 + k, "%sk %sc %so" % (n, n, n), l, lambda r: N3[:, r, :], T[l][:, me, :])
        move("%sk %sc %so" % (n, n, n), l + "o", T[l][:, me, :], N3[:, me, :])

    def enter():
        part[0] = "e"
        for q in (0, 2, 1, 3):
            p = slice(32 * q, 32 * q + 32); b = 5 + q // 2; o = B[b][:, 2 * (q % 2):2 * (q % 2) + 2]
            mm("LB0 GB" + (" !F%d" % (q - 1) if q % 2 else ""), "B%d" % b, o, T.LB0[p, :], T.GB[p, :], True, False)
            mm("LA0 GA", "B%d F%d" % (b, q), o, T.LA0[p, :], T.GA[p, :], False, True)
        for h in range(2): move("B%d" % (5 + h), "DQ%d" % h, T.DQ[:, 512 * h:512 * h + 512], B[5 + h][:])
        ts("N3ak", "n2", T.SN[:, 2, :], T.N3a[:, :, 20], 2048.0, A.is_ge)
        tt("N3ak CO", "n3", T.SN[:, 3, :], T.N3a[:, :, 20], T.CO[:], A.add)
        tt("n2 CK", "n2", T.SN[:, 2, :], T.SN[:, 2, :], T.CK[:], A.mult)
        tt("n2 n3", "n3", T.SN[:, 3, :], T.SN[:, 3, :], T.SN[:, 2, :], A.add)
        tt("nq n3", "n4", T.SN[:, 4, :], T.SN[:, 3, :], T.SN[:, 1, :], A.max)
        for s in range(8): scale("n4 GM", "XQ%d" % s, T.XQ[:, s // 2, :, s % 2], T.SN[:, 4, :], T.GM[:, s:s + 1])
        mm("ON CP", "B4", B[4][:, 0, 0:4], T.ON[:], T.CP[:], True, False)
        mm("SR " + ks("XQ%d", 8), "B4", B[4][:, 0, 0:4], T.SR[:], T.XQ[:], False, True)
        cp("B4", "OQ", T.OQ[:], B[4][:, 0, 0:4])
        scatter("OQ DQ0 DQ1", QK, T.Q[:], T.OQ[:], T.DQ[:])

    def pointers():
        part[0] = "p"
        for y in range(3):
            for t in range(4): move("P", "OP%d%d" % (y, t), T.OP[32 * t:32 * t + 32, :, :, :, :, y], T.P[32 * y:32 * y + 32, :, t])
        for y2 in range(3):
            for x1 in range(2):
                hf, y = divmod(2 * y2 + x1, 3); a = 4 * (y % 2) + hf; pt = T["PT%d" % x1]
                for h2 in range(2):
                    mm("PT%d " % x1 + ks("OP%d%%d" % y2, 4), "B1", B[1][:, :, 0::2, y // 2, a:a + 3:2],
                       pt[:, 1 - h2:129 - h2], T.OP[:, :, h2, :, :, y2], h2 == 0, h2 == 1)
        move("B1", "NPa", T.NP[:, :, 0:8], B[1][:, :, 0::2, 0, :]); move("B1", "NPb", T.NP[:, :, 8:12], B[1][:, :, 0::2, 1, 0:4])
        exchange(4, "NPa NPb", "DP", lambda r: T.NP[:, 2 * r:2 * r + 2, :], T.DP[me])
        dma("y", "NPa NPb", "yn", T.ynodes[16 * me:16 * me + 16, :], T.NP[:, 2 * me:2 * me + 2, :])
        if me > 0: dma("y", "DP", "yn0", T.ynodes[0:16 * me, :], T.DP[0:me])
        if me < 7: dma("y", "DP", "yn1", T.ynodes[16 * me + 16:128, :], T.DP[me + 1:8])

    def settle(k, b):
        part[0] = "sS"[k]; l = "LW" + "ab"[k]; LW = T[l]; R = l + " " + l + "o #3"
        move(R, "XC", T.XC[:], LW[:, :, 0:16]); move(R + " XKz", "XK", T.XK[:, :, 8:12], LW[:, :, 16:20])
        mm("XC ID", "B%d" % b[0], B[b[0]][:, 0], T.XC[:], T.ID[:])
        mm("XK IDF", "B%d" % b[1], B[b[1]][:, 0], T.XK[:], T.IDF[:])
        for gg in range(8): scale(R + " MF", "XO%d" % gg, T.XO[:, gg, :], T.MF[:], LW[:, gg, 21:22])
        mm("GM " + ks("XO%d", 8), "B0", B[0][:, 0, 0, 0, :], T.XO[:], T.GM[:])
        move("B%d" % b[0], "DC", T.DC[:], B[b[0]][:, 0]); move("B%d" % b[1], "DK", T.DK[:], B[b[1]][:, 0])
        ts("B0", "OO", T.OO[:], B[0][:, 0, 0, 0, :], -1024.0, A.add)
        scatter("OO DC CN", "CN", T.CN[:], T.OO[:], T.DC[:])
        scatter("OO DK YK0 YK1", "YK0 YK1", T.YK[:], T.OO[:], T.DK[:])

    grandchildren(0); results(0); lookup(0)
    for y in range(3):
        for t in range(4): cp("P", "O1b%d" % (4 * y + t), T.O1b[32 * t:32 * t + 32, y::3], T.P[32 * y:32 * y + 32, :, t])
    grandchildren(1); claims(0); enter(); results(1); lookup(1); claims(1); pointers(); settle(0, (5, 6)); settle(1, (5, 6))
    dma("s", "CN", "yc", T.ycells[:], T.CN[:, 0:1024])
    for t in range(4): dma("sy"[t % 2], "YK0 YK1", "yk%d" % t, T.ykids[t::4, :], T.YK[8 + t::16, 0:1024])

    cnt, seen, tok, total = {"v": 0, "s": 0, "t": 0, "p": 0}, {}, {}, {}
    def need(e, s, n):
        if seen.get((e, s), 0) < n:
            QU[e].wait_ge(T.sem[s], n); seen[(e, s)] = n
    for i, e in schedule(ops):
        pre, sig = ops[i][5], ops[i][6]
        w = [ops[j][6][k] if ops[j][6] else tok[j] for (j, k), hard in pre.items() if ops[j][6] or hard or tok[j][0] != e]
        for s, n in sorted(w, reverse=True): need(e, s, n)
        call = ops[i][4](e)
        if sig: total.update(sig.values())
        else:
            call.then_inc(T.sem[e], 1); cnt[e] += 1; tok[i] = (e, cnt[e]); total[e] = cnt[e]
    for s, n in total.items(): need("p", s, n)
